import numpy as np
import ml_dtypes


def mxq(x, axis, fmt="e4m3"):
    dtype, down = {"e4m3": (ml_dtypes.float8_e4m3fn, 7), "e5m2": (ml_dtypes.float8_e5m2, 14)}[fmt]
    v = np.moveaxis(np.asarray(x, np.float32).astype(ml_dtypes.bfloat16).astype(np.float64), axis, -1)
    blocks = v.reshape(v.shape[:-1] + (-1, 32))
    amax = np.abs(blocks).max(-1, keepdims=True)
    byte = np.maximum(np.where(amax > 0, np.frexp(amax)[1] - 1 + 127, 0) - down, 1)
    scale = np.exp2(byte - 127.0)
    codes = (blocks / scale).astype(np.float32).astype(dtype).astype(np.float64)
    return np.moveaxis((codes * scale).reshape(v.shape), -1, axis)


WIDE = False


def mx_kscale(k):
    if not WIDE:
        return np.ones(k)
    levels = np.array([10, -10, 5, -5, 0])
    if k % 512:
        return np.exp2(np.random.permutation(np.resize(levels, k // 32))).repeat(32)
    a = np.empty((k // 512, 16))
    for p in range(k // 512):
        a[p, :8] = np.random.permutation(np.resize(levels, 8))
        for g in range(8):
            far = levels[np.abs(levels - a[p, g]) >= 10]
            a[p, g + 8] = far[np.random.randint(len(far))]
    return np.exp2(a.ravel()).repeat(32)


def f64(x):
    return np.asarray(x).astype(np.float64)


def striped(idx):
    return np.tile(np.asarray(idx).reshape(-1, 16).T, (8, 1)).astype(np.uint16)


def unstriped(offs):
    return offs[:16].T.reshape(-1).astype(np.int64)


E2M1 = np.array([0.0, 0.5, 1.0, 1.5, 2.0, 3.0, 4.0, 6.0, -0.0, -0.5, -1.0, -1.5, -2.0, -3.0, -4.0, -6.0])


def pack_weight(w, fmt):
    k, n = w.shape
    w = f64(np.asarray(w, np.float32).astype(ml_dtypes.bfloat16)).reshape(k // 32, 32, n)
    amax = np.abs(w).max(1)
    if fmt == "e4m3":
        byte = np.frexp(amax)[1] - 1 + 127 - 7
    else:
        mant, ex = np.frexp(amax / 6.0)
        byte = np.where(mant > 0.5, ex, ex - 1) + 127
    byte = np.clip(np.where(amax > 0, byte, 1), 1, 254)
    scaled = (w * np.exp2(127.0 - byte)[:, None, :]).reshape(k, n).astype(np.float32)
    by_word = np.ascontiguousarray(scaled.reshape(k // 512, 128, 4, n).transpose(0, 1, 3, 2))
    if fmt == "e4m3":
        words = by_word.astype(ml_dtypes.float8_e4m3fn).view(np.uint8)
    else:
        c = by_word.astype(ml_dtypes.float4_e2m1fn).view(np.uint8) & 0xF
        words = (c[..., 0::2] | (c[..., 1::2] << 4)).reshape(k // 512, 128, 2 * n)
    return np.ascontiguousarray(words), np.ascontiguousarray(byte.astype(np.uint8).reshape(k // 512, 16, n))


def unpack_weight(words, scales, fmt):
    g, _, n = scales.shape
    words = np.ascontiguousarray(words).reshape(g, 128, n, -1)
    if fmt == "e4m3":
        vals = words.view(ml_dtypes.float8_e4m3fn).astype(np.float64)
    else:
        nib = np.empty((g, 128, n, 4), np.uint8)
        nib[..., 0::2] = words & 0xF
        nib[..., 1::2] = words >> 4
        vals = E2M1[nib]
    vals = vals * np.repeat(np.exp2(scales.astype(np.float64) - 127.0), 8, axis=1)[..., None]
    return vals.transpose(0, 1, 3, 2).reshape(g * 512, n)


B, N, T, D, DV, NQ = 1, 512, 2048, 1024, 256, 128
CAP = 2.0


def setup_inputs():
    n = np.random.standard_normal
    idx = np.sort(np.random.permutation(T)[:B * N].reshape(B, N), axis=1).reshape(-1)
    s = mx_kscale(D)[:, None]
    u = np.ones(T)
    u[idx] = mx_kscale(B * N)
    r = np.random.uniform(0.5, 2.0, T)
    qp = [pack_weight(x, "e4m3") for x in n((B, D, NQ)) * s * (1.00 / np.sqrt(D))]
    k = n((D, T)) / s
    v = n((DV, T)) / (u * r)
    kp = pack_weight(k, "e2m1")
    return {
        "q_words": np.stack([x[0] for x in qp]),
        "q_scales": np.stack([x[1] for x in qp]),
        "k_words": np.ascontiguousarray(kp[0].reshape(D // 1024, 2, 128, T, 2).transpose(0, 2, 3, 1, 4)).reshape(D // 1024, 128, T, 4),
        "k_scales": kp[1],
        "vT": v.astype(np.float32),
        "vs": np.tile(u * r, (128, 1)).astype(np.float32),
        "sink": (2.0 + 3.0 * n((B, NQ, 1))).astype(np.float32),
        "offs": striped(idx),
    }


def reference(q_words, q_scales, k_words, k_scales, vT, vs, sink, offs):
    idx = unstriped(offs)
    k = unpack_weight(k_words.reshape(D // 1024, 128, T, 2, 2).transpose(0, 3, 1, 2, 4).reshape(D // 512, 128, 2 * T), k_scales, "e2m1")
    v = f64(vT)
    pick = lambda x: x[:, idx].reshape(x.shape[0], B, N).transpose(1, 0, 2)
    q = np.stack([unpack_weight(q_words[b], q_scales[b], "e4m3") for b in range(B)])
    score = q.transpose(0, 2, 1) @ pick(k)
    score = CAP * np.tanh(score / CAP)
    m = np.maximum(score.max(-1, keepdims=True), f64(sink))
    p = np.exp(score - m)
    total = p.sum(-1, keepdims=True) + np.exp(f64(sink) - m)
    w = p * pick(f64(vs))[:, :1, :]
    y = mxq(w, 2, "e4m3") @ mxq(pick(v).transpose(0, 2, 1), 1, "e4m3")
    y = y / total
    return y

@@ -1,0 +1,181 @@
+from contextlib import ExitStack
+
+import concourse.mybir as mybir
+from concourse.masks import make_identity
+
+N, T, D, DV, NQ = 512, 2048, 1024, 256, 128
+CAP = 2.0
+FLOPS = 2 * NQ * N * (D + DV)
+BYTES = 128 * T * 4 + 32 * T + 128 * 2 * NQ * 4 + 32 * NQ + DV * T * 4 + T * 4 + NQ * 4 + 128 * 64 + NQ * DV * 4
+
+F32 = mybir.dt.float32
+BF16 = mybir.dt.bfloat16
+I32 = mybir.dt.int32
+U32 = mybir.dt.uint32
+U16 = mybir.dt.uint16
+U8 = mybir.dt.uint8
+FP8X4 = mybir.dt.float8_e4m3fn_x4
+FP4X4 = mybir.dt.float4_e2m1fn_x4
+ALU = mybir.AluOpType
+ACT = mybir.ActivationFunctionType
+
+P = 128
+PACK = 4
+PASSES = D // 512
+HALF = N // 2
+GROUP = 128
+VS_ROW = 8
+
+
+def tile_attend_soft_cap_sink_srtq128n512t2048_kernel(
+    tc, q_words, q_scales, k_words, k_scales, vT, vs, sink, offs, out
+):
+    nc = tc.nc
+    with ExitStack() as ctx:
+        sb = ctx.enter_context(tc.tile_pool(name="sb", bufs=1))
+        ps = ctx.enter_context(tc.psum_pool(name="ps", bufs=1))
+
+        offsets = sb.tile([P, N // 16], U16, name="offsets")
+        nc.sync.dma_start(offsets[:], offs)
+
+        k_pool = sb.tile([P, T], I32, name="k_pool", align_bytes=64)
+        nc.scalar.dma_start(k_pool[:], k_words[0].rearrange("g t b -> g (t b)").bitcast(I32))
+
+        zero = sb.tile([P, 1], F32, name="zero")
+        nc.gpsimd.memset(zero[:], 0.0)
+        warm = sb.tile([P, 1], F32, name="warm", tag="values", align_bytes=64)
+        nc.scalar.activation(warm[:], zero[:], ACT.Exp)
+
+        ks_pool = sb.tile([P, PASSES, T // 4], I32, name="ks_pool", tag="early", align_bytes=64)
+        nc.vector.memset(ks_pool[:], 0)
+        ks_rows = k_scales.bitcast(I32).rearrange("o (Q r) t -> r Q o t", r=4)
+        for r in range(4):
+            nc.sync.dma_start(ks_pool[r:P:32, :, :], ks_rows[r])
+
+        v_pool = sb.tile([P, 2, T], F32, name="v_pool", tag="values", align_bytes=64)
+        for h in range(2):
+            nc.scalar.dma_start(v_pool[:, h, :], vT[h * P : (h + 1) * P, :])
+
+        qs = sb.tile([P, PASSES, NQ // 4], I32, name="qs", align_bytes=64)
+        nc.vector.memset(qs[:], 0)
+        vs_pool = sb.tile([P, T], F32, name="vs_pool", align_bytes=64)
+        nc.vector.memset(vs_pool[:], 0.0)
+
+        qw = sb.tile([P, PASSES, NQ], I32, name="qw", align_bytes=64)
+        nc.sync.dma_start(qw[:], q_words[0].rearrange("o g q r -> g o (q r)").bitcast(I32))
+        qs_rows = q_scales[0].bitcast(I32).rearrange("o (Q r) q -> r Q o q", r=4)
+        for r in range(4):
+            nc.sync.dma_start(qs[r:P:32, :, :], qs_rows[r])
+        sink_col = sb.tile([P, 1], F32, name="sink_col")
+        nc.gpsimd.dma_start(sink_col[:], sink[0])
+        ident = sb.tile([P, P], F32, name="ident", align_bytes=64)
+        make_identity(nc, ident[:])
+        nc.sync.dma_start(vs_pool[VS_ROW : VS_ROW + 1, :], vs[0:1, :])
+
+        ks = sb.tile([P, PASSES, N], U8, name="ks", align_bytes=64)
+        for o in range(PASSES):
+            nc.vector.tensor_copy(ks[:, o, :], ks_pool[:, o, :].bitcast(U8).indirect(offsets[:]))
+
+        neg_c = sb.tile([P, N + 1], F32, name="neg_c", align_bytes=64)
+        nc.scalar.activation(neg_c[:, N : N + 1], sink_col[:], ACT.Copy, scale=-1.0)
+
+        k_both = sb.tile([P, 2, HALF], I32, name="k_both", tag="early", align_bytes=64)
+        k_pass = [sb.tile([P, PASSES, 2 * HALF], U8, name="k_pass%d" % h, align_bytes=64) for h in range(2)]
+        cols = HALF // 16
+        for h in range(2):
+            nc.vector.tensor_copy(
+                k_both[:, h, :].bitcast(U32), k_pool[:].bitcast(U32).indirect(offsets[:, h * cols : (h + 1) * cols])
+            )
+            nc.vector.tensor_copy(
+                k_pass[h][:].bitcast(U16), k_both[:, h, :].bitcast(U16).rearrange("p (i o) -> p o i", o=PASSES)
+            )
+
+        th = sb.tile([P, PACK, P], F32, name="th", tag="late", align_bytes=64)
+        neg_m = [sb.tile([P, 1], F32, name="neg_m%d" % h) for h in range(2)]
+        neg_c4 = neg_c[:, 0:N].rearrange("q (t p) -> q t p", t=PACK)
+        for h in range(2):
+            score = ps.tile([P, HALF], F32, name="score%d" % h)
+            for g in range(HALF // GROUP):
+                for o in range(PASSES):
+                    nc.tensor.matmul_mx(
+                        score[:, g * GROUP : (g + 1) * GROUP],
+                        lhsT=qw[:, o, :].bitcast(FP8X4),
+                        lhsT_scale=qs[:, o, :].bitcast(U8),
+                        rhs=k_pass[h][:, o, 2 * g * GROUP : 2 * (g + 1) * GROUP].bitcast(FP4X4),
+                        rhs_scale=ks[:, o, h * HALF + g * GROUP : h * HALF + (g + 1) * GROUP],
+                        start=(o == 0),
+                        stop=(o == PASSES - 1),
+                    )
+            rows = slice(h * P // 2, (h + 1) * P // 2)
+            nc.scalar.activation(
+                th[:, :, rows], score[:].rearrange("q (p t) -> q t p", t=PACK), ACT.Tanh, scale=1.0 / CAP
+            )
+            nc.vector.tensor_scalar(
+                neg_c4[:, :, rows],
+                th[:, :, rows],
+                -CAP,
+                neg_c[:, N : N + 1] if h == 0 else neg_m[0][:],
+                ALU.mult,
+                ALU.min,
+                accum_out=neg_m[h][:],
+            )
+
+        prob = sb.tile([P, N + 1], F32, name="prob", align_bytes=64)
+        total = sb.tile([P, 1], F32, name="total")
+        nc.scalar.activation(prob[:], neg_c[:], ACT.Exp, bias=neg_m[1][:], scale=-1.0, accum_out=total[:])
+        prob_t = ps.tile([P, PACK, P], F32, name="prob_t")
+        for t in range(PACK):
+            nc.tensor.transpose(prob_t[:, t, :], prob[:, t * P : (t + 1) * P], ident[:])
+
+        vs_g = sb.tile([P, N], F32, name="vs_g", tag="early", align_bytes=64)
+        nc.vector.tensor_copy(vs_g[:], vs_pool[:].indirect(offsets[:]))
+        vs_t = ps.tile([P, PACK, P], F32, name="vs_t")
+        for t in range(PACK):
+            nc.tensor.transpose(vs_t[:, t, :], vs_g[:, t:N:PACK], ident[:])
+        vs_col = sb.tile([P, PACK], F32, name="vs_col")
+        nc.scalar.copy(vs_col[:], vs_t[:, :, VS_ROW])
+
+        w = sb.tile([P, NQ, PACK], BF16, name="w", align_bytes=64)
+        nc.vector.tensor_tensor(
+            w[:],
+            prob_t[:].rearrange("p t q -> p q t"),
+            vs_col[:].unsqueeze(1).broadcast_to([P, NQ, PACK]),
+            ALU.mult,
+        )
+        w_codes = sb.tile([P, NQ], U32, name="w_codes", align_bytes=64)
+        w_scales = sb.tile([P, NQ], U8, name="w_scales", align_bytes=64)
+        nc.vector.quantize_mx(w_codes[:].bitcast(FP8X4), w_scales[:], w[:].rearrange("p q t -> p (q t)"))
+        inv_total = sb.tile([P, 1], F32, name="inv_total")
+        nc.vector.reciprocal(inv_total[:], total[:])
+
+        v_g = sb.tile([P, 2, 2, P, 2], BF16, name="v_g", tag="late", align_bytes=64)
+        for h in range(2):
+            nc.vector.tensor_copy(v_g[:, h].rearrange("e u s j -> e s u j"), v_pool[:, h, :].indirect(offsets[:]))
+            v_words = v_g[:, h].rearrange("e u s j -> e u (s j)").bitcast(F32)
+            v_t = ps.tile([P, 2, P], F32, name="v_t%d" % h)
+            for u in range(2):
+                nc.tensor.transpose(v_t[:, u, :], v_words[:, u, :], ident[:])
+            v_b = sb.tile([P, P * PACK], BF16, name="v_b%d" % h, align_bytes=64)
+            nc.scalar.copy(
+                v_b[:].bitcast(F32).rearrange("p (e u) -> p e u", u=2), v_t[:].rearrange("p u e -> p e u")
+            )
+            v_codes = sb.tile([P, P], U32, name="v_codes%d" % h, align_bytes=64)
+            v_scales = sb.tile([P, P], U8, name="v_scales%d" % h, align_bytes=64)
+            nc.vector.quantize_mx(v_codes[:].bitcast(FP8X4), v_scales[:], v_b[:])
+            y = ps.tile([P, P], F32, name="y%d" % h)
+            nc.tensor.matmul_mx(
+                y[:],
+                lhsT=w_codes[:].bitcast(FP8X4),
+                lhsT_scale=w_scales[:],
+                rhs=v_codes[:].bitcast(FP8X4),
+                rhs_scale=v_scales[:],
+                start=True,
+                stop=True,
+            )
+            y_sb = sb.tile([P, P], F32, name="y_sb%d" % h, align_bytes=64)
+            if h == 0:
+                nc.scalar.activation(y_sb[:], y[:], ACT.Copy, scale=inv_total[:])
+                nc.scalar.dma_start(out[0][:, h * P : (h + 1) * P], y_sb[:])
+            else:
+                nc.vector.tensor_scalar(y_sb[:], y[:], inv_total[:], None, ALU.mult)
+                nc.sync.dma_start(out[0][:, h * P : (h + 1) * P], y_sb[:])

@@ -34,49 +34,55 @@ def tile_attend_soft_cap_sink_srtq128n512t2048_kernel(
     with ExitStack() as ctx:
         sb = ctx.enter_context(tc.tile_pool(name="sb", bufs=1))
         ps = ctx.enter_context(tc.psum_pool(name="ps", bufs=1))
+        reuse = ctx.enter_context(tc.tile_pool(name="reuse", bufs=1))
 
         offsets = sb.tile([P, N // 16], U16, name="offsets")
         nc.sync.dma_start(offsets[:], offs)
 
-        k_pool = sb.tile([P, T], I32, name="k_pool", align_bytes=64)
-        nc.scalar.dma_start(k_pool[:], k_words[0].rearrange("g t b -> g (t b)").bitcast(I32))
-
-        zero = sb.tile([P, 1], F32, name="zero")
-        nc.gpsimd.memset(zero[:], 0.0)
-        warm = sb.tile([P, 1], F32, name="warm", tag="values", align_bytes=64)
-        nc.scalar.activation(warm[:], zero[:], ACT.Exp)
-
-        ks_pool = sb.tile([P, PASSES, T // 4], I32, name="ks_pool", tag="early", align_bytes=64)
+        ks_pool = sb.tile([P, PASSES, T // 4], I32, name="ks_pool", align_bytes=64)
         nc.vector.memset(ks_pool[:], 0)
-        ks_rows = k_scales.bitcast(I32).rearrange("o (Q r) t -> r Q o t", r=4)
-        for r in range(4):
-            nc.sync.dma_start(ks_pool[r:P:32, :, :], ks_rows[r])
+        ks_rows = k_scales.bitcast(I32).rearrange("o (Q r) t -> Q r o t", r=4)
+        for Q in range(4):
+            nc.sync.dma_start(ks_pool[32 * Q : 32 * Q + 4, :, :], ks_rows[Q])
 
-        v_pool = sb.tile([P, 2, T], F32, name="v_pool", tag="values", align_bytes=64)
-        for h in range(2):
-            nc.scalar.dma_start(v_pool[:, h, :], vT[h * P : (h + 1) * P, :])
-
-        qs = sb.tile([P, PASSES, NQ // 4], I32, name="qs", align_bytes=64)
-        nc.vector.memset(qs[:], 0)
         vs_pool = sb.tile([P, T], F32, name="vs_pool", align_bytes=64)
         nc.vector.memset(vs_pool[:], 0.0)
+        qs = sb.tile([P, PASSES, NQ // 4], I32, name="qs", align_bytes=64)
+        nc.vector.memset(qs[:], 0)
 
         qw = sb.tile([P, PASSES, NQ], I32, name="qw", align_bytes=64)
         nc.sync.dma_start(qw[:], q_words[0].rearrange("o g q r -> g o (q r)").bitcast(I32))
-        qs_rows = q_scales[0].bitcast(I32).rearrange("o (Q r) q -> r Q o q", r=4)
-        for r in range(4):
-            nc.sync.dma_start(qs[r:P:32, :, :], qs_rows[r])
         sink_col = sb.tile([P, 1], F32, name="sink_col")
-        nc.gpsimd.dma_start(sink_col[:], sink[0])
+        nc.sync.dma_start(sink_col[:], sink[0])
+
+        k_pool = sb.tile([P, T], I32, name="k_pool", align_bytes=64)
+        nc.sync.dma_start(k_pool[:], k_words[0].rearrange("g t b -> g (t b)").bitcast(I32))
+
+        nc.sync.dma_start(vs_pool[VS_ROW : VS_ROW + 1, :], vs[0:1, :])
+        qs_rows = q_scales[0].bitcast(I32).rearrange("o (Q r) q -> Q r o q", r=4)
+        for Q in range(4):
+            nc.sync.dma_start(qs[32 * Q : 32 * Q + 4, :, :], qs_rows[Q])
+
+        v_pool = [
+            sb.tile([P, T], F32, name="v_pool0", align_bytes=64),
+            reuse.tile([P, T], F32, name="v_pool1", align_bytes=64, offset=0),
+        ]
+        for h in range(2):
+            nc.sync.dma_start(v_pool[h][:], vT[h * P : (h + 1) * P, :])
+
+        zero = sb.tile([P, 1], F32, name="zero")
+        nc.gpsimd.memset(zero[:], 0.0)
+        warm = sb.tile([P, 1], F32, name="warm")
+        nc.scalar.activation(warm[:], zero[:], ACT.Exp)
+
         ident = sb.tile([P, P], F32, name="ident", align_bytes=64)
         make_identity(nc, ident[:])
-        nc.sync.dma_start(vs_pool[VS_ROW : VS_ROW + 1, :], vs[0:1, :])
 
         ks = sb.tile([P, PASSES, N], U8, name="ks", align_bytes=64)
         for o in range(PASSES):
             nc.vector.tensor_copy(ks[:, o, :], ks_pool[:, o, :].bitcast(U8).indirect(offsets[:]))
 
-        neg_c = sb.tile([P, N + 1], F32, name="neg_c", align_bytes=64)
+        neg_c = sb.tile([P, N + 1], F32, name="neg_c", tag="mid", align_bytes=64)
         nc.scalar.activation(neg_c[:, N : N + 1], sink_col[:], ACT.Copy, scale=-1.0)
 
         k_both = sb.tile([P, 2, HALF], I32, name="k_both", tag="early", align_bytes=64)
@@ -91,22 +97,24 @@ def tile_attend_soft_cap_sink_srtq128n512t2048_kernel(
             )
 
         th = sb.tile([P, PACK, P], F32, name="th", tag="late", align_bytes=64)
-        neg_m = [sb.tile([P, 1], F32, name="neg_m%d" % h) for h in range(2)]
+        pieces = [(0, 2), (2, 3), (3, 4)]
+        neg_m = [sb.tile([P, 1], F32, name="neg_m%d" % i) for i in range(len(pieces))]
         neg_c4 = neg_c[:, 0:N].rearrange("q (t p) -> q t p", t=PACK)
-        for h in range(2):
-            score = ps.tile([P, HALF], F32, name="score%d" % h)
-            for g in range(HALF // GROUP):
+        for i, (g0, g1) in enumerate(pieces):
+            score = ps.tile([P, (g1 - g0) * GROUP], F32, name="score%d" % i, tag="bank%d" % i)
+            for g in range(g0, g1):
+                h, gh = divmod(g, HALF // GROUP)
                 for o in range(PASSES):
                     nc.tensor.matmul_mx(
-                        score[:, g * GROUP : (g + 1) * GROUP],
+                        score[:, (g - g0) * GROUP : (g - g0 + 1) * GROUP],
                         lhsT=qw[:, o, :].bitcast(FP8X4),
                         lhsT_scale=qs[:, o, :].bitcast(U8),
-                        rhs=k_pass[h][:, o, 2 * g * GROUP : 2 * (g + 1) * GROUP].bitcast(FP4X4),
-                        rhs_scale=ks[:, o, h * HALF + g * GROUP : h * HALF + (g + 1) * GROUP],
+                        rhs=k_pass[h][:, o, 2 * gh * GROUP : 2 * (gh + 1) * GROUP].bitcast(FP4X4),
+                        rhs_scale=ks[:, o, g * GROUP : (g + 1) * GROUP],
                         start=(o == 0),
                         stop=(o == PASSES - 1),
                     )
-            rows = slice(h * P // 2, (h + 1) * P // 2)
+            rows = slice(g0 * GROUP // PACK, g1 * GROUP // PACK)
             nc.scalar.activation(
                 th[:, :, rows], score[:].rearrange("q (p t) -> q t p", t=PACK), ACT.Tanh, scale=1.0 / CAP
             )
@@ -114,28 +122,47 @@ def tile_attend_soft_cap_sink_srtq128n512t2048_kernel(
                 neg_c4[:, :, rows],
                 th[:, :, rows],
                 -CAP,
-                neg_c[:, N : N + 1] if h == 0 else neg_m[0][:],
+                neg_c[:, N : N + 1] if i == 0 else neg_m[i - 1][:],
                 ALU.mult,
                 ALU.min,
-                accum_out=neg_m[h][:],
+                accum_out=neg_m[i][:],
             )
 
         prob = sb.tile([P, N + 1], F32, name="prob", align_bytes=64)
-        total = sb.tile([P, 1], F32, name="total")
-        nc.scalar.activation(prob[:], neg_c[:], ACT.Exp, bias=neg_m[1][:], scale=-1.0, accum_out=total[:])
+        total = sb.tile([P, 2], F32, name="total")
         prob_t = ps.tile([P, PACK, P], F32, name="prob_t")
-        for t in range(PACK):
-            nc.tensor.transpose(prob_t[:, t, :], prob[:, t * P : (t + 1) * P], ident[:])
+        for u, (c0, c1) in enumerate([(0, HALF), (HALF, N + 1)]):
+            nc.scalar.activation(
+                prob[:, c0:c1], neg_c[:, c0:c1], ACT.Exp, bias=neg_m[-1][:], scale=-1.0, accum_out=total[:, u : u + 1]
+            )
+            for t in range(2 * u, 2 * u + 2):
+                nc.tensor.transpose(prob_t[:, t, :], prob[:, t * P : (t + 1) * P], ident[:])
 
         vs_g = sb.tile([P, N], F32, name="vs_g", tag="early", align_bytes=64)
         nc.vector.tensor_copy(vs_g[:], vs_pool[:].indirect(offsets[:]))
-        vs_t = ps.tile([P, PACK, P], F32, name="vs_t")
+        vs_t = ps.tile([P, PACK, P], F32, name="vs_t", tag="bank2")
         for t in range(PACK):
             nc.tensor.transpose(vs_t[:, t, :], vs_g[:, t:N:PACK], ident[:])
-        vs_col = sb.tile([P, PACK], F32, name="vs_col")
+        vs_col = sb.tile([P, PACK], F32, name="vs_col", tag="mid", align_bytes=64)
         nc.scalar.copy(vs_col[:], vs_t[:, :, VS_ROW])
 
-        w = sb.tile([P, NQ, PACK], BF16, name="w", align_bytes=64)
+        v_g = sb.tile([P, 2, 2, P, 2], BF16, name="v_g", tag="late", align_bytes=64)
+        v_b = [
+            reuse.tile([P, P * PACK], BF16, name="v_b0", align_bytes=64, offset=1024),
+            sb.tile([P, P * PACK], BF16, name="v_b1", align_bytes=64),
+        ]
+        v_t = [ps.tile([P, 2, P], F32, name="v_t%d" % h) for h in range(2)]
+        for h in range(2):
+            nc.vector.tensor_copy(v_g[:, h].rearrange("e u s j -> e s u j"), v_pool[h][:].indirect(offsets[:]))
+            v_words = v_g[:, h].rearrange("e u s j -> e u (s j)").bitcast(F32)
+            for u in range(2):
+                nc.tensor.transpose(v_t[h][:, u, :], v_words[:, u, :], ident[:])
+        for h in range(2):
+            nc.scalar.copy(
+                v_b[h][:].bitcast(F32).rearrange("p (e u) -> p e u", u=2), v_t[h][:].rearrange("p u e -> p e u")
+            )
+
+        w = reuse.tile([P, NQ, PACK], BF16, name="w", align_bytes=64, offset=0)
         nc.vector.tensor_tensor(
             w[:],
             prob_t[:].rearrange("p t q -> p q t"),
@@ -146,23 +173,15 @@ def tile_attend_soft_cap_sink_srtq128n512t2048_kernel(
         w_scales = sb.tile([P, NQ], U8, name="w_scales", align_bytes=64)
         nc.vector.quantize_mx(w_codes[:].bitcast(FP8X4), w_scales[:], w[:].rearrange("p q t -> p (q t)"))
         inv_total = sb.tile([P, 1], F32, name="inv_total")
-        nc.vector.reciprocal(inv_total[:], total[:])
+        both = reuse.tile([P, 1], F32, name="both", align_bytes=64, offset=2048)
+        nc.vector.tensor_tensor(both[:], total[:, 0:1], total[:, 1:2], ALU.add)
+        nc.vector.reciprocal(inv_total[:], both[:])
 
-        v_g = sb.tile([P, 2, 2, P, 2], BF16, name="v_g", tag="late", align_bytes=64)
         for h in range(2):
-            nc.vector.tensor_copy(v_g[:, h].rearrange("e u s j -> e s u j"), v_pool[:, h, :].indirect(offsets[:]))
-            v_words = v_g[:, h].rearrange("e u s j -> e u (s j)").bitcast(F32)
-            v_t = ps.tile([P, 2, P], F32, name="v_t%d" % h)
-            for u in range(2):
-                nc.tensor.transpose(v_t[:, u, :], v_words[:, u, :], ident[:])
-            v_b = sb.tile([P, P * PACK], BF16, name="v_b%d" % h, align_bytes=64)
-            nc.scalar.copy(
-                v_b[:].bitcast(F32).rearrange("p (e u) -> p e u", u=2), v_t[:].rearrange("p u e -> p e u")
-            )
             v_codes = sb.tile([P, P], U32, name="v_codes%d" % h, align_bytes=64)
             v_scales = sb.tile([P, P], U8, name="v_scales%d" % h, align_bytes=64)
-            nc.vector.quantize_mx(v_codes[:].bitcast(FP8X4), v_scales[:], v_b[:])
-            y = ps.tile([P, P], F32, name="y%d" % h)
+            nc.vector.quantize_mx(v_codes[:].bitcast(FP8X4), v_scales[:], v_b[h][:])
+            y = ps.tile([P, P], F32, name="y%d" % h, tag="bank%d" % h)
             nc.tensor.matmul_mx(
                 y[:],
                 lhsT=w_codes[:].bitcast(FP8X4),

@@ -34,41 +34,41 @@ def tile_attend_soft_cap_sink_srtq128n512t2048_kernel(
     with ExitStack() as ctx:
         sb = ctx.enter_context(tc.tile_pool(name="sb", bufs=1))
         ps = ctx.enter_context(tc.psum_pool(name="ps", bufs=1))
-        reuse = ctx.enter_context(tc.tile_pool(name="reuse", bufs=1))
+        before_w = ctx.enter_context(tc.tile_pool(name="before_w", bufs=1))
+        after_exp = ctx.enter_context(tc.tile_pool(name="after_exp", bufs=1))
 
         offsets = sb.tile([P, N // 16], U16, name="offsets")
         nc.sync.dma_start(offsets[:], offs)
 
-        ks_pool = sb.tile([P, PASSES, T // 4], I32, name="ks_pool", align_bytes=64)
+        ks_pool = before_w.tile([P, T // 4], I32, name="ks_pool", align_bytes=64, offset=0)
         nc.vector.memset(ks_pool[:], 0)
-        ks_rows = k_scales.bitcast(I32).rearrange("o (Q r) t -> Q r o t", r=4)
+        ks_rows = k_scales.bitcast(I32)
         for Q in range(4):
-            nc.sync.dma_start(ks_pool[32 * Q : 32 * Q + 4, :, :], ks_rows[Q])
+            nc.sync.dma_start(ks_pool[32 * Q : 32 * Q + 8, :], ks_rows[:, 4 * Q : 4 * Q + 4, :])
+
+        qs = sb.tile([P, PASSES, NQ // 4], I32, name="qs", align_bytes=64)
+        nc.vector.memset(qs[:], 0)
+        qs_rows = q_scales[0].bitcast(I32).rearrange("o (Q r) q -> Q r o q", r=4)
 
         vs_pool = sb.tile([P, T], F32, name="vs_pool", align_bytes=64)
         nc.vector.memset(vs_pool[:], 0.0)
-        qs = sb.tile([P, PASSES, NQ // 4], I32, name="qs", align_bytes=64)
-        nc.vector.memset(qs[:], 0)
+        ks1 = sb.tile([P, N // 4], I32, name="ks1", align_bytes=64)
+        nc.vector.memset(ks1[:], 0)
 
         qw = sb.tile([P, PASSES, NQ], I32, name="qw", align_bytes=64)
         nc.sync.dma_start(qw[:], q_words[0].rearrange("o g q r -> g o (q r)").bitcast(I32))
-        sink_col = sb.tile([P, 1], F32, name="sink_col")
-        nc.sync.dma_start(sink_col[:], sink[0])
+        nc.sync.dma_start(qs[0:4, :, :], qs_rows[0])
 
         k_pool = sb.tile([P, T], I32, name="k_pool", align_bytes=64)
         nc.sync.dma_start(k_pool[:], k_words[0].rearrange("g t b -> g (t b)").bitcast(I32))
-
-        nc.sync.dma_start(vs_pool[VS_ROW : VS_ROW + 1, :], vs[0:1, :])
-        qs_rows = q_scales[0].bitcast(I32).rearrange("o (Q r) q -> Q r o q", r=4)
-        for Q in range(4):
+        for Q in range(1, 4):
             nc.sync.dma_start(qs[32 * Q : 32 * Q + 4, :, :], qs_rows[Q])
 
-        v_pool = [
-            sb.tile([P, T], F32, name="v_pool0", align_bytes=64),
-            reuse.tile([P, T], F32, name="v_pool1", align_bytes=64, offset=0),
-        ]
-        for h in range(2):
-            nc.sync.dma_start(v_pool[h][:], vT[h * P : (h + 1) * P, :])
+        v_pool0 = sb.tile([P, T], F32, name="v_pool0", align_bytes=64)
+        nc.sync.dma_start(v_pool0[:], vT[0:P, :])
+        nc.sync.dma_start(vs_pool[VS_ROW : VS_ROW + 1, :], vs[0:1, :])
+        sink_col = sb.tile([P, 1], F32, name="sink_col")
+        nc.sync.dma_start(sink_col[:], sink[0])
 
         zero = sb.tile([P, 1], F32, name="zero")
         nc.gpsimd.memset(zero[:], 0.0)
@@ -78,91 +78,110 @@ def tile_attend_soft_cap_sink_srtq128n512t2048_kernel(
         ident = sb.tile([P, P], F32, name="ident", align_bytes=64)
         make_identity(nc, ident[:])
 
-        ks = sb.tile([P, PASSES, N], U8, name="ks", align_bytes=64)
-        for o in range(PASSES):
-            nc.vector.tensor_copy(ks[:, o, :], ks_pool[:, o, :].bitcast(U8).indirect(offsets[:]))
+        ks0 = sb.tile([P, N // 4], I32, name="ks0", align_bytes=64)
+        nc.vector.tensor_copy(ks0[:].bitcast(U8), ks_pool[:].bitcast(U8).indirect(offsets[:]))
+        for Q in range(4):
+            nc.sync.dma_start(ks1[32 * Q : 32 * Q + 4, :], ks0[32 * Q + 4 : 32 * Q + 8, :])
+        ks = [ks0[:].bitcast(U8), ks1[:].bitcast(U8)]
 
-        neg_c = sb.tile([P, N + 1], F32, name="neg_c", tag="mid", align_bytes=64)
+        v_pool1 = before_w.tile([P, T], F32, name="v_pool1", align_bytes=64, offset=0)
+        nc.sync.dma_start(v_pool1[:], vT[P : 2 * P, :])
+        v_pool = [v_pool0, v_pool1]
+
+        neg_c = after_exp.tile([P, N + 1], F32, name="neg_c", align_bytes=64, offset=0)
         nc.scalar.activation(neg_c[:, N : N + 1], sink_col[:], ACT.Copy, scale=-1.0)
 
-        k_both = sb.tile([P, 2, HALF], I32, name="k_both", tag="early", align_bytes=64)
+        k_both = [sb.tile([P, HALF], I32, name="k_both%d" % h, tag="k_both%d" % h, align_bytes=64) for h in range(2)]
         k_pass = [sb.tile([P, PASSES, 2 * HALF], U8, name="k_pass%d" % h, align_bytes=64) for h in range(2)]
         cols = HALF // 16
         for h in range(2):
             nc.vector.tensor_copy(
-                k_both[:, h, :].bitcast(U32), k_pool[:].bitcast(U32).indirect(offsets[:, h * cols : (h + 1) * cols])
+                k_both[h][:].bitcast(U32), k_pool[:].bitcast(U32).indirect(offsets[:, h * cols : (h + 1) * cols])
             )
             nc.vector.tensor_copy(
-                k_pass[h][:].bitcast(U16), k_both[:, h, :].bitcast(U16).rearrange("p (i o) -> p o i", o=PASSES)
+                k_pass[h][:].bitcast(U16), k_both[h][:].bitcast(U16).rearrange("p (i o) -> p o i", o=PASSES)
             )
 
-        th = sb.tile([P, PACK, P], F32, name="th", tag="late", align_bytes=64)
-        pieces = [(0, 2), (2, 3), (3, 4)]
-        neg_m = [sb.tile([P, 1], F32, name="neg_m%d" % i) for i in range(len(pieces))]
-        neg_c4 = neg_c[:, 0:N].rearrange("q (t p) -> q t p", t=PACK)
-        for i, (g0, g1) in enumerate(pieces):
-            score = ps.tile([P, (g1 - g0) * GROUP], F32, name="score%d" % i, tag="bank%d" % i)
-            for g in range(g0, g1):
+        groups = N // GROUP
+        score = [ps.tile([P, GROUP], F32, name="score%d" % g, tag="bank%d" % g) for g in range(groups)]
+        th = sb.tile([P, PACK, P], F32, name="th", tag="th", align_bytes=64)
+        for o in range(PASSES):
+            for g in range(groups):
                 h, gh = divmod(g, HALF // GROUP)
-                for o in range(PASSES):
-                    nc.tensor.matmul_mx(
-                        score[:, (g - g0) * GROUP : (g - g0 + 1) * GROUP],
-                        lhsT=qw[:, o, :].bitcast(FP8X4),
-                        lhsT_scale=qs[:, o, :].bitcast(U8),
-                        rhs=k_pass[h][:, o, 2 * gh * GROUP : 2 * (gh + 1) * GROUP].bitcast(FP4X4),
-                        rhs_scale=ks[:, o, g * GROUP : (g + 1) * GROUP],
-                        start=(o == 0),
-                        stop=(o == PASSES - 1),
-                    )
-            rows = slice(g0 * GROUP // PACK, g1 * GROUP // PACK)
+                nc.tensor.matmul_mx(
+                    score[g][:],
+                    lhsT=qw[:, o, :].bitcast(FP8X4),
+                    lhsT_scale=qs[:, o, :].bitcast(U8),
+                    rhs=k_pass[h][:, o, 2 * gh * GROUP : 2 * (gh + 1) * GROUP].bitcast(FP4X4),
+                    rhs_scale=ks[o][:, g * GROUP : (g + 1) * GROUP],
+                    start=(o == 0),
+                    stop=(o == PASSES - 1),
+                )
+        for g in range(groups):
+            rows = slice(g * GROUP // PACK, (g + 1) * GROUP // PACK)
             nc.scalar.activation(
-                th[:, :, rows], score[:].rearrange("q (p t) -> q t p", t=PACK), ACT.Tanh, scale=1.0 / CAP
+                th[:, :, rows], score[g][:].rearrange("q (p t) -> q t p", t=PACK), ACT.Tanh, scale=1.0 / CAP
             )
-            nc.vector.tensor_scalar(
-                neg_c4[:, :, rows],
-                th[:, :, rows],
-                -CAP,
-                neg_c[:, N : N + 1] if i == 0 else neg_m[i - 1][:],
-                ALU.mult,
-                ALU.min,
-                accum_out=neg_m[i][:],
-            )
+
+        vs_g = sb.tile([P, N], F32, name="vs_g", tag="k_both0", align_bytes=64)
+        nc.vector.tensor_copy(vs_g[:], vs_pool[:].indirect(offsets[:]))
+
+        def gather_values(h, tag):
+            v_g = sb.tile([P, 2, P, 2], BF16, name="v_g%d" % h, tag=tag, align_bytes=64)
+            nc.vector.tensor_copy(v_g[:].rearrange("e u s j -> e s u j"), v_pool[h][:].indirect(offsets[:]))
+            return v_g
+
+        def turn_values(h, v_g, tag):
+            v_t = ps.tile([P, 2, P], F32, name="v_t%d" % h, tag=tag)
+            v_words = v_g[:].rearrange("e u s j -> e u (s j)").bitcast(F32)
+            for u in range(2):
+                nc.tensor.transpose(v_t[:, u, :], v_words[:, u, :], ident[:])
+            return v_t
+
+        v_g0 = sb.tile([P, N], F32, name="v_g0", align_bytes=64)
+        nc.vector.tensor_copy(v_g0[:], v_pool[0][:].indirect(offsets[:]))
+
+        neg_m_tile = sb.tile([P, 1], F32, name="neg_m")
+        neg_m = neg_m_tile[:, 0:1]
+        nc.vector.tensor_scalar(
+            neg_c[:, 0:N],
+            th[:].rearrange("q t p -> q (t p)"),
+            -CAP,
+            neg_c[:, N : N + 1],
+            ALU.mult,
+            ALU.min,
+            accum_out=neg_m,
+        )
+        v_g1 = gather_values(1, "v_g1")
 
         prob = sb.tile([P, N + 1], F32, name="prob", align_bytes=64)
         total = sb.tile([P, 2], F32, name="total")
         prob_t = ps.tile([P, PACK, P], F32, name="prob_t")
         for u, (c0, c1) in enumerate([(0, HALF), (HALF, N + 1)]):
             nc.scalar.activation(
-                prob[:, c0:c1], neg_c[:, c0:c1], ACT.Exp, bias=neg_m[-1][:], scale=-1.0, accum_out=total[:, u : u + 1]
+                prob[:, c0:c1], neg_c[:, c0:c1], ACT.Exp, bias=neg_m, scale=-1.0, accum_out=total[:, u : u + 1]
             )
             for t in range(2 * u, 2 * u + 2):
                 nc.tensor.transpose(prob_t[:, t, :], prob[:, t * P : (t + 1) * P], ident[:])
 
-        vs_g = sb.tile([P, N], F32, name="vs_g", tag="early", align_bytes=64)
-        nc.vector.tensor_copy(vs_g[:], vs_pool[:].indirect(offsets[:]))
-        vs_t = ps.tile([P, PACK, P], F32, name="vs_t", tag="bank2")
+        vs_t = ps.tile([P, PACK, P], F32, name="vs_t", tag="bank3")
         for t in range(PACK):
             nc.tensor.transpose(vs_t[:, t, :], vs_g[:, t:N:PACK], ident[:])
-        vs_col = sb.tile([P, PACK], F32, name="vs_col", tag="mid", align_bytes=64)
+        vs_col = after_exp.tile([P, PACK], F32, name="vs_col", align_bytes=64, offset=0)
         nc.scalar.copy(vs_col[:], vs_t[:, :, VS_ROW])
 
-        v_g = sb.tile([P, 2, 2, P, 2], BF16, name="v_g", tag="late", align_bytes=64)
+        v_t0 = ps.tile([P, PACK, P], F32, name="v_t0", tag="bank2")
+        for t in range(PACK):
+            nc.tensor.transpose(v_t0[:, t, :], v_g0[:, t:N:PACK], ident[:])
+        v_t1 = turn_values(1, v_g1, "v_t1")
         v_b = [
-            reuse.tile([P, P * PACK], BF16, name="v_b0", align_bytes=64, offset=1024),
+            after_exp.tile([P, P * PACK], BF16, name="v_b0", align_bytes=64, offset=64),
             sb.tile([P, P * PACK], BF16, name="v_b1", align_bytes=64),
         ]
-        v_t = [ps.tile([P, 2, P], F32, name="v_t%d" % h) for h in range(2)]
-        for h in range(2):
-            nc.vector.tensor_copy(v_g[:, h].rearrange("e u s j -> e s u j"), v_pool[h][:].indirect(offsets[:]))
-            v_words = v_g[:, h].rearrange("e u s j -> e u (s j)").bitcast(F32)
-            for u in range(2):
-                nc.tensor.transpose(v_t[h][:, u, :], v_words[:, u, :], ident[:])
-        for h in range(2):
-            nc.scalar.copy(
-                v_b[h][:].bitcast(F32).rearrange("p (e u) -> p e u", u=2), v_t[h][:].rearrange("p u e -> p e u")
-            )
+        nc.scalar.copy(v_b[0][:].rearrange("p (e t) -> p e t", t=PACK), v_t0[:].rearrange("p t e -> p e t"))
+        nc.scalar.copy(v_b[1][:].bitcast(F32).rearrange("p (e u) -> p e u", u=2), v_t1[:].rearrange("p u e -> p e u"))
 
-        w = reuse.tile([P, NQ, PACK], BF16, name="w", align_bytes=64, offset=0)
+        w = before_w.tile([P, NQ, PACK], BF16, name="w", align_bytes=64, offset=0)
         nc.vector.tensor_tensor(
             w[:],
             prob_t[:].rearrange("p t q -> p q t"),
@@ -173,13 +192,16 @@ def tile_attend_soft_cap_sink_srtq128n512t2048_kernel(
         w_scales = sb.tile([P, NQ], U8, name="w_scales", align_bytes=64)
         nc.vector.quantize_mx(w_codes[:].bitcast(FP8X4), w_scales[:], w[:].rearrange("p q t -> p (q t)"))
         inv_total = sb.tile([P, 1], F32, name="inv_total")
-        both = reuse.tile([P, 1], F32, name="both", align_bytes=64, offset=2048)
+        both = before_w.tile([P, 1], F32, name="both", align_bytes=64, offset=2048)
         nc.vector.tensor_tensor(both[:], total[:, 0:1], total[:, 1:2], ALU.add)
         nc.vector.reciprocal(inv_total[:], both[:])
 
         for h in range(2):
             v_codes = sb.tile([P, P], U32, name="v_codes%d" % h, align_bytes=64)
-            v_scales = sb.tile([P, P], U8, name="v_scales%d" % h, align_bytes=64)
+            if h == 0:
+                v_scales = before_w.tile([P, P], U8, name="v_scales0", align_bytes=64, offset=1024)
+            else:
+                v_scales = sb.tile([P, P], U8, name="v_scales1", align_bytes=64)
             nc.vector.quantize_mx(v_codes[:].bitcast(FP8X4), v_scales[:], v_b[h][:])
             y = ps.tile([P, P], F32, name="y%d" % h, tag="bank%d" % h)
             nc.tensor.matmul_mx(

@@ -6,7 +6,7 @@ from concourse.masks import make_identity
 N, T, D, DV, NQ = 512, 2048, 1024, 256, 128
 CAP = 2.0
 FLOPS = 2 * NQ * N * (D + DV)
-BYTES = 128 * T * 4 + 32 * T + 128 * 2 * NQ * 4 + 32 * NQ + DV * T * 4 + T * 4 + NQ * 4 + 128 * 64 + NQ * DV * 4
+BYTES = D * T // 2 + D // 32 * T + D * NQ + D // 32 * NQ + 4 * DV * T + 4 * T + 4 * NQ + 128 * 2 * N // 16 + 4 * NQ * DV
 
 F32 = mybir.dt.float32
 BF16 = mybir.dt.bfloat16
@@ -21,7 +21,8 @@ ACT = mybir.ActivationFunctionType
 
 P = 128
 PACK = 4
-PASSES = D // 512
+PASSES = D // (P * PACK)
+QUADRANTS = 4
 HALF = N // 2
 GROUP = 128
 VS_ROW = 8
@@ -34,39 +35,40 @@ def tile_attend_soft_cap_sink_srtq128n512t2048_kernel(
     with ExitStack() as ctx:
         sb = ctx.enter_context(tc.tile_pool(name="sb", bufs=1))
         ps = ctx.enter_context(tc.psum_pool(name="ps", bufs=1))
-        before_w = ctx.enter_context(tc.tile_pool(name="before_w", bufs=1))
+        last_values = ctx.enter_context(tc.tile_pool(name="last_values", bufs=1))
         after_exp = ctx.enter_context(tc.tile_pool(name="after_exp", bufs=1))
 
         offsets = sb.tile([P, N // 16], U16, name="offsets")
         nc.sync.dma_start(offsets[:], offs)
 
-        ks_pool = before_w.tile([P, T // 4], I32, name="ks_pool", align_bytes=64, offset=0)
+        k_pool = sb.tile([P, T], I32, name="k_pool", align_bytes=64)
+        k_rows = k_words[0].rearrange("g t b -> g (t b)").bitcast(I32)
+        nc.sync.dma_start(k_pool[:, 0 : T // 2], k_rows[:, 0 : T // 2])
+
+        ks_pool = last_values.tile([P, T // 4], I32, name="ks_pool", align_bytes=64, offset=0)
         nc.vector.memset(ks_pool[:], 0)
         ks_rows = k_scales.bitcast(I32)
-        for Q in range(4):
-            nc.sync.dma_start(ks_pool[32 * Q : 32 * Q + 8, :], ks_rows[:, 4 * Q : 4 * Q + 4, :])
-
-        qs = sb.tile([P, PASSES, NQ // 4], I32, name="qs", align_bytes=64)
-        nc.vector.memset(qs[:], 0)
-        qs_rows = q_scales[0].bitcast(I32).rearrange("o (Q r) q -> Q r o q", r=4)
-
-        vs_pool = sb.tile([P, T], F32, name="vs_pool", align_bytes=64)
-        nc.vector.memset(vs_pool[:], 0.0)
-        ks1 = sb.tile([P, N // 4], I32, name="ks1", align_bytes=64)
-        nc.vector.memset(ks1[:], 0)
+        nc.sync.dma_start(ks_pool[4:P:8, :], ks_rows[1])
+        for Q in range(QUADRANTS):
+            nc.sync.dma_start(ks_pool[32 * Q : 32 * Q + 4, :], ks_rows[0, 4 * Q : 4 * Q + 4, :])
+        nc.sync.dma_start(k_pool[:, T // 2 : T], k_rows[:, T // 2 : T])
 
         qw = sb.tile([P, PASSES, NQ], I32, name="qw", align_bytes=64)
         nc.sync.dma_start(qw[:], q_words[0].rearrange("o g q r -> g o (q r)").bitcast(I32))
-        nc.sync.dma_start(qs[0:4, :, :], qs_rows[0])
-
-        k_pool = sb.tile([P, T], I32, name="k_pool", align_bytes=64)
-        nc.sync.dma_start(k_pool[:], k_words[0].rearrange("g t b -> g (t b)").bitcast(I32))
-        for Q in range(1, 4):
+        qs = sb.tile([P, PASSES, NQ // 4], I32, name="qs", align_bytes=64)
+        nc.vector.memset(qs[:], 0)
+        qs_rows = q_scales[0].bitcast(I32).rearrange("o (Q r) q -> Q r o q", r=4)
+        for Q in range(QUADRANTS):
             nc.sync.dma_start(qs[32 * Q : 32 * Q + 4, :, :], qs_rows[Q])
+
+        vs_pool = sb.tile([P, T], F32, name="vs_pool", align_bytes=64)
+        nc.vector.memset(vs_pool[:], 0.0)
+        nc.sync.dma_start(vs_pool[VS_ROW : VS_ROW + 1, :], vs[0:1, :])
+        ks1 = sb.tile([P, N // 4], I32, name="ks1", align_bytes=64)
+        nc.vector.memset(ks1[:], 0)
 
         v_pool0 = sb.tile([P, T], F32, name="v_pool0", align_bytes=64)
         nc.sync.dma_start(v_pool0[:], vT[0:P, :])
-        nc.sync.dma_start(vs_pool[VS_ROW : VS_ROW + 1, :], vs[0:1, :])
         sink_col = sb.tile([P, 1], F32, name="sink_col")
         nc.sync.dma_start(sink_col[:], sink[0])
 
@@ -80,23 +82,23 @@ def tile_attend_soft_cap_sink_srtq128n512t2048_kernel(
 
         ks0 = sb.tile([P, N // 4], I32, name="ks0", align_bytes=64)
         nc.vector.tensor_copy(ks0[:].bitcast(U8), ks_pool[:].bitcast(U8).indirect(offsets[:]))
-        for Q in range(4):
-            nc.sync.dma_start(ks1[32 * Q : 32 * Q + 4, :], ks0[32 * Q + 4 : 32 * Q + 8, :])
+        for Q in range(QUADRANTS):
+            nc.sync.dma_start(ks1[32 * Q : 32 * Q + 4, :], ks0[32 * Q + 4 : 32 * Q + 32 : 8, :])
         ks = [ks0[:].bitcast(U8), ks1[:].bitcast(U8)]
 
-        v_pool1 = before_w.tile([P, T], F32, name="v_pool1", align_bytes=64, offset=0)
+        v_pool1 = last_values.tile([P, T], F32, name="v_pool1", align_bytes=64, offset=0)
         nc.sync.dma_start(v_pool1[:], vT[P : 2 * P, :])
-        v_pool = [v_pool0, v_pool1]
 
         neg_c = after_exp.tile([P, N + 1], F32, name="neg_c", align_bytes=64, offset=0)
         nc.scalar.activation(neg_c[:, N : N + 1], sink_col[:], ACT.Copy, scale=-1.0)
 
         k_both = [sb.tile([P, HALF], I32, name="k_both%d" % h, tag="k_both%d" % h, align_bytes=64) for h in range(2)]
         k_pass = [sb.tile([P, PASSES, 2 * HALF], U8, name="k_pass%d" % h, align_bytes=64) for h in range(2)]
-        cols = HALF // 16
+        list_cols = HALF // 16
         for h in range(2):
             nc.vector.tensor_copy(
-                k_both[h][:].bitcast(U32), k_pool[:].bitcast(U32).indirect(offsets[:, h * cols : (h + 1) * cols])
+                k_both[h][:].bitcast(U32),
+                k_pool[:].bitcast(U32).indirect(offsets[:, h * list_cols : (h + 1) * list_cols]),
             )
             nc.vector.tensor_copy(
                 k_pass[h][:].bitcast(U16), k_both[h][:].bitcast(U16).rearrange("p (i o) -> p o i", o=PASSES)
@@ -104,45 +106,32 @@ def tile_attend_soft_cap_sink_srtq128n512t2048_kernel(
 
         groups = N // GROUP
         score = [ps.tile([P, GROUP], F32, name="score%d" % g, tag="bank%d" % g) for g in range(groups)]
-        th = sb.tile([P, PACK, P], F32, name="th", tag="th", align_bytes=64)
+        th = sb.tile([P, PACK, P], F32, name="th", align_bytes=64)
         for o in range(PASSES):
             for g in range(groups):
-                h, gh = divmod(g, HALF // GROUP)
+                h, g_in_half = divmod(g, HALF // GROUP)
                 nc.tensor.matmul_mx(
                     score[g][:],
                     lhsT=qw[:, o, :].bitcast(FP8X4),
                     lhsT_scale=qs[:, o, :].bitcast(U8),
-                    rhs=k_pass[h][:, o, 2 * gh * GROUP : 2 * (gh + 1) * GROUP].bitcast(FP4X4),
+                    rhs=k_pass[h][:, o, 2 * g_in_half * GROUP : 2 * (g_in_half + 1) * GROUP].bitcast(FP4X4),
                     rhs_scale=ks[o][:, g * GROUP : (g + 1) * GROUP],
                     start=(o == 0),
                     stop=(o == PASSES - 1),
                 )
         for g in range(groups):
-            rows = slice(g * GROUP // PACK, (g + 1) * GROUP // PACK)
+            p_range = slice(g * GROUP // PACK, (g + 1) * GROUP // PACK)
             nc.scalar.activation(
-                th[:, :, rows], score[g][:].rearrange("q (p t) -> q t p", t=PACK), ACT.Tanh, scale=1.0 / CAP
+                th[:, :, p_range], score[g][:].rearrange("q (p t) -> q t p", t=PACK), ACT.Tanh, scale=1.0 / CAP
             )
 
         vs_g = sb.tile([P, N], F32, name="vs_g", tag="k_both0", align_bytes=64)
         nc.vector.tensor_copy(vs_g[:], vs_pool[:].indirect(offsets[:]))
 
-        def gather_values(h, tag):
-            v_g = sb.tile([P, 2, P, 2], BF16, name="v_g%d" % h, tag=tag, align_bytes=64)
-            nc.vector.tensor_copy(v_g[:].rearrange("e u s j -> e s u j"), v_pool[h][:].indirect(offsets[:]))
-            return v_g
-
-        def turn_values(h, v_g, tag):
-            v_t = ps.tile([P, 2, P], F32, name="v_t%d" % h, tag=tag)
-            v_words = v_g[:].rearrange("e u s j -> e u (s j)").bitcast(F32)
-            for u in range(2):
-                nc.tensor.transpose(v_t[:, u, :], v_words[:, u, :], ident[:])
-            return v_t
-
         v_g0 = sb.tile([P, N], F32, name="v_g0", align_bytes=64)
-        nc.vector.tensor_copy(v_g0[:], v_pool[0][:].indirect(offsets[:]))
+        nc.vector.tensor_copy(v_g0[:], v_pool0[:].indirect(offsets[:]))
 
-        neg_m_tile = sb.tile([P, 1], F32, name="neg_m")
-        neg_m = neg_m_tile[:, 0:1]
+        neg_m = sb.tile([P, 1], F32, name="neg_m")
         nc.vector.tensor_scalar(
             neg_c[:, 0:N],
             th[:].rearrange("q t p -> q (t p)"),
@@ -150,18 +139,25 @@ def tile_attend_soft_cap_sink_srtq128n512t2048_kernel(
             neg_c[:, N : N + 1],
             ALU.mult,
             ALU.min,
-            accum_out=neg_m,
+            accum_out=neg_m[:],
         )
-        v_g1 = gather_values(1, "v_g1")
+
+        v_g1 = sb.tile([P, 2, P, 2], BF16, name="v_g1", align_bytes=64)
+        nc.vector.tensor_copy(v_g1[:].rearrange("e u s j -> e s u j"), v_pool1[:].indirect(offsets[:]))
 
         prob = sb.tile([P, N + 1], F32, name="prob", align_bytes=64)
         total = sb.tile([P, 2], F32, name="total")
         prob_t = ps.tile([P, PACK, P], F32, name="prob_t")
-        for u, (c0, c1) in enumerate([(0, HALF), (HALF, N + 1)]):
+        for part, (c0, c1) in enumerate([(0, N // 2), (N // 2, N + 1)]):
             nc.scalar.activation(
-                prob[:, c0:c1], neg_c[:, c0:c1], ACT.Exp, bias=neg_m, scale=-1.0, accum_out=total[:, u : u + 1]
+                prob[:, c0:c1],
+                neg_c[:, c0:c1],
+                ACT.Exp,
+                bias=neg_m[:],
+                scale=-1.0,
+                accum_out=total[:, part : part + 1],
             )
-            for t in range(2 * u, 2 * u + 2):
+            for t in range(2 * part, 2 * part + 2):
                 nc.tensor.transpose(prob_t[:, t, :], prob[:, t * P : (t + 1) * P], ident[:])
 
         vs_t = ps.tile([P, PACK, P], F32, name="vs_t", tag="bank3")
@@ -173,7 +169,10 @@ def tile_attend_soft_cap_sink_srtq128n512t2048_kernel(
         v_t0 = ps.tile([P, PACK, P], F32, name="v_t0", tag="bank2")
         for t in range(PACK):
             nc.tensor.transpose(v_t0[:, t, :], v_g0[:, t:N:PACK], ident[:])
-        v_t1 = turn_values(1, v_g1, "v_t1")
+        v_t1 = ps.tile([P, 2, P], F32, name="v_t1")
+        v_words = v_g1[:].rearrange("e u s j -> e u (s j)").bitcast(F32)
+        for u in range(2):
+            nc.tensor.transpose(v_t1[:, u, :], v_words[:, u, :], ident[:])
         v_b = [
             after_exp.tile([P, P * PACK], BF16, name="v_b0", align_bytes=64, offset=64),
             sb.tile([P, P * PACK], BF16, name="v_b1", align_bytes=64),
@@ -181,7 +180,7 @@ def tile_attend_soft_cap_sink_srtq128n512t2048_kernel(
         nc.scalar.copy(v_b[0][:].rearrange("p (e t) -> p e t", t=PACK), v_t0[:].rearrange("p t e -> p e t"))
         nc.scalar.copy(v_b[1][:].bitcast(F32).rearrange("p (e u) -> p e u", u=2), v_t1[:].rearrange("p u e -> p e u"))
 
-        w = before_w.tile([P, NQ, PACK], BF16, name="w", align_bytes=64, offset=0)
+        w = last_values.tile([P, NQ, PACK], BF16, name="w", align_bytes=64, offset=0)
         nc.vector.tensor_tensor(
             w[:],
             prob_t[:].rearrange("p t q -> p q t"),
@@ -192,14 +191,14 @@ def tile_attend_soft_cap_sink_srtq128n512t2048_kernel(
         w_scales = sb.tile([P, NQ], U8, name="w_scales", align_bytes=64)
         nc.vector.quantize_mx(w_codes[:].bitcast(FP8X4), w_scales[:], w[:].rearrange("p q t -> p (q t)"))
         inv_total = sb.tile([P, 1], F32, name="inv_total")
-        both = before_w.tile([P, 1], F32, name="both", align_bytes=64, offset=2048)
-        nc.vector.tensor_tensor(both[:], total[:, 0:1], total[:, 1:2], ALU.add)
-        nc.vector.reciprocal(inv_total[:], both[:])
+        total_sum = last_values.tile([P, 1], F32, name="total_sum", align_bytes=64, offset=2048)
+        nc.vector.tensor_tensor(total_sum[:], total[:, 0:1], total[:, 1:2], ALU.add)
+        nc.vector.reciprocal(inv_total[:], total_sum[:])
 
         for h in range(2):
             v_codes = sb.tile([P, P], U32, name="v_codes%d" % h, align_bytes=64)
             if h == 0:
-                v_scales = before_w.tile([P, P], U8, name="v_scales0", align_bytes=64, offset=1024)
+                v_scales = last_values.tile([P, P], U8, name="v_scales0", align_bytes=64, offset=1024)
             else:
                 v_scales = sb.tile([P, P], U8, name="v_scales1", align_bytes=64)
             nc.vector.quantize_mx(v_codes[:].bitcast(FP8X4), v_scales[:], v_b[h][:])

@@ -25,6 +25,8 @@ PASSES = D // (P * PACK)
 QUADRANTS = 4
 HALF = N // 2
 GROUP = 128
+V_FIRST = 1536
+K_FIRST = 512
 VS_ROW = 8
 
 
@@ -35,6 +37,7 @@ def tile_attend_soft_cap_sink_srtq128n512t2048_kernel(
     with ExitStack() as ctx:
         sb = ctx.enter_context(tc.tile_pool(name="sb", bufs=1))
         ps = ctx.enter_context(tc.psum_pool(name="ps", bufs=1))
+        first_values = ctx.enter_context(tc.tile_pool(name="first_values", bufs=1))
         last_values = ctx.enter_context(tc.tile_pool(name="last_values", bufs=1))
         after_exp = ctx.enter_context(tc.tile_pool(name="after_exp", bufs=1))
 
@@ -43,51 +46,50 @@ def tile_attend_soft_cap_sink_srtq128n512t2048_kernel(
 
         k_pool = sb.tile([P, T], I32, name="k_pool", align_bytes=64)
         k_rows = k_words[0].rearrange("g t b -> g (t b)").bitcast(I32)
-        nc.sync.dma_start(k_pool[:, 0 : T // 2], k_rows[:, 0 : T // 2])
+        nc.sync.dma_start(k_pool[:, 0:K_FIRST], k_rows[:, 0:K_FIRST])
 
-        ks_pool = last_values.tile([P, T // 4], I32, name="ks_pool", align_bytes=64, offset=0)
+        ks_pool = sb.tile([P, T // 4], I32, name="ks_pool", align_bytes=64)
         nc.vector.memset(ks_pool[:], 0)
         ks_rows = k_scales.bitcast(I32)
-        nc.sync.dma_start(ks_pool[4:P:8, :], ks_rows[1])
-        for Q in range(QUADRANTS):
-            nc.sync.dma_start(ks_pool[32 * Q : 32 * Q + 4, :], ks_rows[0, 4 * Q : 4 * Q + 4, :])
-        nc.sync.dma_start(k_pool[:, T // 2 : T], k_rows[:, T // 2 : T])
+        nc.scalar.dma_start(ks_pool[4:P:8, :], ks_rows[1])
+        for r in range(4):
+            queue = nc.scalar if r == 0 else nc.sync
+            queue.dma_start(ks_pool[r:P:32, :], ks_rows[0, r:16:4, :])
+        nc.sync.dma_start(k_pool[:, K_FIRST:T], k_rows[:, K_FIRST:T])
 
-        qw = sb.tile([P, PASSES, NQ], I32, name="qw", align_bytes=64)
-        nc.sync.dma_start(qw[:], q_words[0].rearrange("o g q r -> g o (q r)").bitcast(I32))
         qs = sb.tile([P, PASSES, NQ // 4], I32, name="qs", align_bytes=64)
         nc.vector.memset(qs[:], 0)
-        qs_rows = q_scales[0].bitcast(I32).rearrange("o (Q r) q -> Q r o q", r=4)
-        for Q in range(QUADRANTS):
-            nc.sync.dma_start(qs[32 * Q : 32 * Q + 4, :, :], qs_rows[Q])
+        qs_rows = q_scales[0].bitcast(I32).rearrange("o (Q r) q -> r Q o q", r=4)
+        for r in range(4):
+            nc.sync.dma_start(qs[r:P:32, :, :], qs_rows[r])
+        qw = sb.tile([P, PASSES, NQ], I32, name="qw", align_bytes=64)
+        nc.sync.dma_start(qw[:], q_words[0].rearrange("o g q r -> g o (q r)").bitcast(I32))
 
-        vs_pool = sb.tile([P, T], F32, name="vs_pool", align_bytes=64)
-        nc.vector.memset(vs_pool[:], 0.0)
-        nc.sync.dma_start(vs_pool[VS_ROW : VS_ROW + 1, :], vs[0:1, :])
         ks1 = sb.tile([P, N // 4], I32, name="ks1", align_bytes=64)
         nc.vector.memset(ks1[:], 0)
+        vs_pool = sb.tile([P, T], F32, name="vs_pool", align_bytes=64)
+        nc.vector.memset(vs_pool[:, 0 : T // 2], 0.0)
+        nc.gpsimd.memset(vs_pool[:, T // 2 : T], 0.0)
+        nc.sync.dma_start(vs_pool[VS_ROW : VS_ROW + 1, :], vs[0:1, :])
 
-        v_pool0 = sb.tile([P, T], F32, name="v_pool0", align_bytes=64)
-        nc.sync.dma_start(v_pool0[:], vT[0:P, :])
         sink_col = sb.tile([P, 1], F32, name="sink_col")
-        nc.sync.dma_start(sink_col[:], sink[0])
-
-        zero = sb.tile([P, 1], F32, name="zero")
-        nc.gpsimd.memset(zero[:], 0.0)
-        warm = sb.tile([P, 1], F32, name="warm")
-        nc.scalar.activation(warm[:], zero[:], ACT.Exp)
-
+        nc.gpsimd.dma_start(sink_col[:], sink[0])
         ident = sb.tile([P, P], F32, name="ident", align_bytes=64)
         make_identity(nc, ident[:])
+        v_pool = [
+            first_values.tile([P, T], F32, name="v_pool0", align_bytes=64, offset=0),
+            last_values.tile([P, T], F32, name="v_pool1", align_bytes=64, offset=0),
+        ]
+        nc.sync.dma_start(v_pool[0][:, 0:V_FIRST], vT[0:P, 0:V_FIRST])
 
         ks0 = sb.tile([P, N // 4], I32, name="ks0", align_bytes=64)
         nc.vector.tensor_copy(ks0[:].bitcast(U8), ks_pool[:].bitcast(U8).indirect(offsets[:]))
-        for Q in range(QUADRANTS):
-            nc.sync.dma_start(ks1[32 * Q : 32 * Q + 4, :], ks0[32 * Q + 4 : 32 * Q + 32 : 8, :])
+        for r in range(4):
+            nc.sync.dma_start(ks1[r:P:32, :], ks0[8 * r + 4 : P : 32, :])
         ks = [ks0[:].bitcast(U8), ks1[:].bitcast(U8)]
 
-        v_pool1 = last_values.tile([P, T], F32, name="v_pool1", align_bytes=64, offset=0)
-        nc.sync.dma_start(v_pool1[:], vT[P : 2 * P, :])
+        nc.sync.dma_start(v_pool[0][:, V_FIRST:T], vT[0:P, V_FIRST:T])
+        nc.sync.dma_start(v_pool[1][:], vT[P : 2 * P, :])
 
         neg_c = after_exp.tile([P, N + 1], F32, name="neg_c", align_bytes=64, offset=0)
         nc.scalar.activation(neg_c[:, N : N + 1], sink_col[:], ACT.Copy, scale=-1.0)
@@ -100,9 +102,13 @@ def tile_attend_soft_cap_sink_srtq128n512t2048_kernel(
                 k_both[h][:].bitcast(U32),
                 k_pool[:].bitcast(U32).indirect(offsets[:, h * list_cols : (h + 1) * list_cols]),
             )
-            nc.vector.tensor_copy(
-                k_pass[h][:].bitcast(U16), k_both[h][:].bitcast(U16).rearrange("p (i o) -> p o i", o=PASSES)
-            )
+        for o in range(PASSES):
+            for h in range(2):
+                nc.vector.tensor_copy(k_pass[h][:, o, :].bitcast(U16), k_both[h][:].bitcast(U16)[:, o : 2 * HALF : PASSES])
+
+        v_g = [sb.tile([P, N], BF16, name="v_g%d" % h, align_bytes=64) for h in range(2)]
+        inv_cap = v_g[0][:, N - 2 : N].bitcast(F32)
+        nc.gpsimd.memset(inv_cap, 1.0 / CAP)
 
         groups = N // GROUP
         score = [ps.tile([P, GROUP], F32, name="score%d" % g, tag="bank%d" % g) for g in range(groups)]
@@ -122,14 +128,16 @@ def tile_attend_soft_cap_sink_srtq128n512t2048_kernel(
         for g in range(groups):
             p_range = slice(g * GROUP // PACK, (g + 1) * GROUP // PACK)
             nc.scalar.activation(
-                th[:, :, p_range], score[g][:].rearrange("q (p t) -> q t p", t=PACK), ACT.Tanh, scale=1.0 / CAP
+                th[:, :, p_range],
+                score[g][:].rearrange("q (p t) -> q t p", t=PACK),
+                ACT.Tanh,
+                scale=inv_cap if g == groups - 1 else 1.0 / CAP,
             )
 
         vs_g = sb.tile([P, N], F32, name="vs_g", tag="k_both0", align_bytes=64)
         nc.vector.tensor_copy(vs_g[:], vs_pool[:].indirect(offsets[:]))
 
-        v_g0 = sb.tile([P, N], F32, name="v_g0", align_bytes=64)
-        nc.vector.tensor_copy(v_g0[:], v_pool0[:].indirect(offsets[:]))
+        nc.vector.tensor_copy(v_g[0][:, 0:HALF], v_pool[0][:].indirect(offsets[:, 0:list_cols]))
 
         neg_m = sb.tile([P, 1], F32, name="neg_m")
         nc.vector.tensor_scalar(
@@ -141,44 +149,35 @@ def tile_attend_soft_cap_sink_srtq128n512t2048_kernel(
             ALU.min,
             accum_out=neg_m[:],
         )
-
-        v_g1 = sb.tile([P, 2, P, 2], BF16, name="v_g1", align_bytes=64)
-        nc.vector.tensor_copy(v_g1[:].rearrange("e u s j -> e s u j"), v_pool1[:].indirect(offsets[:]))
+        nc.vector.tensor_copy(v_g[0][:, HALF:N], v_pool[0][:].indirect(offsets[:, list_cols : 2 * list_cols]))
+        nc.vector.tensor_copy(v_g[1][:], v_pool[1][:].indirect(offsets[:]))
 
         prob = sb.tile([P, N + 1], F32, name="prob", align_bytes=64)
-        total = sb.tile([P, 2], F32, name="total")
-        prob_t = ps.tile([P, PACK, P], F32, name="prob_t")
-        for part, (c0, c1) in enumerate([(0, N // 2), (N // 2, N + 1)]):
-            nc.scalar.activation(
-                prob[:, c0:c1],
-                neg_c[:, c0:c1],
-                ACT.Exp,
-                bias=neg_m[:],
-                scale=-1.0,
-                accum_out=total[:, part : part + 1],
-            )
-            for t in range(2 * part, 2 * part + 2):
-                nc.tensor.transpose(prob_t[:, t, :], prob[:, t * P : (t + 1) * P], ident[:])
+        total = sb.tile([P, 1], F32, name="total")
+        nc.scalar.activation(prob[:], neg_c[:], ACT.Exp, bias=neg_m[:], scale=-1.0, accum_out=total[:])
 
-        vs_t = ps.tile([P, PACK, P], F32, name="vs_t", tag="bank3")
+        vs_t = ps.tile([P, PACK, P], F32, name="vs_t", tag="bank0")
         for t in range(PACK):
             nc.tensor.transpose(vs_t[:, t, :], vs_g[:, t:N:PACK], ident[:])
+        v_t = [ps.tile([P, 2, P], F32, name="v_t0", tag="bank1"), ps.tile([P, 2, P], F32, name="v_t1")]
+        prob_t = ps.tile([P, PACK, P], F32, name="prob_t")
+        for u in range(2):
+            nc.tensor.transpose(v_t[0][:, u, :], v_g[0][:].bitcast(F32)[:, u : N // 2 : 2], ident[:])
+        for t in range(PACK):
+            nc.tensor.transpose(prob_t[:, t, :], prob[:, t * P : (t + 1) * P], ident[:])
+        for u in range(2):
+            nc.tensor.transpose(v_t[1][:, u, :], v_g[1][:].bitcast(F32)[:, u : N // 2 : 2], ident[:])
+
         vs_col = after_exp.tile([P, PACK], F32, name="vs_col", align_bytes=64, offset=0)
         nc.scalar.copy(vs_col[:], vs_t[:, :, VS_ROW])
-
-        v_t0 = ps.tile([P, PACK, P], F32, name="v_t0", tag="bank2")
-        for t in range(PACK):
-            nc.tensor.transpose(v_t0[:, t, :], v_g0[:, t:N:PACK], ident[:])
-        v_t1 = ps.tile([P, 2, P], F32, name="v_t1")
-        v_words = v_g1[:].rearrange("e u s j -> e u (s j)").bitcast(F32)
-        for u in range(2):
-            nc.tensor.transpose(v_t1[:, u, :], v_words[:, u, :], ident[:])
         v_b = [
             after_exp.tile([P, P * PACK], BF16, name="v_b0", align_bytes=64, offset=64),
             sb.tile([P, P * PACK], BF16, name="v_b1", align_bytes=64),
         ]
-        nc.scalar.copy(v_b[0][:].rearrange("p (e t) -> p e t", t=PACK), v_t0[:].rearrange("p t e -> p e t"))
-        nc.scalar.copy(v_b[1][:].bitcast(F32).rearrange("p (e u) -> p e u", u=2), v_t1[:].rearrange("p u e -> p e u"))
+        for h in range(2):
+            nc.scalar.copy(
+                v_b[h][:].bitcast(F32).rearrange("p (e u) -> p e u", u=2), v_t[h][:].rearrange("p u e -> p e u")
+            )
 
         w = last_values.tile([P, NQ, PACK], BF16, name="w", align_bytes=64, offset=0)
         nc.vector.tensor_tensor(
@@ -187,28 +186,27 @@ def tile_attend_soft_cap_sink_srtq128n512t2048_kernel(
             vs_col[:].unsqueeze(1).broadcast_to([P, NQ, PACK]),
             ALU.mult,
         )
+        v_codes = [sb.tile([P, P], U32, name="v_codes%d" % h, align_bytes=64) for h in range(2)]
+        v_scales = [
+            last_values.tile([P, P], U8, name="v_scales0", align_bytes=64, offset=1024),
+            sb.tile([P, P], U8, name="v_scales1", align_bytes=64),
+        ]
         w_codes = sb.tile([P, NQ], U32, name="w_codes", align_bytes=64)
         w_scales = sb.tile([P, NQ], U8, name="w_scales", align_bytes=64)
+        inv_total = last_values.tile([P, 1], F32, name="inv_total", align_bytes=64, offset=2048)
+        nc.vector.quantize_mx(v_codes[0][:].bitcast(FP8X4), v_scales[0][:], v_b[0][:])
         nc.vector.quantize_mx(w_codes[:].bitcast(FP8X4), w_scales[:], w[:].rearrange("p q t -> p (q t)"))
-        inv_total = sb.tile([P, 1], F32, name="inv_total")
-        total_sum = last_values.tile([P, 1], F32, name="total_sum", align_bytes=64, offset=2048)
-        nc.vector.tensor_tensor(total_sum[:], total[:, 0:1], total[:, 1:2], ALU.add)
-        nc.vector.reciprocal(inv_total[:], total_sum[:])
+        nc.vector.quantize_mx(v_codes[1][:].bitcast(FP8X4), v_scales[1][:], v_b[1][:])
+        nc.vector.reciprocal(inv_total[:], total[:])
 
         for h in range(2):
-            v_codes = sb.tile([P, P], U32, name="v_codes%d" % h, align_bytes=64)
-            if h == 0:
-                v_scales = last_values.tile([P, P], U8, name="v_scales0", align_bytes=64, offset=1024)
-            else:
-                v_scales = sb.tile([P, P], U8, name="v_scales1", align_bytes=64)
-            nc.vector.quantize_mx(v_codes[:].bitcast(FP8X4), v_scales[:], v_b[h][:])
-            y = ps.tile([P, P], F32, name="y%d" % h, tag="bank%d" % h)
+            y = ps.tile([P, P], F32, name="y%d" % h, tag="bank%d" % (h + 2))
             nc.tensor.matmul_mx(
                 y[:],
                 lhsT=w_codes[:].bitcast(FP8X4),
                 lhsT_scale=w_scales[:],
-                rhs=v_codes[:].bitcast(FP8X4),
-                rhs_scale=v_scales[:],
+                rhs=v_codes[h][:].bitcast(FP8X4),
+                rhs_scale=v_scales[h][:],
                 start=True,
                 stop=True,
             )

@@ -25,7 +25,6 @@ PASSES = D // (P * PACK)
 QUADRANTS = 4
 HALF = N // 2
 GROUP = 128
-V_FIRST = 1536
 K_FIRST = 512
 VS_ROW = 8
 
@@ -65,22 +64,25 @@ def tile_attend_soft_cap_sink_srtq128n512t2048_kernel(
         qw = sb.tile([P, PASSES, NQ], I32, name="qw", align_bytes=64)
         nc.sync.dma_start(qw[:], q_words[0].rearrange("o g q r -> g o (q r)").bitcast(I32))
 
-        ks1 = sb.tile([P, N // 4], I32, name="ks1", align_bytes=64)
-        nc.vector.memset(ks1[:], 0)
         vs_pool = sb.tile([P, T], F32, name="vs_pool", align_bytes=64)
-        nc.vector.memset(vs_pool[:, 0 : T // 2], 0.0)
-        nc.gpsimd.memset(vs_pool[:, T // 2 : T], 0.0)
+        nc.vector.memset(vs_pool[:], 0.0)
         nc.sync.dma_start(vs_pool[VS_ROW : VS_ROW + 1, :], vs[0:1, :])
 
-        sink_col = sb.tile([P, 1], F32, name="sink_col")
-        nc.gpsimd.dma_start(sink_col[:], sink[0])
+        ks1 = sb.tile([P, N // 4], I32, name="ks1", align_bytes=64)
+        nc.vector.memset(ks1[:], 0)
         ident = sb.tile([P, P], F32, name="ident", align_bytes=64)
-        make_identity(nc, ident[:])
+        nc.vector.memset(ident[:], 0.0)
+        make_identity(nc, ident[:], nomemset=True)
+        v_g = [sb.tile([P, N], BF16, name="v_g%d" % h, align_bytes=64) for h in range(2)]
+        inv_cap = v_g[0][:, N - 2 : N].bitcast(F32)
+        nc.vector.memset(inv_cap, 1.0 / CAP)
+        no_bias = v_g[1][:, 0:2].bitcast(F32)
+        nc.vector.memset(no_bias, 0.0)
         v_pool = [
             first_values.tile([P, T], F32, name="v_pool0", align_bytes=64, offset=0),
             last_values.tile([P, T], F32, name="v_pool1", align_bytes=64, offset=0),
         ]
-        nc.sync.dma_start(v_pool[0][:, 0:V_FIRST], vT[0:P, 0:V_FIRST])
+        nc.sync.dma_start(v_pool[0][:], vT[0:P, :])
 
         ks0 = sb.tile([P, N // 4], I32, name="ks0", align_bytes=64)
         nc.vector.tensor_copy(ks0[:].bitcast(U8), ks_pool[:].bitcast(U8).indirect(offsets[:]))
@@ -88,7 +90,8 @@ def tile_attend_soft_cap_sink_srtq128n512t2048_kernel(
             nc.sync.dma_start(ks1[r:P:32, :], ks0[8 * r + 4 : P : 32, :])
         ks = [ks0[:].bitcast(U8), ks1[:].bitcast(U8)]
 
-        nc.sync.dma_start(v_pool[0][:, V_FIRST:T], vT[0:P, V_FIRST:T])
+        sink_col = sb.tile([P, 1], F32, name="sink_col")
+        nc.sync.dma_start(sink_col[:], sink[0])
         nc.sync.dma_start(v_pool[1][:], vT[P : 2 * P, :])
 
         neg_c = after_exp.tile([P, N + 1], F32, name="neg_c", align_bytes=64, offset=0)
@@ -105,10 +108,6 @@ def tile_attend_soft_cap_sink_srtq128n512t2048_kernel(
         for o in range(PASSES):
             for h in range(2):
                 nc.vector.tensor_copy(k_pass[h][:, o, :].bitcast(U16), k_both[h][:].bitcast(U16)[:, o : 2 * HALF : PASSES])
-
-        v_g = [sb.tile([P, N], BF16, name="v_g%d" % h, align_bytes=64) for h in range(2)]
-        inv_cap = v_g[0][:, N - 2 : N].bitcast(F32)
-        nc.gpsimd.memset(inv_cap, 1.0 / CAP)
 
         groups = N // GROUP
         score = [ps.tile([P, GROUP], F32, name="score%d" % g, tag="bank%d" % g) for g in range(groups)]
@@ -131,6 +130,7 @@ def tile_attend_soft_cap_sink_srtq128n512t2048_kernel(
                 th[:, :, p_range],
                 score[g][:].rearrange("q (p t) -> q t p", t=PACK),
                 ACT.Tanh,
+                bias=no_bias if g == groups - 1 else 0.0,
                 scale=inv_cap if g == groups - 1 else 1.0 / CAP,
             )
 
@@ -159,7 +159,9 @@ def tile_attend_soft_cap_sink_srtq128n512t2048_kernel(
         vs_t = ps.tile([P, PACK, P], F32, name="vs_t", tag="bank0")
         for t in range(PACK):
             nc.tensor.transpose(vs_t[:, t, :], vs_g[:, t:N:PACK], ident[:])
-        v_t = [ps.tile([P, 2, P], F32, name="v_t0", tag="bank1"), ps.tile([P, 2, P], F32, name="v_t1")]
+        vs_col = after_exp.tile([P, PACK], F32, name="vs_col", align_bytes=64, offset=0)
+        nc.scalar.copy(vs_col[:], vs_t[:, :, VS_ROW])
+        v_t = [ps.tile([P, 2, P], F32, name="v_t0", tag="bank1"), ps.tile([P, 2, P], F32, name="v_t1", tag="bank0")]
         prob_t = ps.tile([P, PACK, P], F32, name="prob_t")
         for u in range(2):
             nc.tensor.transpose(v_t[0][:, u, :], v_g[0][:].bitcast(F32)[:, u : N // 2 : 2], ident[:])
@@ -168,8 +170,6 @@ def tile_attend_soft_cap_sink_srtq128n512t2048_kernel(
         for u in range(2):
             nc.tensor.transpose(v_t[1][:, u, :], v_g[1][:].bitcast(F32)[:, u : N // 2 : 2], ident[:])
 
-        vs_col = after_exp.tile([P, PACK], F32, name="vs_col", align_bytes=64, offset=0)
-        nc.scalar.copy(vs_col[:], vs_t[:, :, VS_ROW])
         v_b = [
             after_exp.tile([P, P * PACK], BF16, name="v_b0", align_bytes=64, offset=64),
             sb.tile([P, P * PACK], BF16, name="v_b1", align_bytes=64),

@@ -22,11 +22,10 @@ ACT = mybir.ActivationFunctionType
 P = 128
 PACK = 4
 PASSES = D // (P * PACK)
-QUADRANTS = 4
 HALF = N // 2
 GROUP = 128
+VS_ROW = P - 1
 K_FIRST = 512
-VS_ROW = 8
 
 
 def tile_attend_soft_cap_sink_srtq128n512t2048_kernel(
@@ -36,109 +35,100 @@ def tile_attend_soft_cap_sink_srtq128n512t2048_kernel(
     with ExitStack() as ctx:
         sb = ctx.enter_context(tc.tile_pool(name="sb", bufs=1))
         ps = ctx.enter_context(tc.psum_pool(name="ps", bufs=1))
-        first_values = ctx.enter_context(tc.tile_pool(name="first_values", bufs=1))
-        last_values = ctx.enter_context(tc.tile_pool(name="last_values", bufs=1))
+        key_words = ctx.enter_context(tc.tile_pool(name="key_words", bufs=1))
         after_exp = ctx.enter_context(tc.tile_pool(name="after_exp", bufs=1))
+        last_values = ctx.enter_context(tc.tile_pool(name="last_values", bufs=1))
 
         offsets = sb.tile([P, N // 16], U16, name="offsets")
         nc.sync.dma_start(offsets[:], offs)
 
-        k_pool = sb.tile([P, T], I32, name="k_pool", align_bytes=64)
-        k_rows = k_words[0].rearrange("g t b -> g (t b)").bitcast(I32)
-        nc.sync.dma_start(k_pool[:, 0:K_FIRST], k_rows[:, 0:K_FIRST])
-
-        ks_pool = sb.tile([P, T // 4], I32, name="ks_pool", align_bytes=64)
+        ks_pool = sb.tile([P, PASSES * T // 4], I32, name="ks_pool", align_bytes=64)
         nc.vector.memset(ks_pool[:], 0)
-        ks_rows = k_scales.bitcast(I32)
-        nc.scalar.dma_start(ks_pool[4:P:8, :], ks_rows[1])
-        for r in range(4):
-            queue = nc.scalar if r == 0 else nc.sync
-            queue.dma_start(ks_pool[r:P:32, :], ks_rows[0, r:16:4, :])
-        nc.sync.dma_start(k_pool[:, K_FIRST:T], k_rows[:, K_FIRST:T])
-
         qs = sb.tile([P, PASSES, NQ // 4], I32, name="qs", align_bytes=64)
         nc.vector.memset(qs[:], 0)
-        qs_rows = q_scales[0].bitcast(I32).rearrange("o (Q r) q -> r Q o q", r=4)
-        for r in range(4):
-            nc.sync.dma_start(qs[r:P:32, :, :], qs_rows[r])
-        qw = sb.tile([P, PASSES, NQ], I32, name="qw", align_bytes=64)
-        nc.sync.dma_start(qw[:], q_words[0].rearrange("o g q r -> g o (q r)").bitcast(I32))
-
         vs_pool = sb.tile([P, T], F32, name="vs_pool", align_bytes=64)
-        nc.vector.memset(vs_pool[:], 0.0)
-        nc.sync.dma_start(vs_pool[VS_ROW : VS_ROW + 1, :], vs[0:1, :])
-
-        ks1 = sb.tile([P, N // 4], I32, name="ks1", align_bytes=64)
-        nc.vector.memset(ks1[:], 0)
+        nc.vector.memset(vs_pool[0:VS_ROW, :], 0.0)
         ident = sb.tile([P, P], F32, name="ident", align_bytes=64)
         nc.vector.memset(ident[:], 0.0)
         make_identity(nc, ident[:], nomemset=True)
-        v_g = [sb.tile([P, N], BF16, name="v_g%d" % h, align_bytes=64) for h in range(2)]
-        inv_cap = v_g[0][:, N - 2 : N].bitcast(F32)
-        nc.vector.memset(inv_cap, 1.0 / CAP)
-        no_bias = v_g[1][:, 0:2].bitcast(F32)
-        nc.vector.memset(no_bias, 0.0)
+
+        nc.sync.dma_start(vs_pool[VS_ROW : VS_ROW + 1, :], vs[0:1, :])
+        k_pool = key_words.tile([P, T], I32, name="k_pool", align_bytes=64, offset=0)
+        k_rows = k_words[0].rearrange("g t b -> g (t b)").bitcast(I32)
+        nc.sync.dma_start(k_pool[:, 0:K_FIRST], k_rows[:, 0:K_FIRST])
+        ks_rows = k_scales.bitcast(I32).rearrange("o (Q r) t -> r Q o t", r=4)
+        for r in range(4):
+            nc.sync.dma_start(ks_pool[r:P:32, :].rearrange("Q (o t) -> Q o t", o=PASSES), ks_rows[r])
+        nc.sync.dma_start(k_pool[:, K_FIRST:T], k_rows[:, K_FIRST:T])
+        qw = sb.tile([P, PASSES, NQ], I32, name="qw", align_bytes=64)
+        nc.sync.dma_start(qw[:], q_words[0].rearrange("o g q r -> g o (q r)").bitcast(I32))
+        qs_rows = q_scales[0].bitcast(I32).rearrange("o (Q r) q -> r Q o q", r=4)
+        for r in range(4):
+            nc.sync.dma_start(qs[r:P:32, :, :], qs_rows[r])
         v_pool = [
-            first_values.tile([P, T], F32, name="v_pool0", align_bytes=64, offset=0),
+            sb.tile([P, T], F32, name="v_pool0", align_bytes=64),
             last_values.tile([P, T], F32, name="v_pool1", align_bytes=64, offset=0),
         ]
         nc.sync.dma_start(v_pool[0][:], vT[0:P, :])
-
-        ks0 = sb.tile([P, N // 4], I32, name="ks0", align_bytes=64)
-        nc.vector.tensor_copy(ks0[:].bitcast(U8), ks_pool[:].bitcast(U8).indirect(offsets[:]))
-        for r in range(4):
-            nc.sync.dma_start(ks1[r:P:32, :], ks0[8 * r + 4 : P : 32, :])
-        ks = [ks0[:].bitcast(U8), ks1[:].bitcast(U8)]
-
         sink_col = sb.tile([P, 1], F32, name="sink_col")
         nc.sync.dma_start(sink_col[:], sink[0])
         nc.sync.dma_start(v_pool[1][:], vT[P : 2 * P, :])
 
+        vs_g = sb.tile([P, N], F32, name="vs_g", align_bytes=64)
+        nc.vector.tensor_copy(vs_g[:], vs_pool[:].indirect(offsets[:]))
+        vs_t = ps.tile([P, PACK, P], F32, name="vs_t")
+        for t in range(PACK):
+            nc.tensor.transpose(vs_t[:, t, :], vs_g[:, t:N:PACK], ident[:])
+        vs_col = sb.tile([P, PACK], F32, name="vs_col", align_bytes=64)
+        nc.scalar.copy(vs_col[:], vs_t[:, :, VS_ROW])
+
+        list_cols = HALF // 16
+        halves = [offsets[:, h * list_cols : (h + 1) * list_cols] for h in range(2)]
+        ks_window = [ks_pool[:].bitcast(U8)[:, o * T : (o + 1) * T] for o in range(PASSES)]
+        ks0 = sb.tile([P, N], U8, name="ks0", align_bytes=64)
+        ks1 = [
+            sb.tile([P, HALF], U8, name="ks1a", align_bytes=64),
+            key_words.tile([P, HALF], U8, name="ks1b", align_bytes=64, offset=0),
+        ]
+        nc.vector.tensor_copy(ks0[:], ks_window[0].indirect(offsets[:]))
+        nc.vector.tensor_copy(ks1[0][:], ks_window[1].indirect(halves[0]))
+
         neg_c = after_exp.tile([P, N + 1], F32, name="neg_c", align_bytes=64, offset=0)
-        nc.scalar.activation(neg_c[:, N : N + 1], sink_col[:], ACT.Copy, scale=-1.0)
 
         k_both = [sb.tile([P, HALF], I32, name="k_both%d" % h, tag="k_both%d" % h, align_bytes=64) for h in range(2)]
         k_pass = [sb.tile([P, PASSES, 2 * HALF], U8, name="k_pass%d" % h, align_bytes=64) for h in range(2)]
-        list_cols = HALF // 16
+        for h in range(2):
+            nc.vector.tensor_copy(k_both[h][:].bitcast(U32), k_pool[:].bitcast(U32).indirect(halves[h]))
         for h in range(2):
             nc.vector.tensor_copy(
-                k_both[h][:].bitcast(U32),
-                k_pool[:].bitcast(U32).indirect(offsets[:, h * list_cols : (h + 1) * list_cols]),
+                k_pass[h][:].bitcast(U16), k_both[h][:].bitcast(U16).rearrange("p (j o) -> p o j", o=PASSES)
             )
-        for o in range(PASSES):
-            for h in range(2):
-                nc.vector.tensor_copy(k_pass[h][:, o, :].bitcast(U16), k_both[h][:].bitcast(U16)[:, o : 2 * HALF : PASSES])
+            if h == 0:
+                nc.vector.tensor_copy(ks1[1][:], ks_window[1].indirect(halves[1]))
 
         groups = N // GROUP
         score = [ps.tile([P, GROUP], F32, name="score%d" % g, tag="bank%d" % g) for g in range(groups)]
         th = sb.tile([P, PACK, P], F32, name="th", align_bytes=64)
-        for o in range(PASSES):
-            for g in range(groups):
-                h, g_in_half = divmod(g, HALF // GROUP)
+        for g in range(groups):
+            h, g_in_half = divmod(g, HALF // GROUP)
+            for o in range(PASSES):
                 nc.tensor.matmul_mx(
                     score[g][:],
                     lhsT=qw[:, o, :].bitcast(FP8X4),
                     lhsT_scale=qs[:, o, :].bitcast(U8),
                     rhs=k_pass[h][:, o, 2 * g_in_half * GROUP : 2 * (g_in_half + 1) * GROUP].bitcast(FP4X4),
-                    rhs_scale=ks[o][:, g * GROUP : (g + 1) * GROUP],
+                    rhs_scale=(ks0[:, g * GROUP : (g + 1) * GROUP], ks1[h][:, g_in_half * GROUP : (g_in_half + 1) * GROUP])[o],
                     start=(o == 0),
                     stop=(o == PASSES - 1),
                 )
-        for g in range(groups):
             p_range = slice(g * GROUP // PACK, (g + 1) * GROUP // PACK)
             nc.scalar.activation(
-                th[:, :, p_range],
-                score[g][:].rearrange("q (p t) -> q t p", t=PACK),
-                ACT.Tanh,
-                bias=no_bias if g == groups - 1 else 0.0,
-                scale=inv_cap if g == groups - 1 else 1.0 / CAP,
+                th[:, :, p_range], score[g][:].rearrange("q (p t) -> q t p", t=PACK), ACT.Tanh, scale=1.0 / CAP
             )
 
-        vs_g = sb.tile([P, N], F32, name="vs_g", tag="k_both0", align_bytes=64)
-        nc.vector.tensor_copy(vs_g[:], vs_pool[:].indirect(offsets[:]))
-
-        nc.vector.tensor_copy(v_g[0][:, 0:HALF], v_pool[0][:].indirect(offsets[:, 0:list_cols]))
-
+        nc.scalar.activation(neg_c[:, N : N + 1], sink_col[:], ACT.Copy, scale=-1.0)
+        v_g = [sb.tile([P, N], BF16, name="v_g%d" % h, align_bytes=64) for h in range(2)]
+        nc.vector.tensor_copy(v_g[0][:], v_pool[0][:].indirect(offsets[:]))
         neg_m = sb.tile([P, 1], F32, name="neg_m")
         nc.vector.tensor_scalar(
             neg_c[:, 0:N],
@@ -149,19 +139,13 @@ def tile_attend_soft_cap_sink_srtq128n512t2048_kernel(
             ALU.min,
             accum_out=neg_m[:],
         )
-        nc.vector.tensor_copy(v_g[0][:, HALF:N], v_pool[0][:].indirect(offsets[:, list_cols : 2 * list_cols]))
         nc.vector.tensor_copy(v_g[1][:], v_pool[1][:].indirect(offsets[:]))
 
         prob = sb.tile([P, N + 1], F32, name="prob", align_bytes=64)
         total = sb.tile([P, 1], F32, name="total")
         nc.scalar.activation(prob[:], neg_c[:], ACT.Exp, bias=neg_m[:], scale=-1.0, accum_out=total[:])
 
-        vs_t = ps.tile([P, PACK, P], F32, name="vs_t", tag="bank0")
-        for t in range(PACK):
-            nc.tensor.transpose(vs_t[:, t, :], vs_g[:, t:N:PACK], ident[:])
-        vs_col = after_exp.tile([P, PACK], F32, name="vs_col", align_bytes=64, offset=0)
-        nc.scalar.copy(vs_col[:], vs_t[:, :, VS_ROW])
-        v_t = [ps.tile([P, 2, P], F32, name="v_t0", tag="bank1"), ps.tile([P, 2, P], F32, name="v_t1", tag="bank0")]
+        v_t = [ps.tile([P, 2, P], F32, name="v_t0", tag="v_t0"), ps.tile([P, 2, P], F32, name="v_t1", tag="v_t0")]
         prob_t = ps.tile([P, PACK, P], F32, name="prob_t")
         for u in range(2):
             nc.tensor.transpose(v_t[0][:, u, :], v_g[0][:].bitcast(F32)[:, u : N // 2 : 2], ident[:])
@@ -169,7 +153,6 @@ def tile_attend_soft_cap_sink_srtq128n512t2048_kernel(
             nc.tensor.transpose(prob_t[:, t, :], prob[:, t * P : (t + 1) * P], ident[:])
         for u in range(2):
             nc.tensor.transpose(v_t[1][:, u, :], v_g[1][:].bitcast(F32)[:, u : N // 2 : 2], ident[:])
-
         v_b = [
             after_exp.tile([P, P * PACK], BF16, name="v_b0", align_bytes=64, offset=64),
             sb.tile([P, P * PACK], BF16, name="v_b1", align_bytes=64),

@@ -103,24 +103,27 @@ def tile_attend_soft_cap_sink_srtq128n512t2048_kernel(
             nc.vector.tensor_copy(
                 k_pass[h][:].bitcast(U16), k_both[h][:].bitcast(U16).rearrange("p (j o) -> p o j", o=PASSES)
             )
-            if h == 0:
-                nc.vector.tensor_copy(ks1[1][:], ks_window[1].indirect(halves[1]))
+        nc.vector.tensor_copy(ks1[1][:], ks_window[1].indirect(halves[1]))
 
         groups = N // GROUP
         score = [ps.tile([P, GROUP], F32, name="score%d" % g, tag="bank%d" % g) for g in range(groups)]
         th = sb.tile([P, PACK, P], F32, name="th", align_bytes=64)
-        for g in range(groups):
-            h, g_in_half = divmod(g, HALF // GROUP)
+        per_half = HALF // GROUP
+        for h in range(2):
             for o in range(PASSES):
-                nc.tensor.matmul_mx(
-                    score[g][:],
-                    lhsT=qw[:, o, :].bitcast(FP8X4),
-                    lhsT_scale=qs[:, o, :].bitcast(U8),
-                    rhs=k_pass[h][:, o, 2 * g_in_half * GROUP : 2 * (g_in_half + 1) * GROUP].bitcast(FP4X4),
-                    rhs_scale=(ks0[:, g * GROUP : (g + 1) * GROUP], ks1[h][:, g_in_half * GROUP : (g_in_half + 1) * GROUP])[o],
-                    start=(o == 0),
-                    stop=(o == PASSES - 1),
-                )
+                for j in range(per_half):
+                    g = h * per_half + j
+                    key_scales = ks0[:, g * GROUP : (g + 1) * GROUP] if o == 0 else ks1[h][:, j * GROUP : (j + 1) * GROUP]
+                    nc.tensor.matmul_mx(
+                        score[g][:],
+                        lhsT=qw[:, o, :].bitcast(FP8X4),
+                        lhsT_scale=qs[:, o, :].bitcast(U8),
+                        rhs=k_pass[h][:, o, 2 * j * GROUP : 2 * (j + 1) * GROUP].bitcast(FP4X4),
+                        rhs_scale=key_scales,
+                        start=(o == 0),
+                        stop=(o == PASSES - 1),
+                    )
+        for g in range(groups):
             p_range = slice(g * GROUP // PACK, (g + 1) * GROUP // PACK)
             nc.scalar.activation(
                 th[:, :, p_range], score[g][:].rearrange("q (p t) -> q t p", t=PACK), ACT.Tanh, scale=1.0 / CAP
@@ -142,8 +145,11 @@ def tile_attend_soft_cap_sink_srtq128n512t2048_kernel(
         nc.vector.tensor_copy(v_g[1][:], v_pool[1][:].indirect(offsets[:]))
 
         prob = sb.tile([P, N + 1], F32, name="prob", align_bytes=64)
-        total = sb.tile([P, 1], F32, name="total")
-        nc.scalar.activation(prob[:], neg_c[:], ACT.Exp, bias=neg_m[:], scale=-1.0, accum_out=total[:])
+        part_sum = [sb.tile([P, 1], F32, name="part_sum%d" % h) for h in range(2)]
+        for h, cols in enumerate((slice(0, HALF), slice(HALF, N + 1))):
+            nc.scalar.activation(
+                prob[:, cols], neg_c[:, cols], ACT.Exp, bias=neg_m[:], scale=-1.0, accum_out=part_sum[h][:]
+            )
 
         v_t = [ps.tile([P, 2, P], F32, name="v_t0", tag="v_t0"), ps.tile([P, 2, P], F32, name="v_t1", tag="v_t0")]
         prob_t = ps.tile([P, PACK, P], F32, name="prob_t")
@@ -162,6 +168,8 @@ def tile_attend_soft_cap_sink_srtq128n512t2048_kernel(
                 v_b[h][:].bitcast(F32).rearrange("p (e u) -> p e u", u=2), v_t[h][:].rearrange("p u e -> p e u")
             )
 
+        total = sb.tile([P, 1], F32, name="total")
+        nc.scalar.activation(total[:], part_sum[0][:], ACT.Identity, bias=part_sum[1][:])
         w = last_values.tile([P, NQ, PACK], BF16, name="w", align_bytes=64, offset=0)
         nc.vector.tensor_tensor(
             w[:],

@@ -35,30 +35,31 @@ def tile_attend_soft_cap_sink_srtq128n512t2048_kernel(
     with ExitStack() as ctx:
         sb = ctx.enter_context(tc.tile_pool(name="sb", bufs=1))
         ps = ctx.enter_context(tc.psum_pool(name="ps", bufs=1))
-        key_words = ctx.enter_context(tc.tile_pool(name="key_words", bufs=1))
         after_exp = ctx.enter_context(tc.tile_pool(name="after_exp", bufs=1))
         last_values = ctx.enter_context(tc.tile_pool(name="last_values", bufs=1))
 
         offsets = sb.tile([P, N // 16], U16, name="offsets")
         nc.sync.dma_start(offsets[:], offs)
 
-        ks_pool = sb.tile([P, PASSES * T // 4], I32, name="ks_pool", align_bytes=64)
+        ks_pool = sb.tile([P, T // 4], I32, name="ks_pool", align_bytes=64)
         nc.vector.memset(ks_pool[:], 0)
         qs = sb.tile([P, PASSES, NQ // 4], I32, name="qs", align_bytes=64)
         nc.vector.memset(qs[:], 0)
         vs_pool = sb.tile([P, T], F32, name="vs_pool", align_bytes=64)
         nc.vector.memset(vs_pool[0:VS_ROW, :], 0.0)
+        ks1 = sb.tile([P, N // 4], I32, name="ks1", align_bytes=64)
+        nc.vector.memset(ks1[:], 0)
         ident = sb.tile([P, P], F32, name="ident", align_bytes=64)
         nc.vector.memset(ident[:], 0.0)
         make_identity(nc, ident[:], nomemset=True)
 
         nc.sync.dma_start(vs_pool[VS_ROW : VS_ROW + 1, :], vs[0:1, :])
-        k_pool = key_words.tile([P, T], I32, name="k_pool", align_bytes=64, offset=0)
+        k_pool = sb.tile([P, T], I32, name="k_pool", align_bytes=64)
         k_rows = k_words[0].rearrange("g t b -> g (t b)").bitcast(I32)
         nc.sync.dma_start(k_pool[:, 0:K_FIRST], k_rows[:, 0:K_FIRST])
         ks_rows = k_scales.bitcast(I32).rearrange("o (Q r) t -> r Q o t", r=4)
         for r in range(4):
-            nc.sync.dma_start(ks_pool[r:P:32, :].rearrange("Q (o t) -> Q o t", o=PASSES), ks_rows[r])
+            nc.sync.dma_start(ks_pool[r:P:16, :], ks_rows[r])
         nc.sync.dma_start(k_pool[:, K_FIRST:T], k_rows[:, K_FIRST:T])
         qw = sb.tile([P, PASSES, NQ], I32, name="qw", align_bytes=64)
         nc.sync.dma_start(qw[:], q_words[0].rearrange("o g q r -> g o (q r)").bitcast(I32))
@@ -70,9 +71,6 @@ def tile_attend_soft_cap_sink_srtq128n512t2048_kernel(
             last_values.tile([P, T], F32, name="v_pool1", align_bytes=64, offset=0),
         ]
         nc.sync.dma_start(v_pool[0][:], vT[0:P, :])
-        sink_col = sb.tile([P, 1], F32, name="sink_col")
-        nc.sync.dma_start(sink_col[:], sink[0])
-        nc.sync.dma_start(v_pool[1][:], vT[P : 2 * P, :])
 
         vs_g = sb.tile([P, N], F32, name="vs_g", align_bytes=64)
         nc.vector.tensor_copy(vs_g[:], vs_pool[:].indirect(offsets[:]))
@@ -84,14 +82,14 @@ def tile_attend_soft_cap_sink_srtq128n512t2048_kernel(
 
         list_cols = HALF // 16
         halves = [offsets[:, h * list_cols : (h + 1) * list_cols] for h in range(2)]
-        ks_window = [ks_pool[:].bitcast(U8)[:, o * T : (o + 1) * T] for o in range(PASSES)]
-        ks0 = sb.tile([P, N], U8, name="ks0", align_bytes=64)
-        ks1 = [
-            sb.tile([P, HALF], U8, name="ks1a", align_bytes=64),
-            key_words.tile([P, HALF], U8, name="ks1b", align_bytes=64, offset=0),
-        ]
-        nc.vector.tensor_copy(ks0[:], ks_window[0].indirect(offsets[:]))
-        nc.vector.tensor_copy(ks1[0][:], ks_window[1].indirect(halves[0]))
+        ks0 = sb.tile([P, N // 4], I32, name="ks0", align_bytes=64)
+        nc.vector.tensor_copy(ks0[:].bitcast(U8), ks_pool[:].bitcast(U8).indirect(offsets[:]))
+        for r in range(4):
+            nc.sync.dma_start(ks1[r:P:32, :], ks0[16 + r : P : 32, :])
+        ks = [ks0[:].bitcast(U8), ks1[:].bitcast(U8)]
+        sink_col = sb.tile([P, 1], F32, name="sink_col")
+        nc.sync.dma_start(sink_col[:], sink[0])
+        nc.sync.dma_start(v_pool[1][:], vT[P : 2 * P, :])
 
         neg_c = after_exp.tile([P, N + 1], F32, name="neg_c", align_bytes=64, offset=0)
 
@@ -103,26 +101,23 @@ def tile_attend_soft_cap_sink_srtq128n512t2048_kernel(
             nc.vector.tensor_copy(
                 k_pass[h][:].bitcast(U16), k_both[h][:].bitcast(U16).rearrange("p (j o) -> p o j", o=PASSES)
             )
-        nc.vector.tensor_copy(ks1[1][:], ks_window[1].indirect(halves[1]))
 
         groups = N // GROUP
         score = [ps.tile([P, GROUP], F32, name="score%d" % g, tag="bank%d" % g) for g in range(groups)]
         th = sb.tile([P, PACK, P], F32, name="th", align_bytes=64)
         per_half = HALF // GROUP
-        for h in range(2):
-            for o in range(PASSES):
-                for j in range(per_half):
-                    g = h * per_half + j
-                    key_scales = ks0[:, g * GROUP : (g + 1) * GROUP] if o == 0 else ks1[h][:, j * GROUP : (j + 1) * GROUP]
-                    nc.tensor.matmul_mx(
-                        score[g][:],
-                        lhsT=qw[:, o, :].bitcast(FP8X4),
-                        lhsT_scale=qs[:, o, :].bitcast(U8),
-                        rhs=k_pass[h][:, o, 2 * j * GROUP : 2 * (j + 1) * GROUP].bitcast(FP4X4),
-                        rhs_scale=key_scales,
-                        start=(o == 0),
-                        stop=(o == PASSES - 1),
-                    )
+        for o in range(PASSES):
+            for g in range(groups):
+                h, j = divmod(g, per_half)
+                nc.tensor.matmul_mx(
+                    score[g][:],
+                    lhsT=qw[:, o, :].bitcast(FP8X4),
+                    lhsT_scale=qs[:, o, :].bitcast(U8),
+                    rhs=k_pass[h][:, o, 2 * j * GROUP : 2 * (j + 1) * GROUP].bitcast(FP4X4),
+                    rhs_scale=ks[o][:, g * GROUP : (g + 1) * GROUP],
+                    start=(o == 0),
+                    stop=(o == PASSES - 1),
+                )
         for g in range(groups):
             p_range = slice(g * GROUP // PACK, (g + 1) * GROUP // PACK)
             nc.scalar.activation(
@@ -151,7 +146,7 @@ def tile_attend_soft_cap_sink_srtq128n512t2048_kernel(
                 prob[:, cols], neg_c[:, cols], ACT.Exp, bias=neg_m[:], scale=-1.0, accum_out=part_sum[h][:]
             )
 
-        v_t = [ps.tile([P, 2, P], F32, name="v_t0", tag="v_t0"), ps.tile([P, 2, P], F32, name="v_t1", tag="v_t0")]
+        v_t = [ps.tile([P, 2, P], F32, name="v_t0", tag="bank1"), ps.tile([P, 2, P], F32, name="v_t1", tag="bank1")]
         prob_t = ps.tile([P, PACK, P], F32, name="prob_t")
         for u in range(2):
             nc.tensor.transpose(v_t[0][:, u, :], v_g[0][:].bitcast(F32)[:, u : N // 2 : 2], ident[:])

@@ -26,6 +26,7 @@ HALF = N // 2
 GROUP = 128
 VS_ROW = P - 1
 K_FIRST = 512
+SPARE = 112
 
 
 def tile_attend_soft_cap_sink_srtq128n512t2048_kernel(
@@ -38,11 +39,14 @@ def tile_attend_soft_cap_sink_srtq128n512t2048_kernel(
         after_exp = ctx.enter_context(tc.tile_pool(name="after_exp", bufs=1))
         last_values = ctx.enter_context(tc.tile_pool(name="last_values", bufs=1))
 
+        k_pool = sb.tile([P, T], I32, name="k_pool", align_bytes=64)
+        k_rows = k_words[0].rearrange("g t b -> g (t b)").bitcast(I32)
+        nc.sync.dma_start(k_pool[:, 0:K_FIRST], k_rows[:, 0:K_FIRST])
         offsets = sb.tile([P, N // 16], U16, name="offsets")
         nc.sync.dma_start(offsets[:], offs)
 
         ks_pool = sb.tile([P, T // 4], I32, name="ks_pool", align_bytes=64)
-        nc.vector.memset(ks_pool[:], 0)
+        nc.vector.memset(ks_pool[0:SPARE, :], 0)
         qs = sb.tile([P, PASSES, NQ // 4], I32, name="qs", align_bytes=64)
         nc.vector.memset(qs[:], 0)
         vs_pool = sb.tile([P, T], F32, name="vs_pool", align_bytes=64)
@@ -53,39 +57,29 @@ def tile_attend_soft_cap_sink_srtq128n512t2048_kernel(
         nc.vector.memset(ident[:], 0.0)
         make_identity(nc, ident[:], nomemset=True)
 
-        nc.sync.dma_start(vs_pool[VS_ROW : VS_ROW + 1, :], vs[0:1, :])
-        k_pool = sb.tile([P, T], I32, name="k_pool", align_bytes=64)
-        k_rows = k_words[0].rearrange("g t b -> g (t b)").bitcast(I32)
-        nc.sync.dma_start(k_pool[:, 0:K_FIRST], k_rows[:, 0:K_FIRST])
-        ks_rows = k_scales.bitcast(I32).rearrange("o (Q r) t -> r Q o t", r=4)
+        ks_rows = k_scales.bitcast(I32)
+        nc.sync.dma_start(ks_pool[SPARE:P, :], ks_rows[1])
         for r in range(4):
-            nc.sync.dma_start(ks_pool[r:P:16, :], ks_rows[r])
+            nc.sync.dma_start(ks_pool[r:SPARE:32, :], ks_rows[0, r:16:4, :])
         nc.sync.dma_start(k_pool[:, K_FIRST:T], k_rows[:, K_FIRST:T])
+        nc.sync.dma_start(vs_pool[VS_ROW : VS_ROW + 1, :], vs[0:1, :])
+        v_pool = [
+            sb.tile([P, T], F32, name="v_pool0", align_bytes=64),
+            last_values.tile([P, T], F32, name="v_pool1", align_bytes=64, offset=0),
+        ]
         qw = sb.tile([P, PASSES, NQ], I32, name="qw", align_bytes=64)
         nc.sync.dma_start(qw[:], q_words[0].rearrange("o g q r -> g o (q r)").bitcast(I32))
         qs_rows = q_scales[0].bitcast(I32).rearrange("o (Q r) q -> r Q o q", r=4)
         for r in range(4):
             nc.sync.dma_start(qs[r:P:32, :, :], qs_rows[r])
-        v_pool = [
-            sb.tile([P, T], F32, name="v_pool0", align_bytes=64),
-            last_values.tile([P, T], F32, name="v_pool1", align_bytes=64, offset=0),
-        ]
         nc.sync.dma_start(v_pool[0][:], vT[0:P, :])
-
-        vs_g = sb.tile([P, N], F32, name="vs_g", align_bytes=64)
-        nc.vector.tensor_copy(vs_g[:], vs_pool[:].indirect(offsets[:]))
-        vs_t = ps.tile([P, PACK, P], F32, name="vs_t")
-        for t in range(PACK):
-            nc.tensor.transpose(vs_t[:, t, :], vs_g[:, t:N:PACK], ident[:])
-        vs_col = sb.tile([P, PACK], F32, name="vs_col", align_bytes=64)
-        nc.scalar.copy(vs_col[:], vs_t[:, :, VS_ROW])
 
         list_cols = HALF // 16
         halves = [offsets[:, h * list_cols : (h + 1) * list_cols] for h in range(2)]
         ks0 = sb.tile([P, N // 4], I32, name="ks0", align_bytes=64)
         nc.vector.tensor_copy(ks0[:].bitcast(U8), ks_pool[:].bitcast(U8).indirect(offsets[:]))
         for r in range(4):
-            nc.sync.dma_start(ks1[r:P:32, :], ks0[16 + r : P : 32, :])
+            nc.sync.dma_start(ks1[r:P:32, :], ks0[SPARE + r : P : 4, :])
         ks = [ks0[:].bitcast(U8), ks1[:].bitcast(U8)]
         sink_col = sb.tile([P, 1], F32, name="sink_col")
         nc.sync.dma_start(sink_col[:], sink[0])
@@ -101,6 +95,9 @@ def tile_attend_soft_cap_sink_srtq128n512t2048_kernel(
             nc.vector.tensor_copy(
                 k_pass[h][:].bitcast(U16), k_both[h][:].bitcast(U16).rearrange("p (j o) -> p o j", o=PASSES)
             )
+
+        vs_g = sb.tile([P, N], F32, name="vs_g", tag="k_both0", align_bytes=64)
+        nc.vector.tensor_copy(vs_g[:], vs_pool[:].indirect(offsets[:]))
 
         groups = N // GROUP
         score = [ps.tile([P, GROUP], F32, name="score%d" % g, tag="bank%d" % g) for g in range(groups)]
@@ -146,6 +143,11 @@ def tile_attend_soft_cap_sink_srtq128n512t2048_kernel(
                 prob[:, cols], neg_c[:, cols], ACT.Exp, bias=neg_m[:], scale=-1.0, accum_out=part_sum[h][:]
             )
 
+        vs_t = ps.tile([P, PACK, P], F32, name="vs_t", tag="bank0")
+        for t in range(PACK):
+            nc.tensor.transpose(vs_t[:, t, :], vs_g[:, t:N:PACK], ident[:])
+        vs_col = after_exp.tile([P, PACK], F32, name="vs_col", align_bytes=64, offset=1088)
+        nc.scalar.copy(vs_col[:], vs_t[:, :, VS_ROW])
         v_t = [ps.tile([P, 2, P], F32, name="v_t0", tag="bank1"), ps.tile([P, 2, P], F32, name="v_t1", tag="bank1")]
         prob_t = ps.tile([P, PACK, P], F32, name="prob_t")
         for u in range(2):

@@ -25,8 +25,14 @@ PASSES = D // (P * PACK)
 HALF = N // 2
 GROUP = 128
 VS_ROW = P - 1
-K_FIRST = 512
 SPARE = 112
+V_SHARE = 352
+
+
+def clear_in_odd_runs(nc, words):
+    cut = words.shape[1] // 2 - 1
+    nc.vector.memset(words[:, 0:cut], 0)
+    nc.vector.memset(words[:, cut:], 0)
 
 
 def tile_attend_soft_cap_sink_srtq128n512t2048_kernel(
@@ -37,57 +43,53 @@ def tile_attend_soft_cap_sink_srtq128n512t2048_kernel(
         sb = ctx.enter_context(tc.tile_pool(name="sb", bufs=1))
         ps = ctx.enter_context(tc.psum_pool(name="ps", bufs=1))
         after_exp = ctx.enter_context(tc.tile_pool(name="after_exp", bufs=1))
-        last_values = ctx.enter_context(tc.tile_pool(name="last_values", bufs=1))
+        after_max = ctx.enter_context(tc.tile_pool(name="after_max", bufs=1))
 
-        k_pool = sb.tile([P, T], I32, name="k_pool", align_bytes=64)
-        k_rows = k_words[0].rearrange("g t b -> g (t b)").bitcast(I32)
-        nc.sync.dma_start(k_pool[:, 0:K_FIRST], k_rows[:, 0:K_FIRST])
+        ks_pool = sb.tile([P, PASSES * T // 4], I32, name="ks_pool", align_bytes=64)
+        nc.sync.dma_start(
+            ks_pool[SPARE:P, :].rearrange("f (o t) -> f o t", o=PASSES), k_scales.bitcast(I32).rearrange("o f t -> f o t")
+        )
         offsets = sb.tile([P, N // 16], U16, name="offsets")
         nc.sync.dma_start(offsets[:], offs)
-
-        ks_pool = sb.tile([P, T // 4], I32, name="ks_pool", align_bytes=64)
-        nc.vector.memset(ks_pool[0:SPARE, :], 0)
-        qs = sb.tile([P, PASSES, NQ // 4], I32, name="qs", align_bytes=64)
-        nc.vector.memset(qs[:], 0)
-        vs_pool = sb.tile([P, T], F32, name="vs_pool", align_bytes=64)
-        nc.vector.memset(vs_pool[0:VS_ROW, :], 0.0)
-        ks1 = sb.tile([P, N // 4], I32, name="ks1", align_bytes=64)
-        nc.vector.memset(ks1[:], 0)
-        ident = sb.tile([P, P], F32, name="ident", align_bytes=64)
-        nc.vector.memset(ident[:], 0.0)
-        make_identity(nc, ident[:], nomemset=True)
-
-        ks_rows = k_scales.bitcast(I32)
-        nc.sync.dma_start(ks_pool[SPARE:P, :], ks_rows[1])
-        for r in range(4):
-            nc.sync.dma_start(ks_pool[r:SPARE:32, :], ks_rows[0, r:16:4, :])
-        nc.sync.dma_start(k_pool[:, K_FIRST:T], k_rows[:, K_FIRST:T])
-        nc.sync.dma_start(vs_pool[VS_ROW : VS_ROW + 1, :], vs[0:1, :])
-        v_pool = [
-            sb.tile([P, T], F32, name="v_pool0", align_bytes=64),
-            last_values.tile([P, T], F32, name="v_pool1", align_bytes=64, offset=0),
-        ]
+        sink_col = sb.tile([P, 1], F32, name="sink_col")
+        nc.sync.dma_start(sink_col[:], sink[0])
+        k_pool = sb.tile([P, T], I32, name="k_pool", align_bytes=64)
+        nc.sync.dma_start(k_pool[:], k_words[0].rearrange("g t b -> g (t b)").bitcast(I32))
         qw = sb.tile([P, PASSES, NQ], I32, name="qw", align_bytes=64)
         nc.sync.dma_start(qw[:], q_words[0].rearrange("o g q r -> g o (q r)").bitcast(I32))
+        vs_pool = sb.tile([P, T], F32, name="vs_pool", align_bytes=64)
+        nc.sync.dma_start(vs_pool[VS_ROW : VS_ROW + 1, :], vs[0:1, :])
+
+        qs = sb.tile([P, PASSES, NQ // 4], I32, name="qs", align_bytes=64)
+        clear_in_odd_runs(nc, qs[:].rearrange("p o q -> p (o q)"))
+        clear_in_odd_runs(nc, ks_pool[0:SPARE, :])
+        ident = sb.tile([P, P], F32, name="ident", align_bytes=64)
+        make_identity(nc, ident[:])
+        ks = sb.tile([P, PASSES * N // 4], I32, name="ks", align_bytes=64)
+        clear_in_odd_runs(nc, ks[:])
+        nc.gpsimd.memset(vs_pool[0:VS_ROW, :], 0.0)
+
         qs_rows = q_scales[0].bitcast(I32).rearrange("o (Q r) q -> r Q o q", r=4)
         for r in range(4):
             nc.sync.dma_start(qs[r:P:32, :, :], qs_rows[r])
+        vs_g = sb.tile([P, N], F32, name="vs_g", align_bytes=64)
+        nc.scalar.activation(vs_g[:], vs_pool[:].indirect(offsets[:]), ACT.Copy)
+        v_pool = [sb.tile([P, T], F32, name="v_pool%d" % h, align_bytes=64) for h in range(2)]
         nc.sync.dma_start(v_pool[0][:], vT[0:P, :])
+
+        ks_g = sb.tile([P, PASSES * N // 4], I32, name="ks_g", align_bytes=64)
+        for o in range(PASSES):
+            nc.vector.tensor_copy(
+                ks_g[:].bitcast(U8)[:, o * N : (o + 1) * N],
+                ks_pool[:].bitcast(U8)[:, o * T : (o + 1) * T].indirect(offsets[:]),
+            )
+        for r in range(4):
+            nc.sync.dma_start(ks[r:P:32, :], ks_g[SPARE + r : P : 4, :])
+        nc.sync.dma_start(v_pool[1][:], vT[P : 2 * P, :])
 
         list_cols = HALF // 16
         halves = [offsets[:, h * list_cols : (h + 1) * list_cols] for h in range(2)]
-        ks0 = sb.tile([P, N // 4], I32, name="ks0", align_bytes=64)
-        nc.vector.tensor_copy(ks0[:].bitcast(U8), ks_pool[:].bitcast(U8).indirect(offsets[:]))
-        for r in range(4):
-            nc.sync.dma_start(ks1[r:P:32, :], ks0[SPARE + r : P : 4, :])
-        ks = [ks0[:].bitcast(U8), ks1[:].bitcast(U8)]
-        sink_col = sb.tile([P, 1], F32, name="sink_col")
-        nc.sync.dma_start(sink_col[:], sink[0])
-        nc.sync.dma_start(v_pool[1][:], vT[P : 2 * P, :])
-
-        neg_c = after_exp.tile([P, N + 1], F32, name="neg_c", align_bytes=64, offset=0)
-
-        k_both = [sb.tile([P, HALF], I32, name="k_both%d" % h, tag="k_both%d" % h, align_bytes=64) for h in range(2)]
+        k_both = [sb.tile([P, HALF], I32, name="k_both%d" % h, align_bytes=64) for h in range(2)]
         k_pass = [sb.tile([P, PASSES, 2 * HALF], U8, name="k_pass%d" % h, align_bytes=64) for h in range(2)]
         for h in range(2):
             nc.vector.tensor_copy(k_both[h][:].bitcast(U32), k_pool[:].bitcast(U32).indirect(halves[h]))
@@ -96,45 +98,58 @@ def tile_attend_soft_cap_sink_srtq128n512t2048_kernel(
                 k_pass[h][:].bitcast(U16), k_both[h][:].bitcast(U16).rearrange("p (j o) -> p o j", o=PASSES)
             )
 
-        vs_g = sb.tile([P, N], F32, name="vs_g", tag="k_both0", align_bytes=64)
-        nc.vector.tensor_copy(vs_g[:], vs_pool[:].indirect(offsets[:]))
+        neg_c = after_exp.tile([P, N + 1], F32, name="neg_c", align_bytes=64, offset=0)
+        nc.scalar.activation(neg_c[:, N : N + 1], sink_col[:], ACT.Copy, scale=-1.0)
+
+
+        vs_t = ps.tile([P, PACK, P], F32, name="vs_t")
+        for t in range(PACK):
+            nc.tensor.transpose(vs_t[:, t, :], vs_g[:, t:N:PACK], ident[:])
+        vs_col = sb.tile([P, PACK], F32, name="vs_col", align_bytes=64)
+        nc.scalar.copy(vs_col[:], vs_t[:, :, VS_ROW])
 
         groups = N // GROUP
         score = [ps.tile([P, GROUP], F32, name="score%d" % g, tag="bank%d" % g) for g in range(groups)]
         th = sb.tile([P, PACK, P], F32, name="th", align_bytes=64)
         per_half = HALF // GROUP
-        for o in range(PASSES):
-            for g in range(groups):
-                h, j = divmod(g, per_half)
-                nc.tensor.matmul_mx(
-                    score[g][:],
-                    lhsT=qw[:, o, :].bitcast(FP8X4),
-                    lhsT_scale=qs[:, o, :].bitcast(U8),
-                    rhs=k_pass[h][:, o, 2 * j * GROUP : 2 * (j + 1) * GROUP].bitcast(FP4X4),
-                    rhs_scale=ks[o][:, g * GROUP : (g + 1) * GROUP],
-                    start=(o == 0),
-                    stop=(o == PASSES - 1),
-                )
+        for h in range(2):
+            for o in range(PASSES):
+                for j in range(per_half):
+                    g = h * per_half + j
+                    nc.tensor.matmul_mx(
+                        score[g][:],
+                        lhsT=qw[:, o, :].bitcast(FP8X4),
+                        lhsT_scale=qs[:, o, :].bitcast(U8),
+                        rhs=k_pass[h][:, o, 2 * j * GROUP : 2 * (j + 1) * GROUP].bitcast(FP4X4),
+                        rhs_scale=ks[:].bitcast(U8)[:, o * N + g * GROUP : o * N + (g + 1) * GROUP],
+                        start=(o == 0),
+                        stop=(o == PASSES - 1),
+                    )
+        group_rows = GROUP // PACK
         for g in range(groups):
-            p_range = slice(g * GROUP // PACK, (g + 1) * GROUP // PACK)
             nc.scalar.activation(
-                th[:, :, p_range], score[g][:].rearrange("q (p t) -> q t p", t=PACK), ACT.Tanh, scale=1.0 / CAP
+                th[:, :, g * group_rows : (g + 1) * group_rows],
+                score[g][:].rearrange("q (p t) -> q t p", t=PACK),
+                ACT.Tanh,
+                scale=1.0 / CAP,
             )
 
-        nc.scalar.activation(neg_c[:, N : N + 1], sink_col[:], ACT.Copy, scale=-1.0)
-        v_g = [sb.tile([P, N], BF16, name="v_g%d" % h, align_bytes=64) for h in range(2)]
+        v_g = [
+            sb.tile([P, N], BF16, name="v_g0", align_bytes=64),
+            after_max.tile([P, N], BF16, name="v_g1", align_bytes=64, offset=0),
+        ]
         nc.vector.tensor_copy(v_g[0][:], v_pool[0][:].indirect(offsets[:]))
+        neg_c_slots = neg_c[:, 0:N].rearrange("q (t p) -> q t p", t=PACK)
+        early_rows = P // 2
+        neg_m_early = after_max.tile([P, 1], F32, name="neg_m_early", align_bytes=64, offset=0)
         neg_m = sb.tile([P, 1], F32, name="neg_m")
-        nc.vector.tensor_scalar(
-            neg_c[:, 0:N],
-            th[:].rearrange("q t p -> q (t p)"),
-            -CAP,
-            neg_c[:, N : N + 1],
-            ALU.mult,
-            ALU.min,
-            accum_out=neg_m[:],
-        )
-        nc.vector.tensor_copy(v_g[1][:], v_pool[1][:].indirect(offsets[:]))
+        for rows, start, result in (
+            (slice(0, early_rows), neg_c[:, N : N + 1], neg_m_early),
+            (slice(early_rows, P), neg_m_early[:], neg_m),
+        ):
+            nc.vector.tensor_scalar(
+                neg_c_slots[:, :, rows], th[:, :, rows], -CAP, start, ALU.mult, ALU.min, accum_out=result[:]
+            )
 
         prob = sb.tile([P, N + 1], F32, name="prob", align_bytes=64)
         part_sum = [sb.tile([P, 1], F32, name="part_sum%d" % h) for h in range(2)]
@@ -143,52 +158,50 @@ def tile_attend_soft_cap_sink_srtq128n512t2048_kernel(
                 prob[:, cols], neg_c[:, cols], ACT.Exp, bias=neg_m[:], scale=-1.0, accum_out=part_sum[h][:]
             )
 
-        vs_t = ps.tile([P, PACK, P], F32, name="vs_t", tag="bank0")
-        for t in range(PACK):
-            nc.tensor.transpose(vs_t[:, t, :], vs_g[:, t:N:PACK], ident[:])
-        vs_col = after_exp.tile([P, PACK], F32, name="vs_col", align_bytes=64, offset=1088)
-        nc.scalar.copy(vs_col[:], vs_t[:, :, VS_ROW])
-        v_t = [ps.tile([P, 2, P], F32, name="v_t0", tag="bank1"), ps.tile([P, 2, P], F32, name="v_t1", tag="bank1")]
+        nc.vector.tensor_copy(v_g[1][:, 0:V_SHARE], v_pool[1][:].indirect(offsets[:, 0 : V_SHARE // 16]))
+        nc.scalar.activation(v_g[1][:, V_SHARE:N], v_pool[1][:].indirect(offsets[:, V_SHARE // 16 : N // 16]), ACT.Copy)
+
+        v_t = [ps.tile([P, 2, P], F32, name="v_t0", tag="bank3"), ps.tile([P, 2, P], F32, name="v_t1", tag="bank2")]
         prob_t = ps.tile([P, PACK, P], F32, name="prob_t")
         for u in range(2):
             nc.tensor.transpose(v_t[0][:, u, :], v_g[0][:].bitcast(F32)[:, u : N // 2 : 2], ident[:])
         for t in range(PACK):
             nc.tensor.transpose(prob_t[:, t, :], prob[:, t * P : (t + 1) * P], ident[:])
-        for u in range(2):
-            nc.tensor.transpose(v_t[1][:, u, :], v_g[1][:].bitcast(F32)[:, u : N // 2 : 2], ident[:])
         v_b = [
             after_exp.tile([P, P * PACK], BF16, name="v_b0", align_bytes=64, offset=64),
             sb.tile([P, P * PACK], BF16, name="v_b1", align_bytes=64),
         ]
-        for h in range(2):
-            nc.scalar.copy(
-                v_b[h][:].bitcast(F32).rearrange("p (e u) -> p e u", u=2), v_t[h][:].rearrange("p u e -> p e u")
-            )
-
+        nc.scalar.copy(
+            v_b[0][:].bitcast(F32).rearrange("p (e u) -> p e u", u=2), v_t[0][:].rearrange("p u e -> p e u")
+        )
         total = sb.tile([P, 1], F32, name="total")
         nc.scalar.activation(total[:], part_sum[0][:], ACT.Identity, bias=part_sum[1][:])
-        w = last_values.tile([P, NQ, PACK], BF16, name="w", align_bytes=64, offset=0)
+        w = sb.tile([P, NQ, PACK], BF16, name="w", align_bytes=64)
         nc.vector.tensor_tensor(
             w[:],
             prob_t[:].rearrange("p t q -> p q t"),
             vs_col[:].unsqueeze(1).broadcast_to([P, NQ, PACK]),
             ALU.mult,
         )
+
+        for u in range(2):
+            nc.tensor.transpose(v_t[1][:, u, :], v_g[1][:].bitcast(F32)[:, u : N // 2 : 2], ident[:])
+        nc.scalar.copy(
+            v_b[1][:].bitcast(F32).rearrange("p (e u) -> p e u", u=2), v_t[1][:].rearrange("p u e -> p e u")
+        )
+
         v_codes = [sb.tile([P, P], U32, name="v_codes%d" % h, align_bytes=64) for h in range(2)]
-        v_scales = [
-            last_values.tile([P, P], U8, name="v_scales0", align_bytes=64, offset=1024),
-            sb.tile([P, P], U8, name="v_scales1", align_bytes=64),
-        ]
+        v_scales = [sb.tile([P, P], U8, name="v_scales%d" % h, align_bytes=64) for h in range(2)]
         w_codes = sb.tile([P, NQ], U32, name="w_codes", align_bytes=64)
         w_scales = sb.tile([P, NQ], U8, name="w_scales", align_bytes=64)
-        inv_total = last_values.tile([P, 1], F32, name="inv_total", align_bytes=64, offset=2048)
+        inv_total = sb.tile([P, 1], F32, name="inv_total", align_bytes=64)
         nc.vector.quantize_mx(v_codes[0][:].bitcast(FP8X4), v_scales[0][:], v_b[0][:])
         nc.vector.quantize_mx(w_codes[:].bitcast(FP8X4), w_scales[:], w[:].rearrange("p q t -> p (q t)"))
-        nc.vector.quantize_mx(v_codes[1][:].bitcast(FP8X4), v_scales[1][:], v_b[1][:])
         nc.vector.reciprocal(inv_total[:], total[:])
+        nc.vector.quantize_mx(v_codes[1][:].bitcast(FP8X4), v_scales[1][:], v_b[1][:])
 
         for h in range(2):
-            y = ps.tile([P, P], F32, name="y%d" % h, tag="bank%d" % (h + 2))
+            y = ps.tile([P, P], F32, name="y%d" % h, tag="bank%d" % h)
             nc.tensor.matmul_mx(
                 y[:],
                 lhsT=w_codes[:].bitcast(FP8X4),

@@ -27,6 +27,7 @@ GROUP = 128
 VS_ROW = P - 1
 SPARE = 112
 V_SHARE = 352
+V_FIRST = 1280
 
 
 def clear_in_odd_runs(nc, words):
@@ -43,22 +44,19 @@ def tile_attend_soft_cap_sink_srtq128n512t2048_kernel(
         sb = ctx.enter_context(tc.tile_pool(name="sb", bufs=1))
         ps = ctx.enter_context(tc.psum_pool(name="ps", bufs=1))
         after_exp = ctx.enter_context(tc.tile_pool(name="after_exp", bufs=1))
+        last_values = ctx.enter_context(tc.tile_pool(name="last_values", bufs=1))
         after_max = ctx.enter_context(tc.tile_pool(name="after_max", bufs=1))
 
         ks_pool = sb.tile([P, PASSES * T // 4], I32, name="ks_pool", align_bytes=64)
-        nc.sync.dma_start(
-            ks_pool[SPARE:P, :].rearrange("f (o t) -> f o t", o=PASSES), k_scales.bitcast(I32).rearrange("o f t -> f o t")
-        )
+        ks_rows = k_scales.bitcast(I32)
+        nc.sync.dma_start(ks_pool[SPARE:P, 0 : T // 4], ks_rows[0])
         offsets = sb.tile([P, N // 16], U16, name="offsets")
         nc.sync.dma_start(offsets[:], offs)
         sink_col = sb.tile([P, 1], F32, name="sink_col")
         nc.sync.dma_start(sink_col[:], sink[0])
+        nc.sync.dma_start(ks_pool[SPARE:P, T // 4 : T // 2], ks_rows[1])
         k_pool = sb.tile([P, T], I32, name="k_pool", align_bytes=64)
         nc.sync.dma_start(k_pool[:], k_words[0].rearrange("g t b -> g (t b)").bitcast(I32))
-        qw = sb.tile([P, PASSES, NQ], I32, name="qw", align_bytes=64)
-        nc.sync.dma_start(qw[:], q_words[0].rearrange("o g q r -> g o (q r)").bitcast(I32))
-        vs_pool = sb.tile([P, T], F32, name="vs_pool", align_bytes=64)
-        nc.sync.dma_start(vs_pool[VS_ROW : VS_ROW + 1, :], vs[0:1, :])
 
         qs = sb.tile([P, PASSES, NQ // 4], I32, name="qs", align_bytes=64)
         clear_in_odd_runs(nc, qs[:].rearrange("p o q -> p (o q)"))
@@ -67,15 +65,20 @@ def tile_attend_soft_cap_sink_srtq128n512t2048_kernel(
         make_identity(nc, ident[:])
         ks = sb.tile([P, PASSES * N // 4], I32, name="ks", align_bytes=64)
         clear_in_odd_runs(nc, ks[:])
+        vs_pool = sb.tile([P, T], F32, name="vs_pool", align_bytes=64)
         nc.gpsimd.memset(vs_pool[0:VS_ROW, :], 0.0)
 
         qs_rows = q_scales[0].bitcast(I32).rearrange("o (Q r) q -> r Q o q", r=4)
         for r in range(4):
             nc.sync.dma_start(qs[r:P:32, :, :], qs_rows[r])
-        vs_g = sb.tile([P, N], F32, name="vs_g", align_bytes=64)
-        nc.scalar.activation(vs_g[:], vs_pool[:].indirect(offsets[:]), ACT.Copy)
-        v_pool = [sb.tile([P, T], F32, name="v_pool%d" % h, align_bytes=64) for h in range(2)]
-        nc.sync.dma_start(v_pool[0][:], vT[0:P, :])
+        qw = sb.tile([P, PASSES, NQ], I32, name="qw", align_bytes=64)
+        nc.sync.dma_start(qw[:], q_words[0].rearrange("o g q r -> g o (q r)").bitcast(I32))
+        nc.sync.dma_start(vs_pool[VS_ROW : VS_ROW + 1, :], vs[0:1, :])
+        v_pool = [
+            after_max.tile([P, T], F32, name="v_pool0", align_bytes=64, offset=0),
+            last_values.tile([P, T], F32, name="v_pool1", align_bytes=64, offset=0),
+        ]
+        nc.sync.dma_start(v_pool[0][:, 0:V_FIRST], vT[0:P, 0:V_FIRST])
 
         ks_g = sb.tile([P, PASSES * N // 4], I32, name="ks_g", align_bytes=64)
         for o in range(PASSES):
@@ -85,6 +88,7 @@ def tile_attend_soft_cap_sink_srtq128n512t2048_kernel(
             )
         for r in range(4):
             nc.sync.dma_start(ks[r:P:32, :], ks_g[SPARE + r : P : 4, :])
+        nc.sync.dma_start(v_pool[0][:, V_FIRST:T], vT[0:P, V_FIRST:T])
         nc.sync.dma_start(v_pool[1][:], vT[P : 2 * P, :])
 
         list_cols = HALF // 16
@@ -100,7 +104,8 @@ def tile_attend_soft_cap_sink_srtq128n512t2048_kernel(
 
         neg_c = after_exp.tile([P, N + 1], F32, name="neg_c", align_bytes=64, offset=0)
         nc.scalar.activation(neg_c[:, N : N + 1], sink_col[:], ACT.Copy, scale=-1.0)
-
+        vs_g = sb.tile([P, N], F32, name="vs_g", align_bytes=64)
+        nc.scalar.activation(vs_g[:], vs_pool[:].indirect(offsets[:]), ACT.Copy)
 
         vs_t = ps.tile([P, PACK, P], F32, name="vs_t")
         for t in range(PACK):
@@ -161,22 +166,22 @@ def tile_attend_soft_cap_sink_srtq128n512t2048_kernel(
         nc.vector.tensor_copy(v_g[1][:, 0:V_SHARE], v_pool[1][:].indirect(offsets[:, 0 : V_SHARE // 16]))
         nc.scalar.activation(v_g[1][:, V_SHARE:N], v_pool[1][:].indirect(offsets[:, V_SHARE // 16 : N // 16]), ACT.Copy)
 
-        v_t = [ps.tile([P, 2, P], F32, name="v_t0", tag="bank3"), ps.tile([P, 2, P], F32, name="v_t1", tag="bank2")]
+        v_t = [ps.tile([P, 2, P], F32, name="v_t0"), ps.tile([P, 2, P], F32, name="v_t1", tag="bank2")]
         prob_t = ps.tile([P, PACK, P], F32, name="prob_t")
         for u in range(2):
             nc.tensor.transpose(v_t[0][:, u, :], v_g[0][:].bitcast(F32)[:, u : N // 2 : 2], ident[:])
         for t in range(PACK):
             nc.tensor.transpose(prob_t[:, t, :], prob[:, t * P : (t + 1) * P], ident[:])
         v_b = [
-            after_exp.tile([P, P * PACK], BF16, name="v_b0", align_bytes=64, offset=64),
+            sb.tile([P, P * PACK], BF16, name="v_b0", align_bytes=64),
             sb.tile([P, P * PACK], BF16, name="v_b1", align_bytes=64),
         ]
         nc.scalar.copy(
             v_b[0][:].bitcast(F32).rearrange("p (e u) -> p e u", u=2), v_t[0][:].rearrange("p u e -> p e u")
         )
         total = sb.tile([P, 1], F32, name="total")
-        nc.scalar.activation(total[:], part_sum[0][:], ACT.Identity, bias=part_sum[1][:])
-        w = sb.tile([P, NQ, PACK], BF16, name="w", align_bytes=64)
+        nc.gpsimd.tensor_tensor(total[:], part_sum[0][:], part_sum[1][:], ALU.add)
+        w = last_values.tile([P, NQ, PACK], BF16, name="w", align_bytes=64, offset=0)
         nc.vector.tensor_tensor(
             w[:],
             prob_t[:].rearrange("p t q -> p q t"),
@@ -194,7 +199,7 @@ def tile_attend_soft_cap_sink_srtq128n512t2048_kernel(
         v_scales = [sb.tile([P, P], U8, name="v_scales%d" % h, align_bytes=64) for h in range(2)]
         w_codes = sb.tile([P, NQ], U32, name="w_codes", align_bytes=64)
         w_scales = sb.tile([P, NQ], U8, name="w_scales", align_bytes=64)
-        inv_total = sb.tile([P, 1], F32, name="inv_total", align_bytes=64)
+        inv_total = last_values.tile([P, 1], F32, name="inv_total", align_bytes=64, offset=1024)
         nc.vector.quantize_mx(v_codes[0][:].bitcast(FP8X4), v_scales[0][:], v_b[0][:])
         nc.vector.quantize_mx(w_codes[:].bitcast(FP8X4), w_scales[:], w[:].rearrange("p q t -> p (q t)"))
         nc.vector.reciprocal(inv_total[:], total[:])

@@ -26,8 +26,8 @@ HALF = N // 2
 GROUP = 128
 VS_ROW = P - 1
 SPARE = 112
-V_SHARE = 352
-V_FIRST = 1280
+V_SHARE = 416
+V_FIRST = 1408
 
 
 def clear_in_odd_runs(nc, words):
@@ -43,20 +43,16 @@ def tile_attend_soft_cap_sink_srtq128n512t2048_kernel(
     with ExitStack() as ctx:
         sb = ctx.enter_context(tc.tile_pool(name="sb", bufs=1))
         ps = ctx.enter_context(tc.psum_pool(name="ps", bufs=1))
-        after_exp = ctx.enter_context(tc.tile_pool(name="after_exp", bufs=1))
         last_values = ctx.enter_context(tc.tile_pool(name="last_values", bufs=1))
-        after_max = ctx.enter_context(tc.tile_pool(name="after_max", bufs=1))
 
         ks_pool = sb.tile([P, PASSES * T // 4], I32, name="ks_pool", align_bytes=64)
         ks_rows = k_scales.bitcast(I32)
         nc.sync.dma_start(ks_pool[SPARE:P, 0 : T // 4], ks_rows[0])
         offsets = sb.tile([P, N // 16], U16, name="offsets")
         nc.sync.dma_start(offsets[:], offs)
-        sink_col = sb.tile([P, 1], F32, name="sink_col")
-        nc.sync.dma_start(sink_col[:], sink[0])
         nc.sync.dma_start(ks_pool[SPARE:P, T // 4 : T // 2], ks_rows[1])
-        k_pool = sb.tile([P, T], I32, name="k_pool", align_bytes=64)
-        nc.sync.dma_start(k_pool[:], k_words[0].rearrange("g t b -> g (t b)").bitcast(I32))
+        vs_pool = sb.tile([P, T], F32, name="vs_pool", align_bytes=64)
+        nc.sync.dma_start(vs_pool[VS_ROW : VS_ROW + 1, :], vs[0:1, :])
 
         qs = sb.tile([P, PASSES, NQ // 4], I32, name="qs", align_bytes=64)
         clear_in_odd_runs(nc, qs[:].rearrange("p o q -> p (o q)"))
@@ -65,17 +61,18 @@ def tile_attend_soft_cap_sink_srtq128n512t2048_kernel(
         make_identity(nc, ident[:])
         ks = sb.tile([P, PASSES * N // 4], I32, name="ks", align_bytes=64)
         clear_in_odd_runs(nc, ks[:])
-        vs_pool = sb.tile([P, T], F32, name="vs_pool", align_bytes=64)
         nc.gpsimd.memset(vs_pool[0:VS_ROW, :], 0.0)
 
         qs_rows = q_scales[0].bitcast(I32).rearrange("o (Q r) q -> r Q o q", r=4)
-        for r in range(4):
+        for r in range(3):
             nc.sync.dma_start(qs[r:P:32, :, :], qs_rows[r])
+        k_pool = sb.tile([P, T], I32, name="k_pool", align_bytes=64)
+        nc.sync.dma_start(k_pool[:], k_words[0].rearrange("g t b -> g (t b)").bitcast(I32))
+        nc.sync.dma_start(qs[3:P:32, :, :], qs_rows[3])
         qw = sb.tile([P, PASSES, NQ], I32, name="qw", align_bytes=64)
         nc.sync.dma_start(qw[:], q_words[0].rearrange("o g q r -> g o (q r)").bitcast(I32))
-        nc.sync.dma_start(vs_pool[VS_ROW : VS_ROW + 1, :], vs[0:1, :])
         v_pool = [
-            after_max.tile([P, T], F32, name="v_pool0", align_bytes=64, offset=0),
+            sb.tile([P, T], F32, name="v_pool0", align_bytes=64),
             last_values.tile([P, T], F32, name="v_pool1", align_bytes=64, offset=0),
         ]
         nc.sync.dma_start(v_pool[0][:, 0:V_FIRST], vT[0:P, 0:V_FIRST])
@@ -89,6 +86,8 @@ def tile_attend_soft_cap_sink_srtq128n512t2048_kernel(
         for r in range(4):
             nc.sync.dma_start(ks[r:P:32, :], ks_g[SPARE + r : P : 4, :])
         nc.sync.dma_start(v_pool[0][:, V_FIRST:T], vT[0:P, V_FIRST:T])
+        sink_col = sb.tile([P, 1], F32, name="sink_col")
+        nc.sync.dma_start(sink_col[:], sink[0])
         nc.sync.dma_start(v_pool[1][:], vT[P : 2 * P, :])
 
         list_cols = HALF // 16
@@ -102,8 +101,6 @@ def tile_attend_soft_cap_sink_srtq128n512t2048_kernel(
                 k_pass[h][:].bitcast(U16), k_both[h][:].bitcast(U16).rearrange("p (j o) -> p o j", o=PASSES)
             )
 
-        neg_c = after_exp.tile([P, N + 1], F32, name="neg_c", align_bytes=64, offset=0)
-        nc.scalar.activation(neg_c[:, N : N + 1], sink_col[:], ACT.Copy, scale=-1.0)
         vs_g = sb.tile([P, N], F32, name="vs_g", align_bytes=64)
         nc.scalar.activation(vs_g[:], vs_pool[:].indirect(offsets[:]), ACT.Copy)
 
@@ -139,22 +136,20 @@ def tile_attend_soft_cap_sink_srtq128n512t2048_kernel(
                 scale=1.0 / CAP,
             )
 
-        v_g = [
-            sb.tile([P, N], BF16, name="v_g0", align_bytes=64),
-            after_max.tile([P, N], BF16, name="v_g1", align_bytes=64, offset=0),
-        ]
+        neg_c = sb.tile([P, N + 1], F32, name="neg_c", align_bytes=64)
+        nc.scalar.activation(neg_c[:, N : N + 1], sink_col[:], ACT.Copy, scale=-1.0)
+        v_g = [sb.tile([P, N], BF16, name="v_g%d" % h, align_bytes=64) for h in range(2)]
         nc.vector.tensor_copy(v_g[0][:], v_pool[0][:].indirect(offsets[:]))
-        neg_c_slots = neg_c[:, 0:N].rearrange("q (t p) -> q t p", t=PACK)
-        early_rows = P // 2
-        neg_m_early = after_max.tile([P, 1], F32, name="neg_m_early", align_bytes=64, offset=0)
         neg_m = sb.tile([P, 1], F32, name="neg_m")
-        for rows, start, result in (
-            (slice(0, early_rows), neg_c[:, N : N + 1], neg_m_early),
-            (slice(early_rows, P), neg_m_early[:], neg_m),
-        ):
-            nc.vector.tensor_scalar(
-                neg_c_slots[:, :, rows], th[:, :, rows], -CAP, start, ALU.mult, ALU.min, accum_out=result[:]
-            )
+        nc.vector.tensor_scalar(
+            neg_c[:, 0:N],
+            th[:].rearrange("q t p -> q (t p)"),
+            -CAP,
+            neg_c[:, N : N + 1],
+            ALU.mult,
+            ALU.min,
+            accum_out=neg_m[:],
+        )
 
         prob = sb.tile([P, N + 1], F32, name="prob", align_bytes=64)
         part_sum = [sb.tile([P, 1], F32, name="part_sum%d" % h) for h in range(2)]
@@ -173,7 +168,7 @@ def tile_attend_soft_cap_sink_srtq128n512t2048_kernel(
         for t in range(PACK):
             nc.tensor.transpose(prob_t[:, t, :], prob[:, t * P : (t + 1) * P], ident[:])
         v_b = [
-            sb.tile([P, P * PACK], BF16, name="v_b0", align_bytes=64),
+            last_values.tile([P, P * PACK], BF16, name="v_b0", align_bytes=64, offset=2048),
             sb.tile([P, P * PACK], BF16, name="v_b1", align_bytes=64),
         ]
         nc.scalar.copy(

@@ -26,8 +26,9 @@ HALF = N // 2
 GROUP = 128
 VS_ROW = P - 1
 SPARE = 112
-V_SHARE = 416
-V_FIRST = 1408
+V_SHARE = 288
+V_SHARE0 = 384
+V_FIRST = 1152
 
 
 def clear_in_odd_runs(nc, words):
@@ -43,6 +44,7 @@ def tile_attend_soft_cap_sink_srtq128n512t2048_kernel(
     with ExitStack() as ctx:
         sb = ctx.enter_context(tc.tile_pool(name="sb", bufs=1))
         ps = ctx.enter_context(tc.psum_pool(name="ps", bufs=1))
+        after_max = ctx.enter_context(tc.tile_pool(name="after_max", bufs=1))
         last_values = ctx.enter_context(tc.tile_pool(name="last_values", bufs=1))
 
         ks_pool = sb.tile([P, PASSES * T // 4], I32, name="ks_pool", align_bytes=64)
@@ -51,8 +53,8 @@ def tile_attend_soft_cap_sink_srtq128n512t2048_kernel(
         offsets = sb.tile([P, N // 16], U16, name="offsets")
         nc.sync.dma_start(offsets[:], offs)
         nc.sync.dma_start(ks_pool[SPARE:P, T // 4 : T // 2], ks_rows[1])
-        vs_pool = sb.tile([P, T], F32, name="vs_pool", align_bytes=64)
-        nc.sync.dma_start(vs_pool[VS_ROW : VS_ROW + 1, :], vs[0:1, :])
+        k_pool = sb.tile([P, T], I32, name="k_pool", align_bytes=64)
+        nc.sync.dma_start(k_pool[:], k_words[0].rearrange("g t b -> g (t b)").bitcast(I32))
 
         qs = sb.tile([P, PASSES, NQ // 4], I32, name="qs", align_bytes=64)
         clear_in_odd_runs(nc, qs[:].rearrange("p o q -> p (o q)"))
@@ -61,16 +63,15 @@ def tile_attend_soft_cap_sink_srtq128n512t2048_kernel(
         make_identity(nc, ident[:])
         ks = sb.tile([P, PASSES * N // 4], I32, name="ks", align_bytes=64)
         clear_in_odd_runs(nc, ks[:])
+        vs_pool = sb.tile([P, T], F32, name="vs_pool", align_bytes=64)
         nc.gpsimd.memset(vs_pool[0:VS_ROW, :], 0.0)
 
         qs_rows = q_scales[0].bitcast(I32).rearrange("o (Q r) q -> r Q o q", r=4)
-        for r in range(3):
+        for r in range(4):
             nc.sync.dma_start(qs[r:P:32, :, :], qs_rows[r])
-        k_pool = sb.tile([P, T], I32, name="k_pool", align_bytes=64)
-        nc.sync.dma_start(k_pool[:], k_words[0].rearrange("g t b -> g (t b)").bitcast(I32))
-        nc.sync.dma_start(qs[3:P:32, :, :], qs_rows[3])
         qw = sb.tile([P, PASSES, NQ], I32, name="qw", align_bytes=64)
         nc.sync.dma_start(qw[:], q_words[0].rearrange("o g q r -> g o (q r)").bitcast(I32))
+        nc.sync.dma_start(vs_pool[VS_ROW : VS_ROW + 1, :], vs[0:1, :])
         v_pool = [
             sb.tile([P, T], F32, name="v_pool0", align_bytes=64),
             last_values.tile([P, T], F32, name="v_pool1", align_bytes=64, offset=0),
@@ -92,7 +93,7 @@ def tile_attend_soft_cap_sink_srtq128n512t2048_kernel(
 
         list_cols = HALF // 16
         halves = [offsets[:, h * list_cols : (h + 1) * list_cols] for h in range(2)]
-        k_both = [sb.tile([P, HALF], I32, name="k_both%d" % h, align_bytes=64) for h in range(2)]
+        k_both = [sb.tile([P, HALF], I32, name="k_both%d" % h, tag="k_both%d" % h, align_bytes=64) for h in range(2)]
         k_pass = [sb.tile([P, PASSES, 2 * HALF], U8, name="k_pass%d" % h, align_bytes=64) for h in range(2)]
         for h in range(2):
             nc.vector.tensor_copy(k_both[h][:].bitcast(U32), k_pool[:].bitcast(U32).indirect(halves[h]))
@@ -101,18 +102,12 @@ def tile_attend_soft_cap_sink_srtq128n512t2048_kernel(
                 k_pass[h][:].bitcast(U16), k_both[h][:].bitcast(U16).rearrange("p (j o) -> p o j", o=PASSES)
             )
 
-        vs_g = sb.tile([P, N], F32, name="vs_g", align_bytes=64)
-        nc.scalar.activation(vs_g[:], vs_pool[:].indirect(offsets[:]), ACT.Copy)
-
-        vs_t = ps.tile([P, PACK, P], F32, name="vs_t")
-        for t in range(PACK):
-            nc.tensor.transpose(vs_t[:, t, :], vs_g[:, t:N:PACK], ident[:])
-        vs_col = sb.tile([P, PACK], F32, name="vs_col", align_bytes=64)
-        nc.scalar.copy(vs_col[:], vs_t[:, :, VS_ROW])
+        vs_g = sb.tile([P, N], F32, name="vs_g", tag="k_both0", align_bytes=64)
+        nc.vector.tensor_copy(vs_g[:], vs_pool[:].indirect(offsets[:]))
 
         groups = N // GROUP
         score = [ps.tile([P, GROUP], F32, name="score%d" % g, tag="bank%d" % g) for g in range(groups)]
-        th = sb.tile([P, PACK, P], F32, name="th", align_bytes=64)
+        th = after_max.tile([P, PACK, P], F32, name="th", align_bytes=64, offset=0)
         per_half = HALF // GROUP
         for h in range(2):
             for o in range(PASSES):
@@ -139,7 +134,8 @@ def tile_attend_soft_cap_sink_srtq128n512t2048_kernel(
         neg_c = sb.tile([P, N + 1], F32, name="neg_c", align_bytes=64)
         nc.scalar.activation(neg_c[:, N : N + 1], sink_col[:], ACT.Copy, scale=-1.0)
         v_g = [sb.tile([P, N], BF16, name="v_g%d" % h, align_bytes=64) for h in range(2)]
-        nc.vector.tensor_copy(v_g[0][:], v_pool[0][:].indirect(offsets[:]))
+        nc.vector.tensor_copy(v_g[0][:, 0:V_SHARE0], v_pool[0][:].indirect(offsets[:, 0 : V_SHARE0 // 16]))
+        nc.scalar.activation(v_g[0][:, V_SHARE0:N], v_pool[0][:].indirect(offsets[:, V_SHARE0 // 16 : N // 16]), ACT.Copy)
         neg_m = sb.tile([P, 1], F32, name="neg_m")
         nc.vector.tensor_scalar(
             neg_c[:, 0:N],
@@ -161,7 +157,12 @@ def tile_attend_soft_cap_sink_srtq128n512t2048_kernel(
         nc.vector.tensor_copy(v_g[1][:, 0:V_SHARE], v_pool[1][:].indirect(offsets[:, 0 : V_SHARE // 16]))
         nc.scalar.activation(v_g[1][:, V_SHARE:N], v_pool[1][:].indirect(offsets[:, V_SHARE // 16 : N // 16]), ACT.Copy)
 
-        v_t = [ps.tile([P, 2, P], F32, name="v_t0"), ps.tile([P, 2, P], F32, name="v_t1", tag="bank2")]
+        vs_t = ps.tile([P, PACK, P], F32, name="vs_t", tag="bank0")
+        for t in range(PACK):
+            nc.tensor.transpose(vs_t[:, t, :], vs_g[:, t:N:PACK], ident[:])
+        vs_col = after_max.tile([P, PACK], F32, name="vs_col", align_bytes=64, offset=0)
+        nc.vector.tensor_copy(vs_col[:], vs_t[:, :, VS_ROW])
+        v_t = [ps.tile([P, 2, P], F32, name="v_t0", tag="bank3"), ps.tile([P, 2, P], F32, name="v_t1")]
         prob_t = ps.tile([P, PACK, P], F32, name="prob_t")
         for u in range(2):
             nc.tensor.transpose(v_t[0][:, u, :], v_g[0][:].bitcast(F32)[:, u : N // 2 : 2], ident[:])
@@ -201,7 +202,7 @@ def tile_attend_soft_cap_sink_srtq128n512t2048_kernel(
         nc.vector.quantize_mx(v_codes[1][:].bitcast(FP8X4), v_scales[1][:], v_b[1][:])
 
         for h in range(2):
-            y = ps.tile([P, P], F32, name="y%d" % h, tag="bank%d" % h)
+            y = ps.tile([P, P], F32, name="y%d" % h, tag="bank%d" % (h + 1))
             nc.tensor.matmul_mx(
                 y[:],
                 lhsT=w_codes[:].bitcast(FP8X4),

@@ -25,10 +25,11 @@ PASSES = D // (P * PACK)
 HALF = N // 2
 GROUP = 128
 VS_ROW = P - 1
-SPARE = 112
-V_SHARE = 288
-V_SHARE0 = 384
-V_FIRST = 1152
+SPARE = 96
+PLANE = N + NQ
+KEY_CUTS = (0, 256, 384, 512)
+V_SHARE = 256
+V_FIRST = 1024
 
 
 def clear_in_odd_runs(nc, words):
@@ -44,81 +45,87 @@ def tile_attend_soft_cap_sink_srtq128n512t2048_kernel(
     with ExitStack() as ctx:
         sb = ctx.enter_context(tc.tile_pool(name="sb", bufs=1))
         ps = ctx.enter_context(tc.psum_pool(name="ps", bufs=1))
+        first_values = ctx.enter_context(tc.tile_pool(name="first_values", bufs=1))
         after_max = ctx.enter_context(tc.tile_pool(name="after_max", bufs=1))
+        after_exp = ctx.enter_context(tc.tile_pool(name="after_exp", bufs=1))
         last_values = ctx.enter_context(tc.tile_pool(name="last_values", bufs=1))
 
-        ks_pool = sb.tile([P, PASSES * T // 4], I32, name="ks_pool", align_bytes=64)
-        ks_rows = k_scales.bitcast(I32)
-        nc.sync.dma_start(ks_pool[SPARE:P, 0 : T // 4], ks_rows[0])
+        ks_pool = sb.tile([P, T // 4], I32, name="ks_pool", align_bytes=64)
+        nc.sync.dma_start(ks_pool[SPARE:P, :], k_scales.bitcast(I32).rearrange("o f t -> f o t"))
         offsets = sb.tile([P, N // 16], U16, name="offsets")
         nc.sync.dma_start(offsets[:], offs)
-        nc.sync.dma_start(ks_pool[SPARE:P, T // 4 : T // 2], ks_rows[1])
+        staged = sb.tile([P, PLANE // 4], I32, name="staged", align_bytes=64)
+        nc.scalar.dma_start(staged[SPARE:P, N // 4 :], q_scales[0].bitcast(I32).rearrange("o f q -> f o q"))
+        sink_col = sb.tile([P, 1], F32, name="sink_col")
+        nc.scalar.dma_start(sink_col[:], sink[0])
         k_pool = sb.tile([P, T], I32, name="k_pool", align_bytes=64)
         nc.sync.dma_start(k_pool[:], k_words[0].rearrange("g t b -> g (t b)").bitcast(I32))
 
-        qs = sb.tile([P, PASSES, NQ // 4], I32, name="qs", align_bytes=64)
-        clear_in_odd_runs(nc, qs[:].rearrange("p o q -> p (o q)"))
         clear_in_odd_runs(nc, ks_pool[0:SPARE, :])
+        planes = sb.tile([P, PASSES * PLANE // 4], I32, name="planes", align_bytes=64)
+        clear_in_odd_runs(nc, planes[:])
         ident = sb.tile([P, P], F32, name="ident", align_bytes=64)
         make_identity(nc, ident[:])
-        ks = sb.tile([P, PASSES * N // 4], I32, name="ks", align_bytes=64)
-        clear_in_odd_runs(nc, ks[:])
         vs_pool = sb.tile([P, T], F32, name="vs_pool", align_bytes=64)
         nc.gpsimd.memset(vs_pool[0:VS_ROW, :], 0.0)
 
-        qs_rows = q_scales[0].bitcast(I32).rearrange("o (Q r) q -> r Q o q", r=4)
-        for r in range(4):
-            nc.sync.dma_start(qs[r:P:32, :, :], qs_rows[r])
         qw = sb.tile([P, PASSES, NQ], I32, name="qw", align_bytes=64)
         nc.sync.dma_start(qw[:], q_words[0].rearrange("o g q r -> g o (q r)").bitcast(I32))
         nc.sync.dma_start(vs_pool[VS_ROW : VS_ROW + 1, :], vs[0:1, :])
         v_pool = [
-            sb.tile([P, T], F32, name="v_pool0", align_bytes=64),
+            first_values.tile([P, T], F32, name="v_pool0", align_bytes=64, offset=0),
             last_values.tile([P, T], F32, name="v_pool1", align_bytes=64, offset=0),
         ]
         nc.sync.dma_start(v_pool[0][:, 0:V_FIRST], vT[0:P, 0:V_FIRST])
 
-        ks_g = sb.tile([P, PASSES * N // 4], I32, name="ks_g", align_bytes=64)
-        for o in range(PASSES):
-            nc.vector.tensor_copy(
-                ks_g[:].bitcast(U8)[:, o * N : (o + 1) * N],
-                ks_pool[:].bitcast(U8)[:, o * T : (o + 1) * T].indirect(offsets[:]),
-            )
-        for r in range(4):
-            nc.sync.dma_start(ks[r:P:32, :], ks_g[SPARE + r : P : 4, :])
+        neg_c = after_exp.tile([P, N + 1], F32, name="neg_c", align_bytes=64, offset=0)
+        nc.scalar.activation(neg_c[:, N : N + 1], sink_col[:], ACT.Copy, scale=-1.0)
+
+        ks_g = sb.tile([P, N // 4], I32, name="ks_g", align_bytes=64)
+        nc.vector.tensor_copy(ks_g[:].bitcast(U8), ks_pool[:].bitcast(U8).indirect(offsets[:]))
+        nc.vector.tensor_copy(staged[SPARE:P, 0 : N // 4], ks_g[SPARE:P, :])
+        for Q in range(4):
+            nc.sync.dma_start(planes[32 * Q : 32 * Q + 4, :], staged[SPARE + 8 * Q : SPARE + 8 * (Q + 1), :])
         nc.sync.dma_start(v_pool[0][:, V_FIRST:T], vT[0:P, V_FIRST:T])
-        sink_col = sb.tile([P, 1], F32, name="sink_col")
-        nc.sync.dma_start(sink_col[:], sink[0])
         nc.sync.dma_start(v_pool[1][:], vT[P : 2 * P, :])
 
-        list_cols = HALF // 16
-        halves = [offsets[:, h * list_cols : (h + 1) * list_cols] for h in range(2)]
-        k_both = [sb.tile([P, HALF], I32, name="k_both%d" % h, tag="k_both%d" % h, align_bytes=64) for h in range(2)]
-        k_pass = [sb.tile([P, PASSES, 2 * HALF], U8, name="k_pass%d" % h, align_bytes=64) for h in range(2)]
-        for h in range(2):
-            nc.vector.tensor_copy(k_both[h][:].bitcast(U32), k_pool[:].bitcast(U32).indirect(halves[h]))
-        for h in range(2):
+        pieces = list(zip(KEY_CUTS[:-1], KEY_CUTS[1:]))
+        k_both = [sb.tile([P, b - a], I32, name="k_both%d" % h, align_bytes=64) for h, (a, b) in enumerate(pieces)]
+        k_pass = [
+            sb.tile([P, PASSES, 2 * (b - a)], U8, name="k_pass%d" % h, align_bytes=64)
+            for h, (a, b) in enumerate(pieces)
+        ]
+
+        def part(h):
             nc.vector.tensor_copy(
                 k_pass[h][:].bitcast(U16), k_both[h][:].bitcast(U16).rearrange("p (j o) -> p o j", o=PASSES)
             )
 
-        vs_g = sb.tile([P, N], F32, name="vs_g", tag="k_both0", align_bytes=64)
-        nc.vector.tensor_copy(vs_g[:], vs_pool[:].indirect(offsets[:]))
+        for h, (a, b) in enumerate(pieces):
+            nc.vector.tensor_copy(
+                k_both[h][:].bitcast(U32), k_pool[:].bitcast(U32).indirect(offsets[:, a // 16 : b // 16])
+            )
+            if h > 0:
+                part(h - 1)
+        part(len(pieces) - 1)
+
+        vs_g = sb.tile([P, N], F32, name="vs_g", align_bytes=64)
+        nc.scalar.activation(vs_g[:], vs_pool[:].indirect(offsets[:]), ACT.Copy)
 
         groups = N // GROUP
         score = [ps.tile([P, GROUP], F32, name="score%d" % g, tag="bank%d" % g) for g in range(groups)]
         th = after_max.tile([P, PACK, P], F32, name="th", align_bytes=64, offset=0)
-        per_half = HALF // GROUP
-        for h in range(2):
-            for o in range(PASSES):
-                for j in range(per_half):
-                    g = h * per_half + j
+        plane_bytes = planes[:].bitcast(U8)
+        for h, (a, b) in enumerate(pieces):
+            for g in range(a // GROUP, b // GROUP):
+                j = g - a // GROUP
+                for o in range(PASSES):
                     nc.tensor.matmul_mx(
                         score[g][:],
                         lhsT=qw[:, o, :].bitcast(FP8X4),
-                        lhsT_scale=qs[:, o, :].bitcast(U8),
+                        lhsT_scale=plane_bytes[:, o * PLANE + N : (o + 1) * PLANE],
                         rhs=k_pass[h][:, o, 2 * j * GROUP : 2 * (j + 1) * GROUP].bitcast(FP4X4),
-                        rhs_scale=ks[:].bitcast(U8)[:, o * N + g * GROUP : o * N + (g + 1) * GROUP],
+                        rhs_scale=plane_bytes[:, o * PLANE + g * GROUP : o * PLANE + (g + 1) * GROUP],
                         start=(o == 0),
                         stop=(o == PASSES - 1),
                     )
@@ -131,50 +138,51 @@ def tile_attend_soft_cap_sink_srtq128n512t2048_kernel(
                 scale=1.0 / CAP,
             )
 
-        neg_c = sb.tile([P, N + 1], F32, name="neg_c", align_bytes=64)
-        nc.scalar.activation(neg_c[:, N : N + 1], sink_col[:], ACT.Copy, scale=-1.0)
-        v_g = [sb.tile([P, N], BF16, name="v_g%d" % h, align_bytes=64) for h in range(2)]
-        nc.vector.tensor_copy(v_g[0][:, 0:V_SHARE0], v_pool[0][:].indirect(offsets[:, 0 : V_SHARE0 // 16]))
-        nc.scalar.activation(v_g[0][:, V_SHARE0:N], v_pool[0][:].indirect(offsets[:, V_SHARE0 // 16 : N // 16]), ACT.Copy)
-        neg_m = sb.tile([P, 1], F32, name="neg_m")
-        nc.vector.tensor_scalar(
-            neg_c[:, 0:N],
-            th[:].rearrange("q t p -> q (t p)"),
-            -CAP,
-            neg_c[:, N : N + 1],
-            ALU.mult,
-            ALU.min,
-            accum_out=neg_m[:],
-        )
+        neg_max = neg_c[:, N : N + 1]
+        neg_c_places = neg_c[:, 0:N].rearrange("q (t p) -> q t p", t=PACK)
+        for h, (a, b) in enumerate(((0, HALF), (HALF, N))):
+            so_far = sb.tile([P, 1], F32, name="neg_max%d" % h)
+            nc.vector.tensor_scalar(
+                neg_c_places[:, :, a // PACK : b // PACK],
+                th[:, :, a // PACK : b // PACK],
+                -CAP,
+                neg_max,
+                ALU.mult,
+                ALU.min,
+                accum_out=so_far[:],
+            )
+            neg_max = so_far[:]
 
         prob = sb.tile([P, N + 1], F32, name="prob", align_bytes=64)
         part_sum = [sb.tile([P, 1], F32, name="part_sum%d" % h) for h in range(2)]
         for h, cols in enumerate((slice(0, HALF), slice(HALF, N + 1))):
             nc.scalar.activation(
-                prob[:, cols], neg_c[:, cols], ACT.Exp, bias=neg_m[:], scale=-1.0, accum_out=part_sum[h][:]
+                prob[:, cols], neg_c[:, cols], ACT.Exp, bias=neg_max, scale=-1.0, accum_out=part_sum[h][:]
             )
 
+        v_g = [
+            after_max.tile([P, N], BF16, name="v_g0", align_bytes=64, offset=0),
+            first_values.tile([P, N], BF16, name="v_g1", align_bytes=64, offset=0),
+        ]
+        nc.vector.tensor_copy(v_g[0][:], v_pool[0][:].indirect(offsets[:]))
         nc.vector.tensor_copy(v_g[1][:, 0:V_SHARE], v_pool[1][:].indirect(offsets[:, 0 : V_SHARE // 16]))
         nc.scalar.activation(v_g[1][:, V_SHARE:N], v_pool[1][:].indirect(offsets[:, V_SHARE // 16 : N // 16]), ACT.Copy)
 
         vs_t = ps.tile([P, PACK, P], F32, name="vs_t", tag="bank0")
         for t in range(PACK):
             nc.tensor.transpose(vs_t[:, t, :], vs_g[:, t:N:PACK], ident[:])
-        vs_col = after_max.tile([P, PACK], F32, name="vs_col", align_bytes=64, offset=0)
-        nc.vector.tensor_copy(vs_col[:], vs_t[:, :, VS_ROW])
-        v_t = [ps.tile([P, 2, P], F32, name="v_t0", tag="bank3"), ps.tile([P, 2, P], F32, name="v_t1")]
+        vs_col = after_exp.tile([P, PACK], F32, name="vs_col", align_bytes=64, offset=0)
+        nc.scalar.copy(vs_col[:], vs_t[:, :, VS_ROW])
+        v_t = [ps.tile([P, 2, P], F32, name="v_t0", tag="bank0"), ps.tile([P, 2, P], F32, name="v_t1")]
         prob_t = ps.tile([P, PACK, P], F32, name="prob_t")
-        for u in range(2):
-            nc.tensor.transpose(v_t[0][:, u, :], v_g[0][:].bitcast(F32)[:, u : N // 2 : 2], ident[:])
         for t in range(PACK):
             nc.tensor.transpose(prob_t[:, t, :], prob[:, t * P : (t + 1) * P], ident[:])
+        for u in range(2):
+            nc.tensor.transpose(v_t[0][:, u, :], v_g[0][:].bitcast(F32)[:, u : N // 2 : 2], ident[:])
         v_b = [
             last_values.tile([P, P * PACK], BF16, name="v_b0", align_bytes=64, offset=2048),
             sb.tile([P, P * PACK], BF16, name="v_b1", align_bytes=64),
         ]
-        nc.scalar.copy(
-            v_b[0][:].bitcast(F32).rearrange("p (e u) -> p e u", u=2), v_t[0][:].rearrange("p u e -> p e u")
-        )
         total = sb.tile([P, 1], F32, name="total")
         nc.gpsimd.tensor_tensor(total[:], part_sum[0][:], part_sum[1][:], ALU.add)
         w = last_values.tile([P, NQ, PACK], BF16, name="w", align_bytes=64, offset=0)
@@ -183,6 +191,9 @@ def tile_attend_soft_cap_sink_srtq128n512t2048_kernel(
             prob_t[:].rearrange("p t q -> p q t"),
             vs_col[:].unsqueeze(1).broadcast_to([P, NQ, PACK]),
             ALU.mult,
+        )
+        nc.scalar.copy(
+            v_b[0][:].bitcast(F32).rearrange("p (e u) -> p e u", u=2), v_t[0][:].rearrange("p u e -> p e u")
         )
 
         for u in range(2):

@@ -27,8 +27,8 @@ GROUP = 128
 VS_ROW = P - 1
 SPARE = 96
 PLANE = N + NQ
-KEY_CUTS = (0, 256, 384, 512)
-V_SHARE = 256
+KEY_CUTS = (0, 128, 256, 384, 512)
+V_SHARE = 224
 V_FIRST = 1024
 
 
@@ -45,9 +45,8 @@ def tile_attend_soft_cap_sink_srtq128n512t2048_kernel(
     with ExitStack() as ctx:
         sb = ctx.enter_context(tc.tile_pool(name="sb", bufs=1))
         ps = ctx.enter_context(tc.psum_pool(name="ps", bufs=1))
-        first_values = ctx.enter_context(tc.tile_pool(name="first_values", bufs=1))
-        after_max = ctx.enter_context(tc.tile_pool(name="after_max", bufs=1))
         after_exp = ctx.enter_context(tc.tile_pool(name="after_exp", bufs=1))
+        after_max = ctx.enter_context(tc.tile_pool(name="after_max", bufs=1))
         last_values = ctx.enter_context(tc.tile_pool(name="last_values", bufs=1))
 
         ks_pool = sb.tile([P, T // 4], I32, name="ks_pool", align_bytes=64)
@@ -73,7 +72,7 @@ def tile_attend_soft_cap_sink_srtq128n512t2048_kernel(
         nc.sync.dma_start(qw[:], q_words[0].rearrange("o g q r -> g o (q r)").bitcast(I32))
         nc.sync.dma_start(vs_pool[VS_ROW : VS_ROW + 1, :], vs[0:1, :])
         v_pool = [
-            first_values.tile([P, T], F32, name="v_pool0", align_bytes=64, offset=0),
+            sb.tile([P, T], F32, name="v_pool0", align_bytes=64),
             last_values.tile([P, T], F32, name="v_pool1", align_bytes=64, offset=0),
         ]
         nc.sync.dma_start(v_pool[0][:, 0:V_FIRST], vT[0:P, 0:V_FIRST])
@@ -87,10 +86,9 @@ def tile_attend_soft_cap_sink_srtq128n512t2048_kernel(
         for Q in range(4):
             nc.sync.dma_start(planes[32 * Q : 32 * Q + 4, :], staged[SPARE + 8 * Q : SPARE + 8 * (Q + 1), :])
         nc.sync.dma_start(v_pool[0][:, V_FIRST:T], vT[0:P, V_FIRST:T])
-        nc.sync.dma_start(v_pool[1][:], vT[P : 2 * P, :])
 
         pieces = list(zip(KEY_CUTS[:-1], KEY_CUTS[1:]))
-        k_both = [sb.tile([P, b - a], I32, name="k_both%d" % h, align_bytes=64) for h, (a, b) in enumerate(pieces)]
+        k_both = []
         k_pass = [
             sb.tile([P, PASSES, 2 * (b - a)], U8, name="k_pass%d" % h, align_bytes=64)
             for h, (a, b) in enumerate(pieces)
@@ -102,13 +100,18 @@ def tile_attend_soft_cap_sink_srtq128n512t2048_kernel(
             )
 
         for h, (a, b) in enumerate(pieces):
+            if h == 0:
+                k_both.append(last_values.tile([P, b - a], I32, name="k_both0", align_bytes=64, offset=0))
+            else:
+                k_both.append(sb.tile([P, b - a], I32, name="k_both%d" % h, tag="k_both%d" % (h // 3), align_bytes=64))
             nc.vector.tensor_copy(
                 k_both[h][:].bitcast(U32), k_pool[:].bitcast(U32).indirect(offsets[:, a // 16 : b // 16])
             )
-            if h > 0:
+            if h % 2 == 1:
                 part(h - 1)
-        part(len(pieces) - 1)
+                part(h)
 
+        nc.scalar.dma_start(v_pool[1][:], vT[P : 2 * P, :])
         vs_g = sb.tile([P, N], F32, name="vs_g", align_bytes=64)
         nc.scalar.activation(vs_g[:], vs_pool[:].indirect(offsets[:]), ACT.Copy)
 
@@ -162,17 +165,16 @@ def tile_attend_soft_cap_sink_srtq128n512t2048_kernel(
 
         v_g = [
             after_max.tile([P, N], BF16, name="v_g0", align_bytes=64, offset=0),
-            first_values.tile([P, N], BF16, name="v_g1", align_bytes=64, offset=0),
+            after_exp.tile([P, N], BF16, name="v_g1", align_bytes=64, offset=64),
         ]
-        nc.vector.tensor_copy(v_g[0][:], v_pool[0][:].indirect(offsets[:]))
-        nc.vector.tensor_copy(v_g[1][:, 0:V_SHARE], v_pool[1][:].indirect(offsets[:, 0 : V_SHARE // 16]))
-        nc.scalar.activation(v_g[1][:, V_SHARE:N], v_pool[1][:].indirect(offsets[:, V_SHARE // 16 : N // 16]), ACT.Copy)
-
         vs_t = ps.tile([P, PACK, P], F32, name="vs_t", tag="bank0")
         for t in range(PACK):
             nc.tensor.transpose(vs_t[:, t, :], vs_g[:, t:N:PACK], ident[:])
         vs_col = after_exp.tile([P, PACK], F32, name="vs_col", align_bytes=64, offset=0)
         nc.scalar.copy(vs_col[:], vs_t[:, :, VS_ROW])
+        nc.vector.tensor_copy(v_g[0][:], v_pool[0][:].indirect(offsets[:]))
+        nc.vector.tensor_copy(v_g[1][:, 0:V_SHARE], v_pool[1][:].indirect(offsets[:, 0 : V_SHARE // 16]))
+        nc.scalar.activation(v_g[1][:, V_SHARE:N], v_pool[1][:].indirect(offsets[:, V_SHARE // 16 : N // 16]), ACT.Copy)
         v_t = [ps.tile([P, 2, P], F32, name="v_t0", tag="bank0"), ps.tile([P, 2, P], F32, name="v_t1")]
         prob_t = ps.tile([P, PACK, P], F32, name="prob_t")
         for t in range(PACK):
@@ -185,7 +187,7 @@ def tile_attend_soft_cap_sink_srtq128n512t2048_kernel(
         ]
         total = sb.tile([P, 1], F32, name="total")
         nc.gpsimd.tensor_tensor(total[:], part_sum[0][:], part_sum[1][:], ALU.add)
-        w = last_values.tile([P, NQ, PACK], BF16, name="w", align_bytes=64, offset=0)
+        w = sb.tile([P, NQ, PACK], BF16, name="w", align_bytes=64)
         nc.vector.tensor_tensor(
             w[:],
             prob_t[:].rearrange("p t q -> p q t"),
@@ -198,35 +200,42 @@ def tile_attend_soft_cap_sink_srtq128n512t2048_kernel(
 
         for u in range(2):
             nc.tensor.transpose(v_t[1][:, u, :], v_g[1][:].bitcast(F32)[:, u : N // 2 : 2], ident[:])
-        nc.scalar.copy(
-            v_b[1][:].bitcast(F32).rearrange("p (e u) -> p e u", u=2), v_t[1][:].rearrange("p u e -> p e u")
-        )
+        e_halves = [slice(a * P // 2, (a + 1) * P // 2) for a in range(2)]
+        for e in e_halves:
+            nc.scalar.copy(
+                v_b[1][:].bitcast(F32).rearrange("p (e u) -> p e u", u=2)[:, e, :],
+                v_t[1][:].rearrange("p u e -> p e u")[:, e, :],
+            )
 
         v_codes = [sb.tile([P, P], U32, name="v_codes%d" % h, align_bytes=64) for h in range(2)]
         v_scales = [sb.tile([P, P], U8, name="v_scales%d" % h, align_bytes=64) for h in range(2)]
         w_codes = sb.tile([P, NQ], U32, name="w_codes", align_bytes=64)
         w_scales = sb.tile([P, NQ], U8, name="w_scales", align_bytes=64)
-        inv_total = last_values.tile([P, 1], F32, name="inv_total", align_bytes=64, offset=1024)
+        inv_total = sb.tile([P, 1], F32, name="inv_total")
         nc.vector.quantize_mx(v_codes[0][:].bitcast(FP8X4), v_scales[0][:], v_b[0][:])
         nc.vector.quantize_mx(w_codes[:].bitcast(FP8X4), w_scales[:], w[:].rearrange("p q t -> p (q t)"))
         nc.vector.reciprocal(inv_total[:], total[:])
-        nc.vector.quantize_mx(v_codes[1][:].bitcast(FP8X4), v_scales[1][:], v_b[1][:])
+        for e in e_halves:
+            nc.vector.quantize_mx(
+                v_codes[1][:, e].bitcast(FP8X4), v_scales[1][:, e], v_b[1][:, PACK * e.start : PACK * e.stop]
+            )
 
-        for h in range(2):
-            y = ps.tile([P, P], F32, name="y%d" % h, tag="bank%d" % (h + 1))
+        y_sb = [sb.tile([P, P], F32, name="y_sb%d" % h, align_bytes=64) for h in range(2)]
+        for i, (h, e) in enumerate([(0, slice(0, P))] + [(1, e) for e in e_halves]):
+            y = ps.tile([P, e.stop - e.start], F32, name="y%d" % i, tag="bank%d" % (i + 1))
             nc.tensor.matmul_mx(
                 y[:],
                 lhsT=w_codes[:].bitcast(FP8X4),
                 lhsT_scale=w_scales[:],
-                rhs=v_codes[h][:].bitcast(FP8X4),
-                rhs_scale=v_scales[h][:],
+                rhs=v_codes[h][:, e].bitcast(FP8X4),
+                rhs_scale=v_scales[h][:, e],
                 start=True,
                 stop=True,
             )
-            y_sb = sb.tile([P, P], F32, name="y_sb%d" % h, align_bytes=64)
-            if h == 0:
-                nc.scalar.activation(y_sb[:], y[:], ACT.Copy, scale=inv_total[:])
-                nc.scalar.dma_start(out[0][:, h * P : (h + 1) * P], y_sb[:])
+            if i < 2:
+                nc.scalar.activation(y_sb[h][:, e], y[:], ACT.Copy, scale=inv_total[:])
             else:
-                nc.vector.tensor_scalar(y_sb[:], y[:], inv_total[:], None, ALU.mult)
-                nc.sync.dma_start(out[0][:, h * P : (h + 1) * P], y_sb[:])
+                nc.vector.tensor_scalar(y_sb[h][:, e], y[:], inv_total[:], None, ALU.mult)
+            if i == 0:
+                nc.sync.dma_start(out[0][:, 0:P], y_sb[0][:])
+        nc.sync.dma_start(out[0][:, P : 2 * P], y_sb[1][:])

@@ -28,8 +28,8 @@ VS_ROW = P - 1
 SPARE = 96
 PLANE = N + NQ
 KEY_CUTS = (0, 128, 256, 384, 512)
-V_SHARE = 224
-V_FIRST = 1024
+V_SHARE = 192
+V_FIRST = 1152
 
 
 def clear_in_odd_runs(nc, words):
@@ -50,11 +50,11 @@ def tile_attend_soft_cap_sink_srtq128n512t2048_kernel(
         last_values = ctx.enter_context(tc.tile_pool(name="last_values", bufs=1))
 
         ks_pool = sb.tile([P, T // 4], I32, name="ks_pool", align_bytes=64)
-        nc.sync.dma_start(ks_pool[SPARE:P, :], k_scales.bitcast(I32).rearrange("o f t -> f o t"))
+        nc.scalar.dma_start(ks_pool[SPARE:P, :], k_scales.bitcast(I32).rearrange("o f t -> f o t"))
         offsets = sb.tile([P, N // 16], U16, name="offsets")
         nc.sync.dma_start(offsets[:], offs)
         staged = sb.tile([P, PLANE // 4], I32, name="staged", align_bytes=64)
-        nc.scalar.dma_start(staged[SPARE:P, N // 4 :], q_scales[0].bitcast(I32).rearrange("o f q -> f o q"))
+        nc.sync.dma_start(staged[SPARE:P, N // 4 :], q_scales[0].bitcast(I32).rearrange("o f q -> f o q"))
         sink_col = sb.tile([P, 1], F32, name="sink_col")
         nc.scalar.dma_start(sink_col[:], sink[0])
         k_pool = sb.tile([P, T], I32, name="k_pool", align_bytes=64)
@@ -100,10 +100,11 @@ def tile_attend_soft_cap_sink_srtq128n512t2048_kernel(
             )
 
         for h, (a, b) in enumerate(pieces):
-            if h == 0:
-                k_both.append(last_values.tile([P, b - a], I32, name="k_both0", align_bytes=64, offset=0))
+            if h % 2 == 0:
+                at = 4 * T - 256 + 128 * h
+                k_both.append(last_values.tile([P, b - a], I32, name="k_both%d" % h, align_bytes=64, offset=at))
             else:
-                k_both.append(sb.tile([P, b - a], I32, name="k_both%d" % h, tag="k_both%d" % (h // 3), align_bytes=64))
+                k_both.append(sb.tile([P, b - a], I32, name="k_both%d" % h, tag="k_both_odd", align_bytes=64))
             nc.vector.tensor_copy(
                 k_both[h][:].bitcast(U32), k_pool[:].bitcast(U32).indirect(offsets[:, a // 16 : b // 16])
             )

@@ -28,8 +28,8 @@ VS_ROW = P - 1
 SPARE = 96
 PLANE = N + NQ
 KEY_CUTS = (0, 128, 256, 384, 512)
-V_SHARE = 192
-V_FIRST = 1152
+V_SHARE = 224
+V_FIRST = 960
 
 
 def clear_in_odd_runs(nc, words):

@@ -29,7 +29,7 @@ SPARE = 96
 PLANE = N + NQ
 KEY_CUTS = (0, 128, 256, 384, 512)
 V_SHARE = 224
-V_FIRST = 960
+V_FIRST = 896
 
 
 def clear_in_odd_runs(nc, words):
@@ -68,9 +68,9 @@ def tile_attend_soft_cap_sink_srtq128n512t2048_kernel(
         vs_pool = sb.tile([P, T], F32, name="vs_pool", align_bytes=64)
         nc.gpsimd.memset(vs_pool[0:VS_ROW, :], 0.0)
 
+        nc.sync.dma_start(vs_pool[VS_ROW : VS_ROW + 1, :], vs[0:1, :])
         qw = sb.tile([P, PASSES, NQ], I32, name="qw", align_bytes=64)
         nc.sync.dma_start(qw[:], q_words[0].rearrange("o g q r -> g o (q r)").bitcast(I32))
-        nc.sync.dma_start(vs_pool[VS_ROW : VS_ROW + 1, :], vs[0:1, :])
         v_pool = [
             sb.tile([P, T], F32, name="v_pool0", align_bytes=64),
             last_values.tile([P, T], F32, name="v_pool1", align_bytes=64, offset=0),

from contextlib import ExitStack

import concourse.mybir as mybir
from concourse.masks import make_identity

N, T, D, DV, NQ = 512, 2048, 1024, 256, 128
CAP = 2.0
FLOPS = 2 * NQ * N * (D + DV)
BYTES = D * T // 2 + D // 32 * T + D * NQ + D // 32 * NQ + 4 * DV * T + 4 * T + 4 * NQ + 128 * 2 * N // 16 + 4 * NQ * DV

F32 = mybir.dt.float32
BF16 = mybir.dt.bfloat16
I32 = mybir.dt.int32
U32 = mybir.dt.uint32
U16 = mybir.dt.uint16
U8 = mybir.dt.uint8
FP8X4 = mybir.dt.float8_e4m3fn_x4
FP4X4 = mybir.dt.float4_e2m1fn_x4
ALU = mybir.AluOpType
ACT = mybir.ActivationFunctionType

P = 128
PACK = 4
PASSES = D // (P * PACK)
HALF = N // 2
GROUP = 128
VS_ROW = P - 1
SPARE = 96
PLANE = N + NQ
KEY_CUTS = (0, 128, 256, 384, 512)
V_SHARE = 224
V_FIRST = 896


def clear_in_odd_runs(nc, words):
    cut = words.shape[1] // 2 - 1
    nc.vector.memset(words[:, 0:cut], 0)
    nc.vector.memset(words[:, cut:], 0)


def tile_attend_soft_cap_sink_srtq128n512t2048_kernel(
    tc, q_words, q_scales, k_words, k_scales, vT, vs, sink, offs, out
):
    nc = tc.nc
    with ExitStack() as ctx:
        sb = ctx.enter_context(tc.tile_pool(name="sb", bufs=1))
        ps = ctx.enter_context(tc.psum_pool(name="ps", bufs=1))
        after_exp = ctx.enter_context(tc.tile_pool(name="after_exp", bufs=1))
        after_max = ctx.enter_context(tc.tile_pool(name="after_max", bufs=1))
        last_values = ctx.enter_context(tc.tile_pool(name="last_values", bufs=1))

        ks_pool = sb.tile([P, T // 4], I32, name="ks_pool", align_bytes=64)
        nc.scalar.dma_start(ks_pool[SPARE:P, :], k_scales.bitcast(I32).rearrange("o f t -> f o t"))
        offsets = sb.tile([P, N // 16], U16, name="offsets")
        nc.sync.dma_start(offsets[:], offs)
        staged = sb.tile([P, PLANE // 4], I32, name="staged", align_bytes=64)
        nc.sync.dma_start(staged[SPARE:P, N // 4 :], q_scales[0].bitcast(I32).rearrange("o f q -> f o q"))
        sink_col = sb.tile([P, 1], F32, name="sink_col")
        nc.scalar.dma_start(sink_col[:], sink[0])
        k_pool = sb.tile([P, T], I32, name="k_pool", align_bytes=64)
        nc.sync.dma_start(k_pool[:], k_words[0].rearrange("g t b -> g (t b)").bitcast(I32))

        clear_in_odd_runs(nc, ks_pool[0:SPARE, :])
        planes = sb.tile([P, PASSES * PLANE // 4], I32, name="planes", align_bytes=64)
        clear_in_odd_runs(nc, planes[:])
        ident = sb.tile([P, P], F32, name="ident", align_bytes=64)
        make_identity(nc, ident[:])
        vs_pool = sb.tile([P, T], F32, name="vs_pool", align_bytes=64)
        nc.gpsimd.memset(vs_pool[0:VS_ROW, :], 0.0)

        nc.sync.dma_start(vs_pool[VS_ROW : VS_ROW + 1, :], vs[0:1, :])
        qw = sb.tile([P, PASSES, NQ], I32, name="qw", align_bytes=64)
        nc.sync.dma_start(qw[:], q_words[0].rearrange("o g q r -> g o (q r)").bitcast(I32))
        v_pool = [
            sb.tile([P, T], F32, name="v_pool0", align_bytes=64),
            last_values.tile([P, T], F32, name="v_pool1", align_bytes=64, offset=0),
        ]
        nc.sync.dma_start(v_pool[0][:, 0:V_FIRST], vT[0:P, 0:V_FIRST])

        neg_c = after_exp.tile([P, N + 1], F32, name="neg_c", align_bytes=64, offset=0)
        nc.scalar.activation(neg_c[:, N : N + 1], sink_col[:], ACT.Copy, scale=-1.0)

        ks_g = sb.tile([P, N // 4], I32, name="ks_g", align_bytes=64)
        nc.vector.tensor_copy(ks_g[:].bitcast(U8), ks_pool[:].bitcast(U8).indirect(offsets[:]))
        nc.vector.tensor_copy(staged[SPARE:P, 0 : N // 4], ks_g[SPARE:P, :])
        for Q in range(4):
            nc.sync.dma_start(planes[32 * Q : 32 * Q + 4, :], staged[SPARE + 8 * Q : SPARE + 8 * (Q + 1), :])
        nc.sync.dma_start(v_pool[0][:, V_FIRST:T], vT[0:P, V_FIRST:T])

        pieces = list(zip(KEY_CUTS[:-1], KEY_CUTS[1:]))
        k_both = []
        k_pass = [
            sb.tile([P, PASSES, 2 * (b - a)], U8, name="k_pass%d" % h, align_bytes=64)
            for h, (a, b) in enumerate(pieces)
        ]

        def part(h):
            nc.vector.tensor_copy(
                k_pass[h][:].bitcast(U16), k_both[h][:].bitcast(U16).rearrange("p (j o) -> p o j", o=PASSES)
            )

        for h, (a, b) in enumerate(pieces):
            if h % 2 == 0:
                at = 4 * T - 256 + 128 * h
                k_both.append(last_values.tile([P, b - a], I32, name="k_both%d" % h, align_bytes=64, offset=at))
            else:
                k_both.append(sb.tile([P, b - a], I32, name="k_both%d" % h, tag="k_both_odd", align_bytes=64))
            nc.vector.tensor_copy(
                k_both[h][:].bitcast(U32), k_pool[:].bitcast(U32).indirect(offsets[:, a // 16 : b // 16])
            )
            if h % 2 == 1:
                part(h - 1)
                part(h)

        nc.scalar.dma_start(v_pool[1][:], vT[P : 2 * P, :])
        vs_g = sb.tile([P, N], F32, name="vs_g", align_bytes=64)
        nc.scalar.activation(vs_g[:], vs_pool[:].indirect(offsets[:]), ACT.Copy)

        groups = N // GROUP
        score = [ps.tile([P, GROUP], F32, name="score%d" % g, tag="bank%d" % g) for g in range(groups)]
        th = after_max.tile([P, PACK, P], F32, name="th", align_bytes=64, offset=0)
        plane_bytes = planes[:].bitcast(U8)
        for h, (a, b) in enumerate(pieces):
            for g in range(a // GROUP, b // GROUP):
                j = g - a // GROUP
                for o in range(PASSES):
                    nc.tensor.matmul_mx(
                        score[g][:],
                        lhsT=qw[:, o, :].bitcast(FP8X4),
                        lhsT_scale=plane_bytes[:, o * PLANE + N : (o + 1) * PLANE],
                        rhs=k_pass[h][:, o, 2 * j * GROUP : 2 * (j + 1) * GROUP].bitcast(FP4X4),
                        rhs_scale=plane_bytes[:, o * PLANE + g * GROUP : o * PLANE + (g + 1) * GROUP],
                        start=(o == 0),
                        stop=(o == PASSES - 1),
                    )
        group_rows = GROUP // PACK
        for g in range(groups):
            nc.scalar.activation(
                th[:, :, g * group_rows : (g + 1) * group_rows],
                score[g][:].rearrange("q (p t) -> q t p", t=PACK),
                ACT.Tanh,
                scale=1.0 / CAP,
            )

        neg_max = neg_c[:, N : N + 1]
        neg_c_places = neg_c[:, 0:N].rearrange("q (t p) -> q t p", t=PACK)
        for h, (a, b) in enumerate(((0, HALF), (HALF, N))):
            so_far = sb.tile([P, 1], F32, name="neg_max%d" % h)
            nc.vector.tensor_scalar(
                neg_c_places[:, :, a // PACK : b // PACK],
                th[:, :, a // PACK : b // PACK],
                -CAP,
                neg_max,
                ALU.mult,
                ALU.min,
                accum_out=so_far[:],
            )
            neg_max = so_far[:]

        prob = sb.tile([P, N + 1], F32, name="prob", align_bytes=64)
        part_sum = [sb.tile([P, 1], F32, name="part_sum%d" % h) for h in range(2)]
        for h, cols in enumerate((slice(0, HALF), slice(HALF, N + 1))):
            nc.scalar.activation(
                prob[:, cols], neg_c[:, cols], ACT.Exp, bias=neg_max, scale=-1.0, accum_out=part_sum[h][:]
            )

        v_g = [
            after_max.tile([P, N], BF16, name="v_g0", align_bytes=64, offset=0),
            after_exp.tile([P, N], BF16, name="v_g1", align_bytes=64, offset=64),
        ]
        vs_t = ps.tile([P, PACK, P], F32, name="vs_t", tag="bank0")
        for t in range(PACK):
            nc.tensor.transpose(vs_t[:, t, :], vs_g[:, t:N:PACK], ident[:])
        vs_col = after_exp.tile([P, PACK], F32, name="vs_col", align_bytes=64, offset=0)
        nc.scalar.copy(vs_col[:], vs_t[:, :, VS_ROW])
        nc.vector.tensor_copy(v_g[0][:], v_pool[0][:].indirect(offsets[:]))
        nc.vector.tensor_copy(v_g[1][:, 0:V_SHARE], v_pool[1][:].indirect(offsets[:, 0 : V_SHARE // 16]))
        nc.scalar.activation(v_g[1][:, V_SHARE:N], v_pool[1][:].indirect(offsets[:, V_SHARE // 16 : N // 16]), ACT.Copy)
        v_t = [ps.tile([P, 2, P], F32, name="v_t0", tag="bank0"), ps.tile([P, 2, P], F32, name="v_t1")]
        prob_t = ps.tile([P, PACK, P], F32, name="prob_t")
        for t in range(PACK):
            nc.tensor.transpose(prob_t[:, t, :], prob[:, t * P : (t + 1) * P], ident[:])
        for u in range(2):
            nc.tensor.transpose(v_t[0][:, u, :], v_g[0][:].bitcast(F32)[:, u : N // 2 : 2], ident[:])
        v_b = [
            last_values.tile([P, P * PACK], BF16, name="v_b0", align_bytes=64, offset=2048),
            sb.tile([P, P * PACK], BF16, name="v_b1", align_bytes=64),
        ]
        total = sb.tile([P, 1], F32, name="total")
        nc.gpsimd.tensor_tensor(total[:], part_sum[0][:], part_sum[1][:], ALU.add)
        w = sb.tile([P, NQ, PACK], BF16, name="w", align_bytes=64)
        nc.vector.tensor_tensor(
            w[:],
            prob_t[:].rearrange("p t q -> p q t"),
            vs_col[:].unsqueeze(1).broadcast_to([P, NQ, PACK]),
            ALU.mult,
        )
        nc.scalar.copy(
            v_b[0][:].bitcast(F32).rearrange("p (e u) -> p e u", u=2), v_t[0][:].rearrange("p u e -> p e u")
        )

        for u in range(2):
            nc.tensor.transpose(v_t[1][:, u, :], v_g[1][:].bitcast(F32)[:, u : N // 2 : 2], ident[:])
        e_halves = [slice(a * P // 2, (a + 1) * P // 2) for a in range(2)]
        for e in e_halves:
            nc.scalar.copy(
                v_b[1][:].bitcast(F32).rearrange("p (e u) -> p e u", u=2)[:, e, :],
                v_t[1][:].rearrange("p u e -> p e u")[:, e, :],
            )

        v_codes = [sb.tile([P, P], U32, name="v_codes%d" % h, align_bytes=64) for h in range(2)]
        v_scales = [sb.tile([P, P], U8, name="v_scales%d" % h, align_bytes=64) for h in range(2)]
        w_codes = sb.tile([P, NQ], U32, name="w_codes", align_bytes=64)
        w_scales = sb.tile([P, NQ], U8, name="w_scales", align_bytes=64)
        inv_total = sb.tile([P, 1], F32, name="inv_total")
        nc.vector.quantize_mx(v_codes[0][:].bitcast(FP8X4), v_scales[0][:], v_b[0][:])
        nc.vector.quantize_mx(w_codes[:].bitcast(FP8X4), w_scales[:], w[:].rearrange("p q t -> p (q t)"))
        nc.vector.reciprocal(inv_total[:], total[:])
        for e in e_halves:
            nc.vector.quantize_mx(
                v_codes[1][:, e].bitcast(FP8X4), v_scales[1][:, e], v_b[1][:, PACK * e.start : PACK * e.stop]
            )

        y_sb = [sb.tile([P, P], F32, name="y_sb%d" % h, align_bytes=64) for h in range(2)]
        for i, (h, e) in enumerate([(0, slice(0, P))] + [(1, e) for e in e_halves]):
            y = ps.tile([P, e.stop - e.start], F32, name="y%d" % i, tag="bank%d" % (i + 1))
            nc.tensor.matmul_mx(
                y[:],
                lhsT=w_codes[:].bitcast(FP8X4),
                lhsT_scale=w_scales[:],
                rhs=v_codes[h][:, e].bitcast(FP8X4),
                rhs_scale=v_scales[h][:, e],
                start=True,
                stop=True,
            )
            if i < 2:
                nc.scalar.activation(y_sb[h][:, e], y[:], ACT.Copy, scale=inv_total[:])
            else:
                nc.vector.tensor_scalar(y_sb[h][:, e], y[:], inv_total[:], None, ALU.mult)
            if i == 0:
                nc.sync.dma_start(out[0][:, 0:P], y_sb[0][:])
        nc.sync.dma_start(out[0][:, P : 2 * P], y_sb[1][:])
